import numpy as np, ml_dtypes
CORES = [16,18,20,22]
N = 4
BF = ml_dtypes.bfloat16
NB, T0, P, Q, RO, CM = 4096, 1536, 256, 2, 4, 4096
H = 3 * P // 2
def tally(fork):
    far = np.arange(P) % Q < Q - 1
    return np.add.reduce(np.where(fork, np.where(far, 1, 1 - Q), 0), axis=(1, 2))
def lanes(lv):
    T = lv.shape[2]; o = (np.arange(T) + T - H) % T
    return o[np.argsort(1 - lv[:, :, o], axis=2, kind="stable")[:, :, :P]]
def at(a, ix):
    return np.take_along_axis(a, ix[:, :, None, :], 3)
def play(x, rg, lv, z, w, kap, th, cap, rounds):
    x, rg, lv, z, w, kap, th, cap = [np.asarray(a).astype(np.int32) for a in (x, rg, lv, z, w, kap, th, cap)]
    bal = np.zeros(N, np.int64); far = np.arange(P) % Q < Q - 1; best = None
    for t in range(rounds):
        T = T0 + P * t
        ring = at(rg, lanes(lv))
        xl = at(x, ring.transpose(0, 1, 3, 2).reshape(N, 8, P * 16)).reshape(N, 8, 16, P, 16)
        k = np.argmax(np.add.reduce(np.minimum(xl, z[..., None]), axis=2), axis=3)
        y0 = np.abs(np.take_along_axis(xl, k[:, :, None, :, None], 4)[..., 0] - z)
        y = np.array(y0)
        for c in range(Q - 1): y[..., c::Q] = np.roll(y0[..., c::Q], 1 + (t + c) % (N - 1), axis=0)
        u = np.add.reduce(w[..., None] * y, axis=2) & 4095
        h = ((u * u >> 5)[..., None] + kap[:, :, None, :] * u[..., None]) & 4095
        tau = h * T >> 12; age = h & 15
        b = np.take_along_axis(rg.reshape(N, 8, 16 * T), (age * T + tau).reshape(N, 8, P * 16), 2)
        xb = at(x, b).reshape(N, 8, 16, P, 16)
        far_off = np.add.reduce(np.abs(xb - y[..., None]), axis=2)
        m = np.argmin(far_off, axis=3)[..., None]
        best = np.take_along_axis(far_off, m, 3)[..., 0]; fork = best < th[:, :, None]
        tm = np.take_along_axis(tau, m, 3)[..., 0]; am = np.take_along_axis(age, m, 3)[..., 0]
        xm = np.take_along_axis(xb, m[:, :, None, :, :], 4)[..., 0]
        tail = np.take_along_axis(at(rg, tm), np.minimum(am[:, :, None, :] + np.arange(15)[:, None], 15), 2)
        tail = np.where(fork[:, :, None], tail, ring[:, :, :15])
        new = np.broadcast_to((NB + P * t + np.arange(P)).astype(np.int32), (N, 8, 1, P))
        xn = np.where(fork[:, :, None], (xm + y) >> 1, y)
        bal = bal + tally(fork)
        off = fork & np.where(far, bal[:, None, None] > cap[:, :, None], -bal[:, None, None] > cap[:, :, None])
        x = np.concatenate([x, xn.astype(np.int32)], axis=3); rg = np.concatenate([rg, np.concatenate([new, tail], axis=2).astype(np.int32)], axis=3)
        lv = np.concatenate([lv, np.where(off, 0, 1).astype(np.int32)], axis=2)
    return x, rg, lv, best, bal
def parts(rng):
    x = (rng.integers(24, 65, (N, 8, 1, NB)) * rng.random((N, 8, 16, NB))).astype(np.int64)
    rg = rng.integers(0, NB, (N, 8, 16, T0))
    lv = (np.argsort(rng.random((N, 8, T0)), axis=2) < rng.integers(T0 // 2, T0, (N, 8, 1))).astype(np.int64)
    z = (rng.permutation(np.linspace(16, 64, N))[:, None, None, None] * rng.random((N, 8, 16, P))).astype(np.int64)
    return x, rg, lv, z, rng.integers(0, 4096, (N, 8, 16)), rng.integers(0, 2048, (N, 8, 16))
def tune(rng, x, rg, lv, z, w, kap):
    one = np.ones((N, 8), np.int64); best = play(x, rg, lv, z, w, kap, one, one, 1)[3]
    th = np.take_along_axis(np.sort(best, axis=2), rng.integers(P // 4, 3 * P // 4, (N, 8, 1)), 2)[:, :, 0] + rng.integers(0, 2, (N, 8))
    return np.clip(th, 1, 1008), best
def caps(rng, th, best):
    return np.minimum((1.5 * (np.abs(tally(best < th[:, :, None]))[:, None] + 8) * rng.random((N, 8))).astype(np.int64), CM)
def close(th, best):
    b = np.abs(tally(best < th[:, :, None]))[:, None]; d = np.array([0, -1, 1, 0, -1, -CM, CM, -1])
    return np.clip(b + d[(np.arange(8)[None, :] + 3 * np.arange(N)[:, None]) % 8], 0, CM)
def pack(x, rg, lv, z, w, kap, th, cap):
    i = lambda a, s: np.ascontiguousarray(np.reshape(a, s)).astype(np.int32)
    return {"x0": np.reshape(x, (N, 128, NB)).astype(np.float32).astype(BF), "rings": i(rg, (N, 128, T0)), "live": i(lv, (N, 8, T0)), "z": np.reshape(z, (N, 128, P)).astype(np.float32).astype(BF),
            "w": i(w, (N, 128, 1)), "kap": i(kap, (N, 128, 1)), "th": i(th, (N, 8, 1)), "cap": i(cap, (N, 8, 1))}
def setup_inputs(rng):
    p = parts(rng); th, best = tune(rng, *p)
    return pack(*p, th, caps(rng, th, best))
def setup_inputs_spread(rng):
    x = (np.exp2(6 * rng.random((N, 8, 1, NB))) * rng.random((N, 8, 16, NB))).astype(np.int64)
    z = (np.exp2(6 * rng.random((N, 8, 1, P))) * rng.random((N, 8, 16, P))).astype(np.int64)
    rg = (NB * rng.random((N, 8, 16, T0)) ** rng.integers(1, 5, (N, 8, 1, 1))).astype(np.int64); rg = np.minimum(rg, NB - 1)
    lv = (np.argsort(rng.random((N, 8, T0)), axis=2) < (P * np.exp2(1.3 * rng.random((N, 8, 1)))).astype(np.int64)).astype(np.int64)
    w = np.exp2(12 * rng.random((N, 8, 16))).astype(np.int64); kap = np.exp2(11 * rng.random((N, 8, 16))).astype(np.int64)
    w = np.minimum(w, 4095); kap = np.minimum(kap, 2047); th, best = tune(rng, x, rg, lv, z, w, kap)
    return pack(x, rg, lv, z, w, kap, th, caps(rng, th, best))
def setup_inputs_ends(rng):
    hi = rng.integers(0, 2, (N, 8)); hi[:, 0] = 0; hi[:, 7] = 1; up = rng.permutation(N) % 2 == 0; o = rng.permutation(8); far = np.arange(P) % Q < Q - 1
    x = 63 * rng.integers(0, 2, (N, 8, 16, NB)); x[..., 0] = 63 * (1 - hi)[..., None]; x[..., NB - 1] = 63 * hi[..., None]
    one = (NB - 1) * hi; nil = NB - 1 - one
    rg = np.where(rng.random((N, 8, 16, T0)) < 0.5, one[:, :, None, None], nil[:, :, None, None]); rg[:, :, 0] = one[:, :, None]
    rg[:, :, 0, 0] = np.where(up[:, None], one, nil); rg[:, :, 1, 0] = one
    lv = rng.integers(0, 2, (N, 8, T0)); lv[:, :, T0 - H:] = 1
    z = np.array(np.broadcast_to(np.where(far, 0, 63), (N, 8, 16, P)))
    kap = 2047 * rng.integers(0, 2, (N, 8, 16)); w = 4095 * rng.integers(0, 2, (N, 8, 16)); cap = np.full((N, 8), CM)
    th = np.where(rng.integers(0, 2, (N, 8)) == 0, 1, 1008); th[:, o[0]] = 1; th[:, o[1]] = 1008
    for g in o[5:]:
        r = 63 * rng.integers(0, 2, (N, 16, P)); r[:, 1] = 63 - r[:, 0]
        z[:, g] = np.where(far, r, 63); th[:, g] = np.where(up, 1008, 1); cap[:, g] = 0
    good = []
    for n in range(1, 17):
        u = (4095 * 63 * n) & 4095; hs = [((u * u >> 5) + c * u) & 4095 for c in (0, 2047)]
        if all((h & 15) > 0 and (h * T0 >> 12) > 0 and (h * (T0 + P * (RO - 1)) >> 12) < T0 for h in hs): good.append((n, hs))
    for q in range(N):
        for g in o[:5]:
            n, hs = good[0] if g == o[0] else good[int(rng.integers(0, len(good)))]
            w[q, g] = 4095 * (rng.permutation(16) < n)
            for t in range(RO):
                for h in hs: rg[q, g, h & 15, h * (T0 + P * t) >> 12] = one[q, g] if up[q] else nil[q, g]
    return pack(x, rg, lv, z, w, kap, th, cap)
def setup_inputs_corners(rng):
    x, rg, lv, z, w, kap = parts(rng); v = np.arange(T0)
    for q in range(N):
        for g in range(8):
            lv[q, g] = (v < P, v >= T0 - P, v >= 0, (v < P - 1) | (v == T0 - 1), rng.permutation(T0) < P, (v >= T0 - H - P) & (v < T0 - H), rng.permutation(T0) < 2 * P, v != T0 - H)[(g + q) % 8]
    rg[:, 0] = np.where(rng.random((N, 16, T0)) < 0.5, 0, NB - 1); rg[:, 1] = rg[:, 1, :1]; rg[:, 2] = rng.integers(NB - 16, NB, (N, 16, T0))
    x[:, 3, :, 1::2] = x[:, 3, :, ::2]; x[:, 4, :, ::3] = 0; x[:, 4, :, 1::3] = 63
    w[:, 5:7] = 0; x[:, 5:7, 0] = 63
    w[:, 5, 0] = 65; z[:, 5, 0] = rng.choice(np.array([0, 62, 63]), (N, P)); kap[:, 5, 15] = 2047
    w[:, 6, 0] = 1; z[:, 6, 0] = rng.choice(np.array([60, 61, 63]), (N, P)); kap[:, 6] = np.where(rng.random((N, 16)) < 0.5, 1365, kap[:, 6])
    w[:, 7] = 4095; kap[:, 7] = 2047 * rng.integers(0, 2, (N, 16))
    th, best = tune(rng, x, rg, lv, z, w, kap); m = rng.integers(0, 5, (N, 8)); th = np.where(m == 0, 1, np.where(m == 1, 1008, th))
    return pack(x, rg, lv, z, w, kap, th, close(th, best))
def setup_inputs_crowd(rng):
    x, rg, lv, z, w, kap = parts(rng); lv[:, ::2] = 1
    for g in (0, 1, 4, 5): rg[:, g] = rg[:, g, :, :1]; z[:, g] = z[:, g, :, :1]
    z[:, 1, :, 0] = 63 - z[:, 1, :, 0]; z[:, 5, :, P - 1] = 63 - z[:, 5, :, P - 1]
    w[:, 2:4] = 0; w[:, 3, 7] = 3; x[:, 3, 7] = 63; z[:, 3, 7] = 63; z[:, 3, 7, 1] = 0
    kap[:, 6] = kap[:, 6, :1]; kap[:, 7] = 0; rg[:, 7] = np.where(rng.random((N, 16, T0)) < 0.5, 0, NB - 1)
    w[:, 7] = 4095; x[:, 7, :, 0] = 63; x[:, 7, :, NB - 1] = 63; z[:, 7, :, ::5] = 0
    th, best = tune(rng, x, rg, lv, z, w, kap); th[:, 0] = np.max(best[:, 0], axis=1) + 1; th[:, 4] = np.min(best[:, 4], axis=1); th[:, 1] = np.max(best[:, 1], axis=1)
    th = np.clip(th, 1, 1008)
    return pack(x, rg, lv, z, w, kap, th, close(th, best))
def setup_inputs_balance(rng):
    x, rg, lv, z, w, kap = parts(rng); far = np.arange(P) % Q < Q - 1; own = np.flatnonzero(~far); own = own[own >= P // 2]
    o = rng.permutation(N); m = int(o[2]); j = int(np.flatnonzero(o == (m - 3) % N)[0]); o[j] = o[1]; o[1] = (m - 3) % N
    tall = np.isin(np.arange(N), np.concatenate([o[:1], o[3::2]]))
    up = np.repeat(tall[:, None], 8, axis=1); up[m] = rng.permutation(8) < 4
    k = int(rng.choice(np.flatnonzero(up[m]))); dn = np.flatnonzero(~up[m]); dn = np.concatenate([dn[dn == (k - 1) % 8], dn[dn != (k - 1) % 8]])
    one = rng.integers(0, NB, (N, 8)); nil = (one + 1) % NB; near = (one + 2) % NB; dim = (one + 3) % NB
    n = rng.integers(1, 4, N); n[o[:3]] = 0; n[o[3]] = 1
    th = np.where(rng.integers(0, 2, (N, 8)) == 0, 1, 1008); th[:, k] = np.where(tall, 1008, 1); th[o[1], k - 1] = 1008; th[o[1], dn[2]] = 1; th[m, dn[2]] = 1008
    d = np.array([0, -1, 1, 0, -1, 0, -1, CM])
    cap = np.clip((CM - (Q - 1) * n)[:, None] + d[(np.arange(8)[None, :] + 3 * np.arange(N)[:, None]) % 8], 0, CM)
    cap[m] = rng.choice(np.array([0, 1, 2, CM]), 8); cap[m, dn[:2]] = 0; cap[m, dn[2]] = 1; cap[m, k] = 0
    lv[:, :, T0 - H:] = 1; lv[:, :, 0] = 0; lv[m, dn[:2]] = np.arange(T0) >= T0 - P
    z = np.array(np.broadcast_to(np.where(far, 0, 63), (N, 8, 16, P)))
    a = rng.integers(1, 4096, (N, 8, 8)); w[..., ::2] = a; w[..., 1::2] = 4096 - a; w[..., 14:] = 0
    for q in range(N):
        c = rng.permutation(own)
        for g in range(8):
            x[q, g, :, one[q, g]] = 63; x[q, g, :, nil[q, g]] = 0; x[q, g, :, near[q, g]] = 63; x[q, g, 15, near[q, g]] = 62
            x[q, g, :, dim[q, g]] = 0; x[q, g, 15, dim[q, g]] = 1
            rg[q, g, 0] = one[q, g]; rg[q, g, 1, 0] = one[q, g]; rg[q, g, 0, 0] = one[q, g] if up[q, g] else nil[q, g]
            if not up[q, g] and th[q, g] == 1008: z[q, g, :, c[0]] = 0; z[q, g, 15, c[0]] = 1
        for v in c[1:1 + int(n[q])]: z[q, int(rng.integers(0, 8)), :, v] = 0
    s = (m - 1) % N; i = P // 2 + Q * int(rng.integers(0, P // 2 // Q))
    rg[s, k, 0, T0 - H + i] = near[s, k]
    s = (m - 5) % N; i = Q * int(rng.integers(0, P // 2 // Q))
    rg[s, dn[2], 0, T0 - P // 2 + i] = dim[s, dn[2]]
    return pack(x, rg, lv, z, w, kap, th, cap)
def check_inputs(d):
    bad = []
    for k, lo, hi in (("x0", 0, 63), ("rings", 0, NB - 1), ("live", 0, 1), ("z", 0, 63), ("w", 0, 4095), ("kap", 0, 2047), ("th", 1, 1008), ("cap", 0, CM)):
        a = np.asarray(d[k]).astype(np.float64)
        if not (np.min(a) >= lo and np.max(a) <= hi): bad.append("range of " + k)
        elif np.any(a != np.floor(a)): bad.append("whole numbers of " + k)
    if np.min(np.add.reduce(np.asarray(d["live"]).astype(np.int64), axis=2)) < P: bad.append("live timelines")
    return bad
def reference(x0, rings, live, z, w, kap, th, cap):
    x, rg, lv, best, bal = play(x0.astype(np.float32).reshape(N, 8, 16, NB), rings.reshape(N, 8, 16, T0), live.reshape(N, 8, T0), z.astype(np.float32).reshape(N, 8, 16, P),
                                w.reshape(N, 8, 16), kap.reshape(N, 8, 16), th.reshape(N, 8), cap.reshape(N, 8), RO)
    return {"yx": x[..., NB:].reshape(N, 128, P * RO).astype(np.float32).astype(BF), "yt": rg[..., T0:].reshape(N, 128, P * RO).astype(np.float32), "ya": lv[..., T0:].reshape(N, 8, P * RO).astype(np.float32)}

@@ -1,0 +1,632 @@
+from concourse.mybir import AluOpType as ALU, AxisListType, ActivationFunctionType as AF
+
+NB, T0, P, RO = 4096, 1536, 256, 4
+BIG = float(2 ** 20)
+TAU = [(T0 + P * t) // 256 for t in range(RO)]
+DG0 = [sum(TAU[1:t]) for t in range(RO + 1)]
+CFG = dict(pv=8, mv=8, cy=1.04, g=1.56, sc=3.8, pe=0.52, sem=60.0, fix=40.0, dma=2000.0, bw=200.0, rem=2500.0,
+           iters=10, margin=300.0, seed=0, noise=100.0, ck=32, pool=1, sabs=1, rf=0, e0=6000, e1=0)
+PLAN = {}
+
+F32, BF, I32, U16, F16 = "float32", "bfloat16", "int32", "uint16", "float16"
+SCRATCH = {}
+for _n, _c, _d in [
+        ("RI", 1536, I32), ("LI", 1536, I32), ("SI", 8, I32), ("LB", 1536, BF), ("X", 5120, BF), ("R", 2560, F32),
+        ("RHI", 2304, BF), ("RLO", 2304, BF), ("XH0", 4352, BF), ("XH1", 4352, BF), ("RHS", 4352, F32),
+        ("D", 1920, F32), ("Z", 256, BF), ("ZR", 4096, BF), ("ZS", 256, BF), ("DX", 4096, BF), ("M", 4096, BF),
+        ("DX5", 4096, BF), ("M5", 4096, BF), ("YL", 256, BF),
+        ("PI", 8, I32), ("CC", 24, F32), ("S8", 8, F32), ("ZT", 256, BF), ("IF", 128, F32), ("TF", 256, F32),
+        ("XA", 144, F32), ("SEL", 144, BF), ("SELW", 144, F16), ("E8", 144, BF), ("E8F", 128, F32),
+        ("IB", 128, BF), ("NIB", 128, BF), ("BO", 128, BF), ("BOF", 128, F32), ("NU", 128, BF), ("SGN", 128, BF),
+        ("SH", 2048, BF), ("SHF", 128, F32), ("DGF", 768, F32), ("DG", 24 * 128, BF), ("MK", 40, F32),
+        ("JJ", 96, F32), ("KJ", 96, F32), ("CI", 16, F32), ("LN", 32, F32), ("NJ", 24, F32), ("NEG", 96, BF), ("RST", 256, F32),
+        ("IDX2", 128, BF), ("IDX5", 256, BF), ("PAYC", 256, F32), ("CN", 1024, F32), ("KAP", 256, F32), ("LT", 8, F32),
+        ("C1", 256, F32), ("C2", 256, F32), ("C3", 256, F32), ("C4", 256, F32), ("C5", 256, F32), ("C6", 256, BF), ("C7", 32, F32),
+        ("OZ", 256, U16), ("OC", 64, U16), ("DEAD", 160, BF), ("SC", 96, BF), ("E", 96, F32), ("E2", 96, F32),
+        ("DST", 96, U16), ("GO", 32, U16), ("OT", 256, U16), ("RR", 256, F32), ("O0", 256, U16), ("O1", 256, U16),
+        ("K0", 256, F32), ("K1", 256, F32), ("K2", 256, F32), ("K3", 256, F32), ("K4", 256, F32), ("K5", 256, F32), ("PAY", 256, F32),
+        ("A1", 32, I32), ("A2", 32, I32), ("A3", 8, I32), ("AU", 32, U16), ("TY", 256, BF), ("NY", 256, BF),
+        ("YS", 512, BF), ("YE", 1024, BF), ("UQ", 64, I32), ("H1", 256, F32), ("H2", 256, I32), ("H3", 256, I32),
+        ("HU", 256, U16), ("FK", 64, BF), ("SM", 64, F32), ("SN", 96, F32), ("OF", 16, U16), ("XI", 256, BF), ("XJ", 256, BF),
+        ("DU", 64, U16), ("YA", 1024, F32)]:
+    SCRATCH[_n] = ("sbuf", [128, _c], _d)
+for _b in range(8):
+    SCRATCH["B%d" % _b] = ("psum", [128, 512], F32)
+LOADS = ["ld%d" % i for i in range(10)]
+SEMAPHORES = ["cv", "cs", "ct", "cg", "out"] + LOADS + ["arr%d" % t for t in range(RO)] + ["snt%d" % t for t in range(RO)]
+WIDE = {F32: 4, BF: 2, I32: 4, U16: 2, F16: 2}
+
+
+def lay_out(ops):
+    n, sem = len(ops), CFG["sem"]
+    succ = [[] for _ in ops]
+    for i, o in enumerate(ops):
+        for d in o["deps"]:
+            succ[d].append(i)
+    rnd = [CFG["seed"] * 7919 + 1]
+
+    def draw():
+        rnd[0] = (rnd[0] * 1103515245 + 12345) % 2 ** 31
+        return rnd[0] / 2 ** 31
+
+    prio = [0.0] * n
+    for i in range(n - 1, -1, -1):
+        o = ops[i]
+        prio[i] = min(o["cost"].values()) + o["lat"] + max([prio[j] + (0 if ops[j]["deps"][i] == "o" else sem) for j in succ[i]] or [0])
+    fwd = [o["deps"] for o in ops]
+    bwd = [{j: ops[j]["deps"][i] for j in succ[i]} for i in range(n)]
+
+    def place(deps, seq, back):
+        fin, eng, start = [0.0] * n, [None] * n, [0.0] * n
+        busy = {q: [] for q in "vstgyr"}
+        for i in seq:
+            o, best = ops[i], None
+            for q, c in o["cost"].items():
+                r = 0.0
+                for d, k in deps[i].items():
+                    x = fin[d] - (0 if back else ops[d]["lat"]) if (k == "o" or (k == "rr" and eng[d] == q)) else fin[d] + sem
+                    if x > r:
+                        r = x
+                if back:
+                    r += o["lat"]
+                b = busy[q]
+                lo, hi = 0, len(b)
+                while lo < hi:
+                    mid = (lo + hi) // 2
+                    if b[mid][1] <= r:
+                        lo = mid + 1
+                    else:
+                        hi = mid
+                while lo < len(b) and b[lo][0] < r + c:
+                    r = max(r, b[lo][1])
+                    lo += 1
+                key = r + c + (CFG["margin"] if q == "v" else 0)
+                if best is None or key < best[0]:
+                    best = (key, q, r, c, lo)
+            _, q, r, c, lo = best
+            busy[q].insert(lo, (r, r + c))
+            eng[i], start[i] = q, r
+            fin[i] = r + c + (0 if back else o["lat"])
+        return start, fin, eng
+
+    def topo_order(deps, nxt, key):
+        left = [len(d) for d in deps]
+        cand = sorted(((key[i], i) for i in range(n) if left[i] == 0), reverse=True)
+        seq = []
+        while cand:
+            _, i = cand.pop()
+            seq.append(i)
+            new = False
+            for j in nxt[i]:
+                left[j] -= 1
+                if left[j] == 0:
+                    cand.append((key[j], j))
+                    new = True
+            if new:
+                cand.sort(reverse=True)
+        return seq
+
+    key, best = [-x for x in prio], None
+    for it in range(CFG["iters"]):
+        for i in range(n - 1, -1, -1):
+            key[i] = min([key[i] - ops[i].get("early", 0)] + [key[j] - 1 for j in succ[i]])
+        seq = topo_order(fwd, bwd, key)
+        start, fin, eng = place(fwd, seq, False)
+        if best is None or max(fin) < best[1]:
+            pos = {i: k for k, i in enumerate(seq)}
+            best = ([(i, eng[i]) for i in sorted(range(n), key=lambda i: (start[i], pos[i]))], max(fin))
+        _, fin, _ = place(bwd, topo_order(bwd, fwd, [-x + CFG["noise"] * draw() for x in fin]), True)
+        key = [-x + CFG["noise"] * draw() for x in fin]
+    return best
+
+
+def rank_program(g, core, T, topo):
+    rank = T.rank_of(core)
+    if rank is None:
+        return
+    N = len(T.cores)
+    PV, MV, CK, CY = CFG["pv"], CFG["mv"], CFG["ck"], CFG["cy"]
+    Q = {"v": g.vector, "s": g.scalar, "t": g.tensor, "g": g, "y": g.sync}
+    ops, hist = [], {}
+
+    def a(n, c0=0, c1=None, st=1, p=None):
+        where, shape, dty = SCRATCH[n]
+        c1 = shape[1] if c1 is None else c1
+        m = 0
+        if st == 1:
+            m = ((1 << (c1 - c0)) - 1) << c0
+        else:
+            for c in range(c0, c1, st):
+                m |= 1 << c
+        ps = slice(None) if p is None else p
+        ap = T[n][ps, c0:c1] if st == 1 else T[n][ps, c0:c1:st]
+        return {"ap": ap, "acc": [(n, m)], "n": len(range(c0, c1, st)), "w": WIDE[dty], "ps": where == "psum", "fl": dty in (F32, BF)}
+
+    def ind(win, off):
+        return {"ap": win["ap"].indirect(off["ap"]), "acc": win["acc"], "off": off["acc"], "n": 16 * off["n"], "w": win["w"], "ps": False}
+
+    def issue(fns, outs, ins, lat=0.0, sem=None, inc=1, grp=None, after=None):
+        acc = []
+        for o in outs:
+            acc += [(n, m, True) for n, m in o["acc"]] + [(n, m, False) for n, m in o.get("off", [])]
+        for i in ins:
+            if isinstance(i, dict):
+                acc += [(n, m, False) for n, m in i["acc"] + i.get("off", [])]
+        deps, me = {}, len(ops)
+        if after is not None:
+            deps[after] = "o"
+        for n, m, w in acc:
+            h = hist.setdefault(n, [])
+            if SCRATCH[n][0] == "psum":
+                for (m2, w2, d) in h:
+                    if d != me:
+                        k = "o" if grp is not None and ops[d]["grp"] == grp else ("w" if w or w2 else "rr")
+                        deps[d] = "w" if deps.get(d) == "w" else k
+                continue
+            for (m2, w2, d) in h:
+                if m & m2 and (w or w2) and d != me:
+                    deps[d] = "w"
+        for n, m, w in acc:
+            h = hist[n]
+            if SCRATCH[n][0] == "psum":
+                h[:] = [(m, w, me)]
+            else:
+                if w:
+                    h[:] = [e for e in h if e[0] & ~m]
+                h.append((m, w, me))
+        ops.append({"fn": {q: f for q, (f, c) in fns.items()}, "cost": {q: c for q, (f, c) in fns.items()}, "deps": deps,
+                    "lat": lat, "sem": sem, "inc": inc, "grp": grp})
+        return me
+
+    def sv(x):
+        return x["ap"] if isinstance(x, dict) else x
+
+    def cost(o, ins, per=None):
+        if "off" in o:
+            return 50 + o["n"] * CFG["sc"] * CY
+        if any("off" in i for i in ins):
+            return 55 + o["n"] * CFG["g"] * CY
+        if per is None:
+            per = 0.5 if all(x["w"] == 2 for x in [o] + ins) else 1
+        return CFG["fix"] + max(64, per * o["n"]) * CY
+
+    def f_cp(o, i):
+        return lambda: g.vector.tensor_copy(o["ap"], i["ap"]), cost(o, [i])
+
+    def f_ts(o, i, s1, op0, s2=None, op1=None):
+        if op1 is None:
+            return lambda: g.vector.tensor_scalar(o["ap"], i["ap"], sv(s1), None, op0), cost(o, [i])
+        return lambda: g.vector.tensor_scalar(o["ap"], i["ap"], sv(s1), sv(s2), op0, op1), cost(o, [i])
+
+    def f_act(o, i, f=AF.Copy, bias=None, scale=None):
+        if bias is not None and scale is not None:
+            return lambda: g.scalar.activation(o["ap"], i["ap"], f, bias=sv(bias), scale=sv(scale)), cost(o, [i], 1)
+        if bias is not None:
+            return lambda: g.scalar.activation(o["ap"], i["ap"], f, bias=sv(bias)), cost(o, [i], 1)
+        if scale is not None:
+            return lambda: g.scalar.activation(o["ap"], i["ap"], f, scale=sv(scale)), cost(o, [i], 1)
+        return lambda: g.scalar.activation(o["ap"], i["ap"], f), cost(o, [i], 1)
+
+    def cp(o, i):
+        issue({"v": f_cp(o, i)}, [o], [i])
+
+    def cp2(o, i):
+        fns = {"v": f_cp(o, i), "s": f_act(o, i)}
+        if CFG["pool"] and "off" not in i and not i["ps"]:
+            fns["g"] = (lambda: g.affine_select(o["ap"], i["ap"], [[0, o["n"]]], ALU.is_ge, 0.0, 0, 0), 170 + 2 * o["n"] * CY)
+        issue(fns, [o], [i])
+
+    def add2(o, i, col):
+        issue({"v": f_ts(o, i, col, ALU.add), "s": f_act(o, i, AF.Identity, bias=col)}, [o], [i, col])
+
+    def mul2(o, i, col):
+        issue({"v": f_ts(o, i, col, ALU.mult), "s": f_act(o, i, AF.Copy, scale=col)}, [o], [i, col])
+
+    def tt(o, i, j, op):
+        per = 1 if i["ps"] or j["ps"] or o["w"] + i["w"] + j["w"] == 6 else 2
+        issue({"v": (lambda: g.vector.tensor_tensor(o["ap"], i["ap"], j["ap"], op), cost(o, [i, j], per))}, [o], [i, j])
+
+    def ts(o, i, s1, op0, s2=None, op1=None):
+        fns = {"v": f_ts(o, i, s1, op0, s2, op1)}
+        if o["fl"] and i["fl"] and not any(isinstance(x, dict) and x["ps"] for x in (s1, s2)):
+            if op0 == ALU.mult and op1 is None:
+                fns["s"] = f_act(o, i, AF.Copy, scale=s1)
+            elif op0 == ALU.add and op1 is None:
+                fns["s"] = f_act(o, i, AF.Identity, bias=s1)
+            elif op0 == ALU.mult and op1 == ALU.add:
+                fns["s"] = f_act(o, i, AF.Identity, bias=s2, scale=s1)
+        issue(fns, [o], [i, s1, s2])
+
+    def scan(o, d0, d1, init, op0, op1):
+        issue({"v": (lambda: g.vector.tensor_tensor_scan(o["ap"], d0["ap"], d1["ap"], init, op0, op1), cost(o, [d0, d1]))}, [o], [d0, d1])
+
+    def ms(o, c):
+        issue({"v": (lambda: g.vector.memset(o["ap"], c), cost(o, []))}, [o], [])
+
+    def act(o, i, f=AF.Copy, bias=None, scale=None):
+        issue({"s": f_act(o, i, f, bias, scale)}, [o], [i, bias, scale])
+
+    gid = [0]
+
+    def mm1(o, l, r, first, last):
+        c = max(64, r["n"]) * CFG["pe"] * (4 if l["w"] == 4 else 1)
+        issue({"t": (lambda: g.tensor.matmul(o["ap"], l["ap"], r["ap"], first, last), c)}, [o], [l, r], grp=gid[0])
+
+    def mm(o, terms):
+        gid[0] += 1
+        for k, (l, r) in enumerate(terms):
+            mm1(o, l, r, k == 0, k == len(terms) - 1)
+
+    def iota(o, pat, base=0, cm=0):
+        if SCRATCH[o["acc"][0][0]][2] == I32:
+            f = lambda: g.iota(o["ap"], pat, base, cm)
+        else:
+            f = lambda: g.iota(o["ap"], pat, base, cm, allow_small_or_imprecise_dtypes=True)
+        issue({"g": (f, 130 + 2 * o["n"] * CY)}, [o], [])
+
+    def asel(o, pat, op, base, cm, i=None):
+        i = i or o
+        issue({"g": (lambda: g.affine_select(o["ap"], i["ap"], pat, op, 0.0, base, cm), 170 + 2 * o["n"] * CY)}, [o], [i])
+
+    nld = [0, None]
+
+    def load(q, o, src, nbytes):
+        s = LOADS[nld[0]]
+        nld[0] += 1
+        nld[1] = issue({q: (lambda: Q[q].dma_start(o["ap"], src), 100.0)}, [o], [], lat=CFG["dma"] + nbytes / CFG["bw"], sem=s, inc=16, after=nld[1])
+
+    def store(dst, i):
+        issue({"y": (lambda: g.sync.dma_start(dst, i["ap"]), 100.0)}, [], [i], lat=CFG["dma"] + 500, sem="out", inc=16)
+
+    cc = lambda k: a("CC", k, k + 1)
+    s8 = lambda k: a("S8", k, k + 1)
+    P8 = slice(0, 8)
+    sel = lambda n, p, pp=None: a(n, 15 - p, 143 - p, p=pp)
+
+    load("y", a("LI", p=P8), T.live[:], 49152)
+    load("y", a("RI", 0, 768), T.rings[:, 0:768], 440000)
+    load("y", a("RI", 768, T0), T.rings[:, 768:T0], 830000)
+    load("y", a("Z"), T.z[:], 900000)
+    load("y", a("X", 0, NB), T.x0[:], 1950000)
+    load("y", a("SI", 0, 1), T.w[:], 0)
+    load("y", a("SI", 1, 2), T.kap[:], 0)
+    load("y", a("SI", 2, 3, p=P8), T.th[:], 0)
+    load("y", a("SI", 3, 4, p=P8), T.cap[:], 0)
+
+    iota(a("PI", 0, 1), [[0, 1]], 0, 1)
+    iota(a("XA"), [[1, 144]])
+    iota(a("JJ"), [[16, 96]])
+    iota(a("TF", 0, 128), [[16, 8], [0, 16]])
+    iota(a("TF", 128, 144), [[1, 2], [4, 8]])
+    iota(a("TF", 144, 160), [[1, 2], [32, 8]])
+    ts(a("PI", 1, 2), a("PI", 0, 1), 15, ALU.bitwise_and)
+    ts(a("PI", 2, 3), a("PI", 0, 1), 7, ALU.bitwise_and)
+    ts(a("PI", 3, 4), a("PI", 0, 1), 3, ALU.logical_shift_right, 1, ALU.bitwise_and)
+    ts(a("PI", 4, 5), a("PI", 0, 1), 1, ALU.bitwise_and)
+    ms(a("NEG"), -1.0)
+    ms(a("IB"), 1.0)
+    cp(a("S8", 0, 5), a("PI", 0, 5))
+    ts(cc(1), s8(0), s8(1), ALU.subtract, 15.0, ALU.add)
+    ts(cc(2), s8(0), 16.0, ALU.mult, 15.0, ALU.add)
+    ts(cc(14), s8(0), s8(1), ALU.subtract)
+    ts(cc(4), s8(1), -16.0, ALU.add)
+    ts(a("E8", p=P8), a("XA", p=P8), a("CC", 2, 3, p=P8), ALU.is_equal)
+    cp(a("LB", p=P8), a("LI", p=P8))
+    mm(a("B7", 0, 96), [(sel("E8", p, P8), a("LB", p, T0, 16, p=P8)) for p in range(16)])
+    ts(a("BO"), a("TF", 0, 128), cc(14), ALU.is_equal)
+    ts(a("JJ"), a("JJ"), s8(1), ALU.add)
+    ts(a("NU"), a("BO"), -1.0, ALU.mult)
+    asel(a("NU"), [[-1, 128]], ALU.is_gt, 0, 1)
+    asel(a("IB"), [[-1, 128]], ALU.is_equal, 0, 1)
+    ts(cc(7), s8(2), 32.0, ALU.mult)
+    ts(cc(15), s8(3), 2.0, ALU.mult, cc(7), ALU.add)
+    ts(a("LN", 0, 16), a("TF", 128, 144), cc(15), ALU.add)
+    cp2(a("LN", 16, 32), a("JJ", 0, 16))
+    mul2(a("NJ"), a("JJ", 0, 24), -1.0)
+    cp(a("OZ", 0, 16), a("LN", 0, 16))
+    cp2(a("ZT"), ind(a("Z"), a("OZ", 0, 16)))
+    for k in range(16):
+        cp2(a("ZR", k, 4096, 16), a("ZT"))
+    ts(a("KJ"), a("JJ"), -1.0, ALU.mult, float(T0), ALU.add)
+    ts(a("DEAD", 0, 96), a("B7", 0, 96), -1.0, ALU.mult, 1.0, ALU.add)
+    scan(a("SC"), a("DEAD", 0, 96), a("NEG"), 0.0, ALU.add, ALU.add)
+    tt(a("E"), a("DEAD", 0, 96), a("KJ"), ALU.mult)
+    mm(a("B7", 0, 96), [(a("BO"), a("SC")), (a("NU"), a("DEAD", 0, 96))])
+    mm(a("B7", 96, 98), [(a("BO"), a("SC", 71, 96, 24))])
+    cp(a("R", 0, 768), a("RI", 0, 768))
+    cp(a("R", 768, T0), a("RI", 768, T0))
+    tt(a("E2"), a("E"), a("B7", 0, 96), ALU.subtract)
+    cp(a("SM", 0, 2), a("B7", 96, 98))
+    ts(a("DST"), a("E2"), cc(4), ALU.add)
+    for c in range(0, 96, 24):
+        cp(ind(a("D", 384, 1920), a("DST", c, c + 24)), a("R" if c >= CFG["rf"] else "RI", 16 * c, 16 * c + 384))
+    for d in range(TAU[0]):
+        asel(a("DGF", 128 * d, 128 * d + 128), [[0, 8], [TAU[0], 16]], ALU.is_ge, -16 * d, 0, a("IB"))
+        asel(a("DGF", 128 * d, 128 * d + 128), [[0, 8], [-TAU[0], 16]], ALU.is_ge, 16 * d + 15, 0)
+    mm(a("B6", 0, 256), [(a("DGF", 128 * d, 128 * d + 128), a("R", d, T0, TAU[0])) for d in range(TAU[0])])
+
+    def places_x(t, c0, c1, nb):
+        cp(a("O%d" % (t % 2), c0, c1), a("B6", 0, c1 - c0))
+        ops[-1]["early"] = CFG["e0"] if t == 0 else CFG["e1"]
+        for c in range(c0, c1, CK):
+            e = min(c + CK, c1)
+            cp2(a("XH%d" % (t % 2), 16 * c, 16 * e), ind(a("X", 0, nb), a("O%d" % (t % 2), c, e)))
+
+    places_x(0, 0, 256, NB)
+    ts(a("SM", 2, 3), a("SM", 1, 2), a("SM", 0, 1), ALU.subtract)
+    ts(a("SM", 3, 4), a("SM", 1, 2), -1.0, ALU.mult)
+    ts(a("SN", 0, 32), a("LN"), a("SM", 2, 3), ALU.add)
+    ts(a("SN", 32, 64), a("SN", 0, 32), 0.0, ALU.is_lt, a("SM", 3, 4), ALU.mult)
+    tt(a("SN", 64, 96), a("SN", 0, 32), a("SN", 32, 64), ALU.add)
+    cp(a("GO"), a("SN", 64, 96))
+    ts(a("SEL"), a("XA"), cc(1), ALU.is_equal, BIG, ALU.mult)
+    ts(a("NIB"), a("IB"), -1.0, ALU.mult)
+    ts(a("IDX2"), a("XA", 0, 128), 8192.0, ALU.mult)
+    ms(cc(21), 127.75)
+    ms(cc(22), -128.0)
+    ms(cc(16), float(2 ** 40))
+    ts(cc(6), s8(1), 128.0, ALU.mult)
+    ts(cc(12), s8(1), 2.0, ALU.mult)
+    ts(a("OC", 0, 16), a("TF", 144, 160), cc(12), ALU.add)
+    iota(a("C5"), [[0, 16], [1, 16]])
+    act(a("RST"), a("C5"), AF.Relu, bias=cc(16), scale=-float(2 ** 40))
+    cp2(a("ZS"), ind(a("Z"), a("OC", 0, 16)))
+    asel(a("ZS"), [[0, 16], [1, 16]], ALU.is_ge, -PV, 0)
+    ts(a("PAYC"), a("C5"), -4096.0, ALU.mult, 15 * 4096.0, ALU.add)
+    iota(a("C1"), [[1, 16], [0, 16]])
+    iota(a("C3", 0, 128), [[0, 64], [-2, 2]], 1)
+    cp(a("S8", 6, 8), a("SI", 0, 2))
+    ts(cc(8), s8(6), 2048.0, ALU.is_ge, -4096.0, ALU.mult)
+    ts(cc(9), s8(6), cc(8), ALU.add)
+    ts(a("SELW"), a("XA"), cc(1), ALU.is_equal, cc(9), ALU.mult)
+    mul2(a("IDX5"), a("C1"), 65536.0)
+    ts(a("C4"), a("C1"), s8(1), ALU.is_equal, s8(7), ALU.mult)
+    cp2(a("BOF"), a("BO"))
+    mm(a("B5", 0, 256), [(a("BOF"), a("C4"))])
+    cp2(a("KAP"), a("B5", 0, 256))
+    ts(cc(13), s8(1), 0.0, ALU.is_equal)
+    for t in range(RO):
+        iota(a("CN", P * t, P * t + P), [[1, P]], NB + P * t)
+        mul2(a("CN", P * t, P * t + P), a("CN", P * t, P * t + P), cc(13))
+    ts(cc(3), s8(4), -2.0, ALU.mult, 1.0, ALU.add)
+    mul2(a("SGN"), a("C3", 0, 128), cc(3))
+    ts(cc(5), s8(1), 368.0, ALU.add)
+    ts(cc(20), s8(1), 16.0, ALU.mult)
+    ts(a("OC", 16, 32), a("XA", 0, 16), 0.0, ALU.mult, s8(1), ALU.add)
+    ts(a("OC", 32, 48), a("XA", 0, 16), cc(20), ALU.add)
+    ts(a("CI"), a("JJ", 0, 16), 4096.0, ALU.add)
+    ts(a("LT"), a("XA", 0, 8), -1.0, ALU.mult, 1.0, ALU.add)
+    cp(a("C7", 4, 6, p=P8), a("SI", 2, 4, p=P8))
+    ts(a("E8F", p=P8), a("TF", 0, 128, p=P8), 15.0, ALU.add, a("CC", 2, 3, p=P8), ALU.is_equal)
+    mm(a("B4", 0, 2), [(a("E8F", p=P8), a("C7", 4, 6, p=P8))])
+    ts(cc(10), a("B4", 0, 1), BIG, ALU.mult)
+    cp(cc(11), a("B4", 1, 2))
+    for c in range(0, 16, 2):
+        sh = a("SH", 128 * c, 128 * c + 256)
+        iota(sh, [[1, 2], [0, 8], [1, 16]], c - 1)
+        ts(sh, sh, 15.0, ALU.min, s8(1), ALU.is_equal)
+        asel(sh, [[0, 2], [-16, 8], [0, 16]], ALU.is_ge, 0, 1)
+        asel(sh, [[0, 2], [16, 8], [0, 16]], ALU.is_ge, 15, -1)
+    cp2(a("SHF"), a("SH", 0, 128))
+    cp2(a("IF"), a("IB"))
+    for t in range(1, RO):
+        for d in range(TAU[t]):
+            c = 128 * (DG0[t] + d)
+            asel(a("DG", c, c + 128), [[0, 8], [TAU[t], 16]], ALU.is_ge, -16 * d, 0, a("IB"))
+            asel(a("DG", c, c + 128), [[0, 8], [-TAU[t], 16]], ALU.is_ge, 16 * d + 15, 0)
+
+    def hilo(c0, c1):
+        cp2(a("RHI", c0, c1), a("R", c0, c1))
+        mm(a("B6", 0, c1 - c0), [(a("IF"), a("R", c0, c1)), (a("NIB"), a("RHI", c0, c1))])
+        cp2(a("RLO", c0, c1), a("B6", 0, c1 - c0))
+
+    for c in range(0, T0, 256):
+        hilo(c, c + 256)
+
+    def places_o(t, c0, c1):
+        tau = TAU[t]
+        terms = []
+        for d in range(tau):
+            for n in ("RHI", "RLO"):
+                terms.append((a("DG", 128 * (DG0[t] + d), 128 * (DG0[t] + d) + 128), a(n, c0 * tau + d, c1 * tau, tau)))
+        mm(a("B6", 0, c1 - c0), terms)
+
+    def tails(t, ages):
+        tau = TAU[t]
+        for ag in ages:
+            b = "B%d" % (4 + ag % 2)
+            d = ag * tau >> 4
+            mm(a(b, 0, 256), [(a("SH", 128 * ag, 128 * ag + 128), a(n, d, 256 * tau, tau)) for n in ("RHI", "RLO")])
+            cp2(a("RHS", ag, 4096, 16), a(b, 0, 256))
+
+    old = lambda t: (((T0 + P * (t - 1)) // TAU[t]) // 2) * 2
+
+    def s2(t, h, p0, p1, b):
+        c0, c1 = 128 * h + 8 * p0, 128 * h + 8 * p1
+        act(a("DX", 16 * c0, 16 * c1), ind(a("X", 0, NB + P * t), a("OT", c0, c1)))
+        mm(a(b, 0, 16 * (c1 - c0)), [(a("IB"), a("ZR", 16 * c0, 16 * c1)), (a("NIB"), a("DX", 16 * c0, 16 * c1))])
+        act(a("M", 16 * c0, 16 * c1), a(b, 0, 16 * (c1 - c0)), AF.Relu)
+
+    def v2(t, h, p0, p1):
+        c0, c1 = 128 * h + 8 * p0, 128 * h + 8 * p1
+        d, m = a("DX", 16 * c0, 16 * c1), a("M", 16 * c0, 16 * c1)
+        tt(d, ind(a("X", 0, NB + P * t), a("OT", c0, c1)), a("ZR", 16 * c0, 16 * c1), ALU.subtract)
+        ts(m, d, -1.0, ALU.mult, 0.0, ALU.max)
+
+    def step2(t, h):
+        pm, sm = (PV + 1) // 2, min(PV + 4, 16)
+        v2(t, h, 0, pm)
+        s2(t, h, PV, sm, "B2")
+        v2(t, h, pm, PV)
+        for k, p0 in enumerate(range(sm, 16, 4)):
+            s2(t, h, p0, min(p0 + 4, 16), "B%d" % (3 - k % 2))
+        order = list(range(0, pm)) + list(range(PV, sm)) + list(range(pm, PV)) + list(range(sm, 16))
+        mm(a("B%d" % h, 0, 128), [(a("IB"), a("IDX2"))] +
+           [(sel("SEL", p), a("M", 2048 * h + 128 * p, 2048 * h + 128 * p + 128)) for p in order])
+        c = 128 * h
+        scan(a("K0", c, c + 128), a("RST", 0, 128), a("B%d" % h, 0, 128), 0.0, ALU.add, ALU.min)
+        cp(a("A1", 8 * h, 8 * h + 8), a("K0", c + 15, c + 128, 16))
+        ts(a("A2", 8 * h, 8 * h + 8), a("A1", 8 * h, 8 * h + 8), 13, ALU.logical_shift_right, 127, ALU.bitwise_and)
+        ts(a("AU", 8 * h, 8 * h + 8), a("A2", 8 * h, 8 * h + 8), cc(6), ALU.add)
+        tt(a("TY", c, c + 128), ind(a("DX", 2048 * h, 2048 * h + 2048), a("AU", 8 * h, 8 * h + 8)), a("ZS", c, c + 128), ALU.subtract)
+        dst = a("YS", 128 * t, 128 * t + 128) if h == 0 else a("YE", 256 * t + 128, 256 * t + 256)
+        if CFG["sabs"]:
+            act(dst, a("TY", c, c + 128), AF.Abs)
+        else:
+            ts(a("NY", c, c + 128), a("TY", c, c + 128), -1.0, ALU.mult)
+            tt(dst, a("TY", c, c + 128), a("NY", c, c + 128), ALU.max)
+
+    def move(t):
+        to = T.cores[(rank + 1 + t % (N - 1)) % N]
+        fr = T.cores[(rank - 1 - t % (N - 1)) % N]
+        rid, pid, _ = topo.addr(to)
+        eng = topo.engines(core, to)[::2]
+        mask = sum(1 << e for e in eng)
+        src, dst = a("YS", 128 * t, 128 * t + 128), a("YE", 256 * t, 256 * t + 128)
+
+        def send():
+            g.remote_dma(dst["ap"], src["ap"], T.sem["arr%d" % t], T.sem["snt%d" % t], pid, rid, mask)
+
+        me = issue({"g": (send, 300.0)}, [], [src], sem="snt%d" % t, inc=len(eng))
+        issue({"r": (lambda: None, 0.0)}, [dst], [], lat=CFG["rem"] + 300, sem="arr%d" % t, inc=len(topo.engines(fr, core)[::2]), after=me)
+
+    for t in range(RO):
+        Tt = T0 + P * t
+        XH = "XH%d" % (t % 2)
+        last = t == RO - 1
+        dw0 = a("D", 384, 1920) if t == 0 else a("D", 0, 640)
+        cp(a("OT", 0, 128), ind(dw0, a("GO", 0, 8)))
+        cp(a("OT", 128, 256), ind(dw0, a("GO", 8, 16)))
+        step2(t, 0)
+        move(t)
+        step2(t, 1)
+        if t:
+            hilo(Tt - P, Tt)
+            places_o(t, old(t), 256)
+            places_x(t, old(t), 256, NB + P * t)
+        if not last:
+            places_o(t + 1, 0, old(t + 1))
+            places_x(t + 1, 0, old(t + 1), NB + P * t)
+        cp2(a("RR"), ind(dw0, a("GO", 16, 32)))
+        mm(a("B1", 0, 256), [(a("SHF"), a("RR"))])
+        cp2(a("RHS", 4096, 4352), a("B1", 0, 256))
+        tails(t, range(0, 16))
+        ye = 256 * t
+        po = list(range(1, 16, 2)) + list(range(0, 16, 2))
+        mm(a("B7", 0, 16), [(sel("SELW", p), a("YE", ye + (p % 2) * 128 + p // 2, ye + (p % 2) * 128 + 128, 8)) for p in po])
+        Y = a("YL")
+        cp2(a("YL", 1, 256, 2), a("YE", ye + 128, ye + 256))
+        cp2(a("YL", 0, 256, 2), a("YE", ye, ye + 128))
+        cp2(a(XH, 4096, 4352), Y)
+        cp(a("UQ", 32, 48), a("B7", 0, 16))
+        ts(a("UQ", 0, 16), a("UQ", 32, 48), 4095, ALU.bitwise_and)
+        tt(a("UQ", 48, 64), a("UQ", 0, 16), a("UQ", 0, 16), ALU.mult)
+        tt(a("H1"), ind(a("UQ", 0, 16), a("OC", 16, 32)), a("KAP"), ALU.mult)
+        ts(a("UQ", 16, 32), a("UQ", 48, 64), 5, ALU.logical_shift_right)
+        tt(a("H2"), ind(a("UQ", 16, 32), a("OC", 16, 32)), a("H1"), ALU.add)
+        ts(a("H3"), a("H2"), 4095, ALU.bitwise_and)
+        cp(a("HU"), a("H3"))
+        win = a(XH, 0, 4096)
+
+        def v5(m0, m1):
+            for m in range(m0, m1):
+                tt(a("DX5", 256 * m, 256 * m + 256), ind(win, a("HU", 16 * m, 16 * m + 16)), Y, ALU.subtract)
+            ts(a("M5", 256 * m0, 256 * m1), a("DX5", 256 * m0, 256 * m1), 0.0, ALU.min, -2.0, ALU.mult)
+
+        def s5(m0, m1, b):
+            act(a("DX5", 256 * m0, 256 * m1), ind(win, a("HU", 16 * m0, 16 * m1)))
+            for m in range(m0, m1):
+                mm(a(b, 256 * (m - m0), 256 * (m - m0) + 256), [(a("NIB"), Y), (a("IB"), a("DX5", 256 * m, 256 * m + 256))])
+            act(a("M5", 256 * m0, 256 * m1), a(b, 0, 256 * (m1 - m0)), AF.Abs)
+
+        def sc5(m0, m1, both):
+            terms = [(a("IB"), a("IDX5", 16 * m0, 16 * m1))]
+            for n in (("DX5", "M5") if both else ("M5",)):
+                terms += [(sel("SEL", p), a(n, 256 * m0 + p, 256 * m1, 16)) for p in range(16)]
+            mm(a("B0", 16 * m0, 16 * m1), terms)
+
+        vm, sm = (MV + 1) // 2, (MV + 16) // 2
+        v5(0, vm)
+        sl = list(range(MV, 16, 2))
+        for k, m in enumerate(sl):
+            s5(m, min(m + 2, 16), "B%d" % (2 + k % 2))
+        v5(vm, MV)
+        sm = sl[len(sl) // 2]
+        sc5(0, vm, True)
+        sc5(MV, sm, False)
+        sc5(vm, MV, True)
+        sc5(sm, 16, False)
+        tt(a("PAY"), ind(a("H3"), a("OC", 32, 48)), a("PAYC"), ALU.add)
+        cp2(a("K2"), a("B0", 0, 256))
+        cp2(a("K3"), ind(a("K2"), a("OC", 32, 48)))
+        scan(a("B1", 0, 256), a("RST"), a("K3"), 0.0, ALU.add, ALU.min)
+        best = a("B1", 15, 256, 16)
+        fk = a("FK", 16 * t, 16 * t + 16)
+        ts(fk, best, cc(10), ALU.is_lt)
+        mm(a("B7", 0, 16 * t + 16), [(a("SGN"), a("FK", 0, 16 * t + 16))])
+        tt(a("K5"), a("K3"), a("B1", 0, 256), ALU.subtract)
+        ts(a("SM", 16, 32), best, cc(10), ALU.is_ge)
+        sb, b7 = a("SM", 6, 7), a("B7", 0, 16 * t + 16)
+        issue({"v": (lambda sb=sb, b7=b7: g.vector.tensor_reduce(sb["ap"], b7["ap"], AxisListType.X, ALU.add), cost(b7, []))}, [sb], [b7])
+        scan(a("K4"), a("K5"), a("PAY"), 0.0, ALU.min, ALU.max)
+        dc = Tt // 16
+        ts(a("DEAD", dc, dc + 16), fk, sb, ALU.mult, cc(11), ALU.is_gt)
+        cp(a("A1", 16, 32), a("K4", 15, 256, 16))
+        ts(a("A2", 16, 32), a("A1", 16, 32), 4095, ALU.bitwise_and)
+        tt(a("SM", 32, 48), a("SM", 16, 32), a("CI"), ALU.mult)
+        tt(a("SM", 48, 64), a("A2", 16, 32), a("SM", 32, 48), ALU.max)
+        cp(a("OF"), a("SM", 48, 64))
+        tt(a("R", Tt, Tt + P), ind(a("RHS"), a("OF")), a("CN", P * t, P * t + P), ALU.max)
+        store(T.yt[:, P * t:P * t + P], a("R", Tt, Tt + P))
+        act(a("XI"), ind(a(XH), a("OF")))
+        mm(a("B1", 0, 256), [(a("IB"), Y), (a("IB"), a("XI"))])
+        act(a("XJ"), a("B1", 0, 256), AF.Identity, bias=cc(21), scale=0.5)
+        act(a("X", NB + P * t, NB + P * t + P), a("XJ"), AF.Identity, bias=cc(22))
+        store(T.yx[:, P * t:P * t + P], a("X", NB + P * t, NB + P * t + P))
+        cp(a("DU", 16 * t, 16 * t + 16), a("DEAD", dc, dc + 16))
+        cp2(a("YA", P * t, P * t + P), ind(a("LT"), a("DU", 16 * t, 16 * t + 16)))
+        store(T.ya[:, P * t:P * t + P], a("YA", P * t, P * t + P, p=slice(0, 128, 16)))
+        if not last:
+            dw = a("DEAD", dc - 8, dc + 16)
+            scan(a("SC", 0, 24), dw, a("NEG", 0, 24), 0.0, ALU.add, ALU.add)
+            mm(a("B7", 0, 24), [(a("NU"), dw), (a("BO"), a("SC", 0, 24))])
+            mm(a("B7", 24, 25), [(a("BO"), a("SC", 23, 24))])
+            tt(a("E", 0, 24), dw, a("NJ"), ALU.mult)
+            tt(a("E2", 0, 24), a("E", 0, 24), a("B7", 0, 24), ALU.subtract)
+            ts(a("DST", 0, 24), a("E2", 0, 24), a("B7", 24, 25), ALU.add, cc(5), ALU.add)
+            ts(a("GO"), a("LN"), a("B7", 24, 25), ALU.add, 384.0, ALU.add)
+            cp(ind(a("D", 0, 384), a("DST", 0, 24)), a("R", Tt - 128, Tt + P))
+
+    if "order" not in PLAN:
+        PLAN["order"], PLAN["time"] = lay_out(ops)
+    cnt, clock, mark, snap, eng = {}, {q: {} for q in Q}, {}, {}, {}
+
+    def wait(q, sem, val):
+        if clock[q].get(sem, 0) < val:
+            Q[q].wait_ge(T.sem[sem], val)
+            clock[q][sem] = val
+            for s2_, v2_ in snap.get((sem, val), {}).items():
+                clock[q][s2_] = max(clock[q].get(s2_, 0), v2_)
+
+    for i, q in PLAN["order"]:
+        o = ops[i]
+        eng[i] = q
+        sem = o["sem"] or "c" + q
+        cnt[sem] = cnt.get(sem, 0) + o["inc"]
+        mark[i] = (sem, cnt[sem])
+        if q == "r":
+            continue
+        need = {}
+        for d, k in o["deps"].items():
+            if k == "w" or (k == "rr" and eng[d] != q):
+                need[mark[d][0]] = max(need.get(mark[d][0], 0), mark[d][1])
+        for s_ in sorted(need, key=lambda s_: s_ == "c" + q):
+            wait(q, s_, need[s_])
+        call = o["fn"][q]()
+        if call is not None:
+            call.then_inc(T.sem[sem], o["inc"])
+        snap[mark[i]] = dict(clock[q])
+    for s_ in sorted(cnt):
+        if s_ != "out" and not any(clock[q].get(s_, 0) >= cnt[s_] for q in "vstg"):
+            wait("g", s_, cnt[s_])
+    g.sync.wait_ge(T.sem["out"], cnt["out"])

@@ -1,11 +1,13 @@
 from concourse.mybir import AluOpType as ALU, AxisListType, ActivationFunctionType as AF
 
 NB, T0, P, RO = 4096, 1536, 256, 4
-BIG = float(2 ** 20)
+BIG = float(2 ** 21)
 TAU = [(T0 + P * t) // 256 for t in range(RO)]
 DG0 = [sum(TAU[1:t]) for t in range(RO + 1)]
-CFG = dict(pv=8, mv=8, cy=1.04, g=1.56, sc=3.8, pe=0.52, sem=60.0, fix=40.0, dma=2000.0, bw=200.0, rem=2500.0,
-           iters=10, margin=300.0, seed=0, noise=100.0, ck=32, pool=1, sabs=1, rf=0, e0=6000, e1=0)
+CFG = dict(pv=8, mv=8, cy=0.83, g=1.56, sc=3.8, pe=0.42, sem=100.0, fix=40.0, dma=2000.0, bw=200.0, rem=2500.0,
+           views=[(1, 0, 1, 0, 200.0, 1, 1), (1.4, 0, 1.4, 0, 180.0, 1.2, 1.3),
+                  (1.25, 0, 1.25, 0, 220.0, 0.8, 0.7), (1.2, 0, 1.2, 0, 160.0, 1.15, 0.9)],
+           starts=24, iters=5, tries=25000, temp=600.0, pelo=1, yr=2, margin=300.0, seed=0, noise=100.0, ck=32, pool=1, sabs=1, rf=0, e0=6000, e1=0)
 PLAN = {}
 
 F32, BF, I32, U16, F16 = "float32", "bfloat16", "int32", "uint16", "float16"
@@ -14,12 +16,12 @@ for _n, _c, _d in [
         ("RI", 1536, I32), ("LI", 1536, I32), ("SI", 8, I32), ("LB", 1536, BF), ("X", 5120, BF), ("R", 2560, F32),
         ("RHI", 2304, BF), ("RLO", 2304, BF), ("XH0", 4352, BF), ("XH1", 4352, BF), ("RHS", 4352, F32),
         ("D", 1920, F32), ("Z", 256, BF), ("ZR", 4096, BF), ("ZS", 256, BF), ("DX", 4096, BF), ("M", 4096, BF),
-        ("DX5", 4096, BF), ("M5", 4096, BF), ("YL", 256, BF),
+        ("DX5", 4096, BF), ("M5", 4096, BF), ("YL", 1024, BF),
         ("PI", 8, I32), ("CC", 24, F32), ("S8", 8, F32), ("ZT", 256, BF), ("IF", 128, F32), ("TF", 256, F32),
         ("XA", 144, F32), ("SEL", 144, BF), ("SELW", 144, F16), ("E8", 144, BF), ("E8F", 128, F32),
         ("IB", 128, BF), ("NIB", 128, BF), ("BO", 128, BF), ("BOF", 128, F32), ("NU", 128, BF), ("SGN", 128, BF),
         ("SH", 2048, BF), ("SHF", 128, F32), ("DGF", 768, F32), ("DG", 24 * 128, BF), ("MK", 40, F32),
-        ("JJ", 96, F32), ("KJ", 96, F32), ("CI", 16, F32), ("LN", 32, F32), ("NJ", 24, F32), ("NEG", 96, BF), ("RST", 256, F32),
+        ("JJ", 96, F32), ("KJ", 96, F32), ("CI", 16, F32), ("LN", 32, F32), ("NBO", 128, BF), ("N16", 128, BF), ("PU", 128, BF), ("NEG", 96, BF), ("RST", 256, F32),
         ("IDX2", 128, BF), ("IDX5", 256, BF), ("PAYC", 256, F32), ("CN", 1024, F32), ("KAP", 256, F32), ("LT", 8, F32),
         ("C1", 256, F32), ("C2", 256, F32), ("C3", 256, F32), ("C4", 256, F32), ("C5", 256, F32), ("C6", 256, BF), ("C7", 32, F32),
         ("OZ", 256, U16), ("OC", 64, U16), ("DEAD", 160, BF), ("SC", 96, BF), ("E", 96, F32), ("E2", 96, F32),
@@ -53,6 +55,7 @@ def lay_out(ops):
     for i in range(n - 1, -1, -1):
         o = ops[i]
         prio[i] = min(o["cost"].values()) + o["lat"] + max([prio[j] + (0 if ops[j]["deps"][i] == "o" else sem) for j in succ[i]] or [0])
+    cur = [None, 0.0, 0.0]
     fwd = [o["deps"] for o in ops]
     bwd = [{j: ops[j]["deps"][i] for j in succ[i]} for i in range(n)]
 
@@ -61,10 +64,10 @@ def lay_out(ops):
         busy = {q: [] for q in "vstgyr"}
         for i in seq:
             o, best = ops[i], None
-            for q, c in o["cost"].items():
+            for q, c in cur[0][i].items():
                 r = 0.0
                 for d, k in deps[i].items():
-                    x = fin[d] - (0 if back else ops[d]["lat"]) if (k == "o" or (k == "rr" and eng[d] == q)) else fin[d] + sem
+                    x = fin[d] - (0 if back else ops[d]["lat"]) if (k == "o" or (k == "rr" and eng[d] == q)) else fin[d] + cur[1]
                     if x > r:
                         r = x
                 if back:
@@ -80,7 +83,7 @@ def lay_out(ops):
                 while lo < len(b) and b[lo][0] < r + c:
                     r = max(r, b[lo][1])
                     lo += 1
-                key = r + c + (CFG["margin"] if q == "v" else 0)
+                key = r + c + (cur[2] if q == "v" else 0)
                 if best is None or key < best[0]:
                     best = (key, q, r, c, lo)
             _, q, r, c, lo = best
@@ -106,17 +109,99 @@ def lay_out(ops):
                 cand.sort(reverse=True)
         return seq
 
-    key, best = [-x for x in prio], None
-    for it in range(CFG["iters"]):
-        for i in range(n - 1, -1, -1):
-            key[i] = min([key[i] - ops[i].get("early", 0)] + [key[j] - 1 for j in succ[i]])
-        seq = topo_order(fwd, bwd, key)
-        start, fin, eng = place(fwd, seq, False)
-        if best is None or max(fin) < best[1]:
-            pos = {i: k for k, i in enumerate(seq)}
-            best = ([(i, eng[i]) for i in sorted(range(n), key=lambda i: (start[i], pos[i]))], max(fin))
-        _, fin, _ = place(bwd, topo_order(bwd, fwd, [-x + CFG["noise"] * draw() for x in fin]), True)
-        key = [-x + CFG["noise"] * draw() for x in fin]
+    def priced(h):
+        f = {"v": (h[0], h[1]), "s": (h[0], h[1]), "g": (h[0], 0), "t": (h[2], h[3])}
+        return [{q: c * f.get(q, (1, 0))[0] * (1, h[5], h[6])[o["ix"]] + f.get(q, (1, 0))[1] for q, c in o["cost"].items()} for o in ops]
+
+    hard = [[d for d, k in f.items() if k == "w"] for f in fwd]
+    soft = [[(d, k) for d, k in f.items() if k != "w"] for f in fwd]
+    lats = [o["lat"] for o in ops]
+
+    def replay(order, cs, wake, pairs=None):
+        fin, end, eng, free = [0.0] * n, [0.0] * n, [None] * n, {q: 0.0 for q in "vstgyr"}
+        why, prev = [None] * n, {}
+        for i, q in order:
+            r, y = free[q], None
+            for d in hard[i]:
+                if fin[d] > r:
+                    r, y = fin[d], d
+            for d, k in soft[i]:
+                x = end[d] if (k == "o" or eng[d] == q) else fin[d]
+                if x > r:
+                    r, y = x, d
+            eng[i] = q
+            free[q] = end[i] = r + cs[i][q]
+            fin[i] = end[i] + lats[i] + wake
+            if pairs is not None:
+                why[i] = (y, False) if y is not None else (prev.get(q), True)
+                prev[q] = i
+        if pairs is not None:
+            i = fin.index(max(fin))
+            while why[i][0] is not None:
+                if why[i][1]:
+                    pairs.append((why[i][0], i))
+                i = why[i][0]
+        return max(fin)
+
+    views = [(priced(h), h[4]) for h in CFG["views"]]
+    best = None
+    for rs in range(CFG["starts"]):
+        h = CFG["views"][rs % len(views)]
+        cur[0], cur[1], cur[2] = views[rs % len(views)][0], h[4], CFG["margin"] * 2 * draw()
+        key, nz = [-x for x in prio], CFG["noise"] * 2 * draw()
+        for it in range(CFG["iters"]):
+            for i in range(n - 1, -1, -1):
+                key[i] = min([key[i] - ops[i].get("early", 0)] + [key[j] - 1 for j in succ[i]])
+            seq = topo_order(fwd, bwd, key)
+            start, fin, eng = place(fwd, seq, False)
+            if it:
+                pos = {i: k for k, i in enumerate(seq)}
+                order = [(i, eng[i]) for i in sorted(range(n), key=lambda i: (start[i], pos[i]))]
+                tm = [replay(order, cs, w) for cs, w in views]
+                if best is None or sum(tm) < sum(best[1]):
+                    best = (order, tm)
+            _, fin, _ = place(bwd, topo_order(bwd, fwd, [-x + nz * draw() for x in fin]), True)
+            key = [-x + nz * draw() for x in fin]
+    now = None
+    for rs in range(CFG["tries"]):
+        if now is None or rs % 8 == 0:
+            now = now or best
+            pairs = []
+            replay(now[0], *views[int(len(views) * draw())], pairs)
+            pos = {i: k for k, (i, q) in enumerate(now[0])}
+        order = list(now[0])
+        i, j = pairs[int(len(pairs) * draw())]
+        k, q, u = pos[i], order[pos[i]][1], draw()
+        if u < 0.3 and len(ops[i]["cost"]) > 1:
+            qs = [x for x in sorted(ops[i]["cost"]) if x != q]
+            order[k] = (i, qs[int(len(qs) * draw())])
+        else:
+            hops, m, to = 1 + int(4 * draw() * draw()), k + 1, None
+            while m < n and hops and order[m][0] not in bwd[i]:
+                if order[m][1] == q:
+                    hops, to = hops - 1, m
+                m += 1
+            if to is None:
+                m = pos[j] - 1
+                while m >= k and order[m][0] not in fwd[j]:
+                    m -= 1
+                if m >= k:
+                    continue
+                order.insert(k, order.pop(pos[j]))
+            else:
+                order.insert(to, order.pop(k))
+        tm = []
+        for cs, w in views:
+            tm.append(replay(order, cs, w))
+            if tm[-1] > now[1][len(tm) - 1] + 600:
+                break
+        if len(tm) == len(views) and sum(tm) <= sum(now[1]) + CFG["temp"] * draw() * (1 - rs / CFG["tries"]):
+            now = (order, tm)
+            pairs = []
+            replay(order, *views[int(len(views) * draw())], pairs)
+            pos = {i: k for k, (i, q) in enumerate(order)}
+            if sum(tm) < sum(best[1]):
+                best = now
     return best
 
 
@@ -175,7 +260,8 @@ def rank_program(g, core, T, topo):
                     h[:] = [e for e in h if e[0] & ~m]
                 h.append((m, w, me))
         ops.append({"fn": {q: f for q, (f, c) in fns.items()}, "cost": {q: c for q, (f, c) in fns.items()}, "deps": deps,
-                    "lat": lat, "sem": sem, "inc": inc, "grp": grp})
+                    "lat": lat, "sem": sem, "inc": inc, "grp": grp,
+                    "ix": 2 if any("off" in o for o in outs) else int(any(isinstance(i, dict) and "off" in i for i in ins))})
         return me
 
     def sv(x):
@@ -322,7 +408,10 @@ def rank_program(g, core, T, topo):
     ts(cc(15), s8(3), 2.0, ALU.mult, cc(7), ALU.add)
     ts(a("LN", 0, 16), a("TF", 128, 144), cc(15), ALU.add)
     cp2(a("LN", 16, 32), a("JJ", 0, 16))
-    mul2(a("NJ"), a("JJ", 0, 24), -1.0)
+    mul2(a("NBO"), a("BO"), -1.0)
+    mul2(a("N16"), a("IB"), -16.0)
+    ts(a("PU"), a("IB"), s8(1), ALU.mult, -1.0, ALU.mult)
+    tt(a("PU"), a("PU"), a("NU"), ALU.subtract)
     cp(a("OZ", 0, 16), a("LN", 0, 16))
     cp2(a("ZT"), ind(a("Z"), a("OZ", 0, 16)))
     for k in range(16):
@@ -372,14 +461,14 @@ def rank_program(g, core, T, topo):
     act(a("RST"), a("C5"), AF.Relu, bias=cc(16), scale=-float(2 ** 40))
     cp2(a("ZS"), ind(a("Z"), a("OC", 0, 16)))
     asel(a("ZS"), [[0, 16], [1, 16]], ALU.is_ge, -PV, 0)
-    ts(a("PAYC"), a("C5"), -4096.0, ALU.mult, 15 * 4096.0, ALU.add)
+    ts(a("PAYC"), a("C5"), -8192.0, ALU.mult, 15 * 8192.0, ALU.add)
     iota(a("C1"), [[1, 16], [0, 16]])
     iota(a("C3", 0, 128), [[0, 64], [-2, 2]], 1)
     cp(a("S8", 6, 8), a("SI", 0, 2))
     ts(cc(8), s8(6), 2048.0, ALU.is_ge, -4096.0, ALU.mult)
     ts(cc(9), s8(6), cc(8), ALU.add)
     ts(a("SELW"), a("XA"), cc(1), ALU.is_equal, cc(9), ALU.mult)
-    mul2(a("IDX5"), a("C1"), 65536.0)
+    mul2(a("IDX5"), a("C1"), 131072.0)
     ts(a("C4"), a("C1"), s8(1), ALU.is_equal, s8(7), ALU.mult)
     cp2(a("BOF"), a("BO"))
     mm(a("B5", 0, 256), [(a("BOF"), a("C4"))])
@@ -394,7 +483,7 @@ def rank_program(g, core, T, topo):
     ts(cc(20), s8(1), 16.0, ALU.mult)
     ts(a("OC", 16, 32), a("XA", 0, 16), 0.0, ALU.mult, s8(1), ALU.add)
     ts(a("OC", 32, 48), a("XA", 0, 16), cc(20), ALU.add)
-    ts(a("CI"), a("JJ", 0, 16), 4096.0, ALU.add)
+    ts(a("CI"), a("JJ", 0, 16), 4096.0 + 131072.0, ALU.add)
     ts(a("LT"), a("XA", 0, 8), -1.0, ALU.mult, 1.0, ALU.add)
     cp(a("C7", 4, 6, p=P8), a("SI", 2, 4, p=P8))
     ts(a("E8F", p=P8), a("TF", 0, 128, p=P8), 15.0, ALU.add, a("CC", 2, 3, p=P8), ALU.is_equal)
@@ -417,8 +506,11 @@ def rank_program(g, core, T, topo):
 
     def hilo(c0, c1):
         cp2(a("RHI", c0, c1), a("R", c0, c1))
-        mm(a("B6", 0, c1 - c0), [(a("IF"), a("R", c0, c1)), (a("NIB"), a("RHI", c0, c1))])
-        cp2(a("RLO", c0, c1), a("B6", 0, c1 - c0))
+        if CFG["pelo"] == 1 or (CFG["pelo"] == 2 and c0 < T0):
+            mm(a("B6", 0, c1 - c0), [(a("IF"), a("R", c0, c1)), (a("NIB"), a("RHI", c0, c1))])
+            cp2(a("RLO", c0, c1), a("B6", 0, c1 - c0))
+        else:
+            tt(a("RLO", c0, c1), a("R", c0, c1), a("RHI", c0, c1), ALU.subtract)
 
     for c in range(0, T0, 256):
         hilo(c, c + 256)
@@ -512,11 +604,13 @@ def rank_program(g, core, T, topo):
         cp2(a("RHS", 4096, 4352), a("B1", 0, 256))
         tails(t, range(0, 16))
         ye = 256 * t
-        po = list(range(1, 16, 2)) + list(range(0, 16, 2))
+        po = list(range(0, 16, 2)) + list(range(1, 16, 2))
         mm(a("B7", 0, 16), [(sel("SELW", p), a("YE", ye + (p % 2) * 128 + p // 2, ye + (p % 2) * 128 + 128, 8)) for p in po])
-        Y = a("YL")
+        Y = a("YL", 0, 256)
         cp2(a("YL", 1, 256, 2), a("YE", ye + 128, ye + 256))
         cp2(a("YL", 0, 256, 2), a("YE", ye, ye + 128))
+        for k in range(1, CFG["yr"]):
+            cp2(a("YL", 256 * k, 256 * k + 256), Y)
         cp2(a(XH, 4096, 4352), Y)
         cp(a("UQ", 32, 48), a("B7", 0, 16))
         ts(a("UQ", 0, 16), a("UQ", 32, 48), 4095, ALU.bitwise_and)
@@ -529,8 +623,9 @@ def rank_program(g, core, T, topo):
         win = a(XH, 0, 4096)
 
         def v5(m0, m1):
-            for m in range(m0, m1):
-                tt(a("DX5", 256 * m, 256 * m + 256), ind(win, a("HU", 16 * m, 16 * m + 16)), Y, ALU.subtract)
+            for m in range(m0, m1, CFG["yr"]):
+                e = min(m + CFG["yr"], m1)
+                tt(a("DX5", 256 * m, 256 * e), ind(win, a("HU", 16 * m, 16 * e)), a("YL", 0, 256 * (e - m)), ALU.subtract)
             ts(a("M5", 256 * m0, 256 * m1), a("DX5", 256 * m0, 256 * m1), 0.0, ALU.min, -2.0, ALU.mult)
 
         def s5(m0, m1, b):
@@ -571,11 +666,10 @@ def rank_program(g, core, T, topo):
         scan(a("K4"), a("K5"), a("PAY"), 0.0, ALU.min, ALU.max)
         dc = Tt // 16
         ts(a("DEAD", dc, dc + 16), fk, sb, ALU.mult, cc(11), ALU.is_gt)
-        cp(a("A1", 16, 32), a("K4", 15, 256, 16))
-        ts(a("A2", 16, 32), a("A1", 16, 32), 4095, ALU.bitwise_and)
         tt(a("SM", 32, 48), a("SM", 16, 32), a("CI"), ALU.mult)
-        tt(a("SM", 48, 64), a("A2", 16, 32), a("SM", 32, 48), ALU.max)
-        cp(a("OF"), a("SM", 48, 64))
+        tt(a("A1", 16, 32), a("K4", 15, 256, 16), a("SM", 32, 48), ALU.max)
+        ts(a("A2", 16, 32), a("A1", 16, 32), 8191, ALU.bitwise_and)
+        cp(a("OF"), a("A2", 16, 32))
         tt(a("R", Tt, Tt + P), ind(a("RHS"), a("OF")), a("CN", P * t, P * t + P), ALU.max)
         store(T.yt[:, P * t:P * t + P], a("R", Tt, Tt + P))
         act(a("XI"), ind(a(XH), a("OF")))
@@ -589,11 +683,10 @@ def rank_program(g, core, T, topo):
         if not last:
             dw = a("DEAD", dc - 8, dc + 16)
             scan(a("SC", 0, 24), dw, a("NEG", 0, 24), 0.0, ALU.add, ALU.add)
-            mm(a("B7", 0, 24), [(a("NU"), dw), (a("BO"), a("SC", 0, 24))])
+            tt(a("SC", 32, 56), dw, a("XA", 0, 24), ALU.mult)
             mm(a("B7", 24, 25), [(a("BO"), a("SC", 23, 24))])
-            tt(a("E", 0, 24), dw, a("NJ"), ALU.mult)
-            tt(a("E2", 0, 24), a("E", 0, 24), a("B7", 0, 24), ALU.subtract)
-            ts(a("DST", 0, 24), a("E2", 0, 24), a("B7", 24, 25), ALU.add, cc(5), ALU.add)
+            mm(a("B7", 0, 24), [(a("PU"), dw), (a("NBO"), a("SC", 0, 24)), (a("N16"), a("SC", 32, 56))])
+            ts(a("DST", 0, 24), a("B7", 0, 24), a("B7", 24, 25), ALU.add, cc(5), ALU.add)
             ts(a("GO"), a("LN"), a("B7", 24, 25), ALU.add, 384.0, ALU.add)
             cp(ind(a("D", 0, 384), a("DST", 0, 24)), a("R", Tt - 128, Tt + P))
 

@@ -3,9 +3,10 @@ from concourse.mybir import AluOpType as ALU, AxisListType, ActivationFunctionTy
 NB, T0, P, RO = 4096, 1536, 256, 4
 BIG = float(2 ** 21)
 TAU = [(T0 + P * t) // 256 for t in range(RO)]
-DG0 = [sum(TAU[1:t]) for t in range(RO + 1)]
-CFG = dict(pv=8, mv=8, cy=0.83, g=1.56, sc=3.8, pe=0.42, sem=100.0, fix=40.0, dma=2000.0, bw=200.0, rem=2500.0,
-           views=[(1, 0, 1, 0, 200.0, 1, 1), (1.4, 0, 1.4, 0, 180.0, 1.2, 1.3),
+DG0 = [sum(TAU[:t]) for t in range(RO + 1)]
+XW = [NB + 2 * P * t for t in range(RO)]
+CFG = dict(pv=8, vc=[4, 4], sc5=[4, 4], po=1, xv=[0, 1, 2, 3], sn=48, gm=300.0, cy=0.83, g=1.56, sc=3.8, pe=0.42, sem=100.0, fix=40.0, dma=2000.0, bw=200.0, rem=2500.0,
+           views=[(1, 0, 1, 0, 200.0, 1, 1), (1.4, 0, 1.7, 0, 180.0, 1.2, 1.3),
                   (1.25, 0, 1.25, 0, 220.0, 0.8, 0.7), (1.2, 0, 1.2, 0, 160.0, 1.15, 0.9)],
            starts=24, iters=5, tries=25000, temp=600.0, pelo=1, yr=2, margin=300.0, seed=0, noise=100.0, ck=32, pool=1, sabs=1, rf=0, e0=6000, e1=0)
 PLAN = {}
@@ -13,29 +14,35 @@ PLAN = {}
 F32, BF, I32, U16, F16 = "float32", "bfloat16", "int32", "uint16", "float16"
 SCRATCH = {}
 for _n, _c, _d in [
-        ("RI", 1536, I32), ("LI", 1536, I32), ("SI", 8, I32), ("LB", 1536, BF), ("X", 5120, BF), ("R", 2560, F32),
-        ("RHI", 2304, BF), ("RLO", 2304, BF), ("XH0", 4352, BF), ("XH1", 4352, BF), ("RHS", 4352, F32),
-        ("D", 1920, F32), ("Z", 256, BF), ("ZR", 4096, BF), ("ZS", 256, BF), ("DX", 4096, BF), ("M", 4096, BF),
-        ("DX5", 4096, BF), ("M5", 4096, BF), ("YL", 1024, BF),
-        ("PI", 8, I32), ("CC", 24, F32), ("S8", 8, F32), ("ZT", 256, BF), ("IF", 128, F32), ("TF", 256, F32),
+        ("RI", 1536, I32), ("LI", 1536, I32), ("SI", 8, I32), ("LB", 1536, BF), ("X", 5632, BF), ("R", 2560, F32),
+        ("RH", 2304, F16), ("XN", 1024, BF), ("YT", 1024, F32), ("XH0", 4352, BF), ("XH1", 4352, BF), ("RHS", 4352, F32),
+        ("D", 1920, F32), ("Z", 256, BF), ("ZR", 4096, BF), ("DX", 4096, BF), ("M", 4096, BF),
+        ("XS", 4096, BF), ("YL", 1024, BF), ("SELH", 144, BF), ("SELN", 144, BF), ("T3", 384, BF), ("MK3", 384, BF),
+        ("IDXB", 288, BF), ("RS18", 288, F32), ("S1", 288, F32), ("KP", 288, F32), ("H3P", 290, F16),
+        ("OP", 32, U16), ("FA", 8, F32), ("FX", 32, BF), ("SUF", 32, BF), ("FI", 32, F16), ("NI", 32, F32), ("II", 32, F16),
+        ("DO", 32, BF), ("SUO", 32, BF), ("DI", 32, F16), ("ZE", 32, BF), ("SGF", 128, F32),
+        ("PI", 8, I32), ("CC", 24, F32), ("S8", 8, F32), ("ZT", 256, BF), ("TF", 256, F32),
         ("XA", 144, F32), ("SEL", 144, BF), ("SELW", 144, F16), ("E8", 144, BF), ("E8F", 128, F32),
-        ("IB", 128, BF), ("NIB", 128, BF), ("BO", 128, BF), ("BOF", 128, F32), ("NU", 128, BF), ("SGN", 128, BF),
-        ("SH", 2048, BF), ("SHF", 128, F32), ("DGF", 768, F32), ("DG", 24 * 128, BF), ("MK", 40, F32),
-        ("JJ", 96, F32), ("KJ", 96, F32), ("CI", 16, F32), ("LN", 32, F32), ("NBO", 128, BF), ("N16", 128, BF), ("PU", 128, BF), ("NEG", 96, BF), ("RST", 256, F32),
-        ("IDX2", 128, BF), ("IDX5", 256, BF), ("PAYC", 256, F32), ("CN", 1024, F32), ("KAP", 256, F32), ("LT", 8, F32),
-        ("C1", 256, F32), ("C2", 256, F32), ("C3", 256, F32), ("C4", 256, F32), ("C5", 256, F32), ("C6", 256, BF), ("C7", 32, F32),
-        ("OZ", 256, U16), ("OC", 64, U16), ("DEAD", 160, BF), ("SC", 96, BF), ("E", 96, F32), ("E2", 96, F32),
+        ("IB", 128, BF), ("NIB", 128, BF), ("BO", 128, BF), ("BOF", 128, F32), ("NU", 128, BF),
+        ("SH", 2048, BF), ("DG", 30 * 128, BF),
+        ("JJ", 96, F32), ("KJ", 96, F32), ("LN", 32, F32), ("NEG", 96, BF), ("RST", 128, F32),
+        ("IDX2", 128, BF), ("CN", 1024, F32), ("KAP", 256, F32), ("LT", 8, F32),
+        ("C1", 256, F32), ("C3", 128, F32), ("C4", 256, F32), ("C7", 32, F32),
+        ("OZ", 16, U16), ("OC", 16, U16), ("DEAD", 160, BF), ("SC", 96, BF), ("E", 96, F32), ("E2", 96, F32),
         ("DST", 96, U16), ("GO", 32, U16), ("OT", 256, U16), ("RR", 256, F32), ("O0", 256, U16), ("O1", 256, U16),
-        ("K0", 256, F32), ("K1", 256, F32), ("K2", 256, F32), ("K3", 256, F32), ("K4", 256, F32), ("K5", 256, F32), ("PAY", 256, F32),
-        ("A1", 32, I32), ("A2", 32, I32), ("A3", 8, I32), ("AU", 32, U16), ("TY", 256, BF), ("NY", 256, BF),
-        ("YS", 512, BF), ("YE", 1024, BF), ("UQ", 64, I32), ("H1", 256, F32), ("H2", 256, I32), ("H3", 256, I32),
-        ("HU", 256, U16), ("FK", 64, BF), ("SM", 64, F32), ("SN", 96, F32), ("OF", 16, U16), ("XI", 256, BF), ("XJ", 256, BF),
-        ("DU", 64, U16), ("YA", 1024, F32)]:
+        ("K0", 256, F32), ("K3", 288, F32), ("K4", 288, F32),
+        ("A1", 32, I32), ("A2", 32, I32), ("AU", 32, U16),
+        ("YS", 512, BF), ("YE", 1024, BF), ("UQ", 64, I32), ("H1", 256, F32), ("H2", 256, I32), ("H3", 288, I32),
+        ("HU", 256, U16), ("SM", 64, F32), ("SN", 96, F32), ("OF", 16, U16), ("XI", 256, BF), ("XJ", 256, BF),
+        ("CV", 1024, F32), ("LV", 64, F32), ("LVT", 64, F32), ("C4K", 16, BF), ("HIB", 128, BF), ("THL", 16, BF)]:
     SCRATCH[_n] = ("sbuf", [128, _c], _d)
 for _b in range(8):
     SCRATCH["B%d" % _b] = ("psum", [128, 512], F32)
+SCRATCH["B0"] = ("psum", [128, 16, 32], F32)
+SCRATCH["DX5"] = ("sbuf", [128, 256, 16], BF)
+SCRATCH["M5"] = ("sbuf", [128, 256, 16], BF)
 LOADS = ["ld%d" % i for i in range(10)]
-SEMAPHORES = ["cv", "cs", "ct", "cg", "out"] + LOADS + ["arr%d" % t for t in range(RO)] + ["snt%d" % t for t in range(RO)]
+SEMAPHORES = ["cv", "cs", "ct", "cg", "out", "cn"] + LOADS + ["nf%d" % t for t in range(RO)] + ["arr%d" % t for t in range(RO)] + ["snt%d" % t for t in range(RO)]
 WIDE = {F32: 4, BF: 2, I32: 4, U16: 2, F16: 2}
 
 
@@ -55,7 +62,7 @@ def lay_out(ops):
     for i in range(n - 1, -1, -1):
         o = ops[i]
         prio[i] = min(o["cost"].values()) + o["lat"] + max([prio[j] + (0 if ops[j]["deps"][i] == "o" else sem) for j in succ[i]] or [0])
-    cur = [None, 0.0, 0.0]
+    cur = [None, 0.0, 0.0, 0.0]
     fwd = [o["deps"] for o in ops]
     bwd = [{j: ops[j]["deps"][i] for j in succ[i]} for i in range(n)]
 
@@ -83,7 +90,7 @@ def lay_out(ops):
                 while lo < len(b) and b[lo][0] < r + c:
                     r = max(r, b[lo][1])
                     lo += 1
-                key = r + c + (cur[2] if q == "v" else 0)
+                key = r + c + (cur[2] if q == "v" else -cur[3] if q == "g" else 0)
                 if best is None or key < best[0]:
                     best = (key, q, r, c, lo)
             _, q, r, c, lo = best
@@ -148,6 +155,7 @@ def lay_out(ops):
     for rs in range(CFG["starts"]):
         h = CFG["views"][rs % len(views)]
         cur[0], cur[1], cur[2] = views[rs % len(views)][0], h[4], CFG["margin"] * 2 * draw()
+        cur[3] = CFG["gm"] * 2 * draw()
         key, nz = [-x for x in prio], CFG["noise"] * 2 * draw()
         for it in range(CFG["iters"]):
             for i in range(n - 1, -1, -1):
@@ -210,7 +218,7 @@ def rank_program(g, core, T, topo):
     if rank is None:
         return
     N = len(T.cores)
-    PV, MV, CK, CY = CFG["pv"], CFG["mv"], CFG["ck"], CFG["cy"]
+    PV, CK, CY = CFG["pv"], CFG["ck"], CFG["cy"]
     Q = {"v": g.vector, "s": g.scalar, "t": g.tensor, "g": g, "y": g.sync}
     ops, hist = [], {}
 
@@ -226,6 +234,15 @@ def rank_program(g, core, T, topo):
         ps = slice(None) if p is None else p
         ap = T[n][ps, c0:c1] if st == 1 else T[n][ps, c0:c1:st]
         return {"ap": ap, "acc": [(n, m)], "n": len(range(c0, c1, st)), "w": WIDE[dty], "ps": where == "psum", "fl": dty in (F32, BF)}
+
+    def a3(n, r, c):
+        where, shape, dty = SCRATCH[n]
+        rs = range(*r)
+        cs = range(*c) if isinstance(c, tuple) else [c]
+        row = sum(1 << x for x in cs)
+        m = sum(row << (shape[2] * x) for x in rs)
+        ap = T[n][:, slice(*r), slice(*c) if isinstance(c, tuple) else c]
+        return {"ap": ap, "acc": [(n, m)], "n": len(rs) * len(cs), "w": WIDE[dty], "ps": where == "psum", "fl": True}
 
     def ind(win, off):
         return {"ap": win["ap"].indirect(off["ap"]), "acc": win["acc"], "off": off["acc"], "n": 16 * off["n"], "w": win["w"], "ps": False}
@@ -245,7 +262,7 @@ def rank_program(g, core, T, topo):
             if SCRATCH[n][0] == "psum":
                 for (m2, w2, d) in h:
                     if d != me:
-                        k = "o" if grp is not None and ops[d]["grp"] == grp else ("w" if w or w2 else "rr")
+                        k = "o" if grp is not None and ops[d]["grp"] is not None else ("w" if w or w2 else "rr")
                         deps[d] = "w" if deps.get(d) == "w" else k
                 continue
             for (m2, w2, d) in h:
@@ -259,7 +276,7 @@ def rank_program(g, core, T, topo):
                 if w:
                     h[:] = [e for e in h if e[0] & ~m]
                 h.append((m, w, me))
-        ops.append({"fn": {q: f for q, (f, c) in fns.items()}, "cost": {q: c for q, (f, c) in fns.items()}, "deps": deps,
+        ops.append({"nm": outs[0]["acc"][0][0] if outs else "-", "fn": {q: f for q, (f, c) in fns.items()}, "cost": {q: c for q, (f, c) in fns.items()}, "deps": deps,
                     "lat": lat, "sem": sem, "inc": inc, "grp": grp,
                     "ix": 2 if any("off" in o for o in outs) else int(any(isinstance(i, dict) and "off" in i for i in ins))})
         return me
@@ -324,13 +341,20 @@ def rank_program(g, core, T, topo):
         issue(fns, [o], [i, s1, s2])
 
     def scan(o, d0, d1, init, op0, op1):
-        issue({"v": (lambda: g.vector.tensor_tensor_scan(o["ap"], d0["ap"], d1["ap"], init, op0, op1), cost(o, [d0, d1]))}, [o], [d0, d1])
+        issue({"v": (lambda: g.vector.tensor_tensor_scan(o["ap"], d0["ap"], d1["ap"], sv(init), op0, op1), cost(o, [d0, d1]))}, [o], [d0, d1, init])
 
     def ms(o, c):
-        issue({"v": (lambda: g.vector.memset(o["ap"], c), cost(o, []))}, [o], [])
+        fns = {"v": (lambda: g.vector.memset(o["ap"], c), cost(o, []))}
+        if o["fl"] and c == int(c) and abs(c) < 256:
+            fns["g"] = (lambda: g.iota(o["ap"], [[0, o["n"]]], int(c), 0, allow_small_or_imprecise_dtypes=True), 130 + 2 * o["n"] * CY)
+        issue(fns, [o], [])
 
     def act(o, i, f=AF.Copy, bias=None, scale=None):
         issue({"s": f_act(o, i, f, bias, scale)}, [o], [i, bias, scale])
+
+    def act_sum(o, i, f, col, bias, scale):
+        fn = lambda: g.scalar.activation(o["ap"], i["ap"], f, bias=sv(bias), scale=sv(scale), accum_out=col["ap"])
+        issue({"s": (fn, cost(o, [i], 1) + 20)}, [o, col], [i, bias, scale])
 
     gid = [0]
 
@@ -361,6 +385,9 @@ def rank_program(g, core, T, topo):
         nld[0] += 1
         nld[1] = issue({q: (lambda: Q[q].dma_start(o["ap"], src), 100.0)}, [o], [], lat=CFG["dma"] + nbytes / CFG["bw"], sem=s, inc=16, after=nld[1])
 
+    def shift(o, i, sem):
+        issue({"y": (lambda: g.sync.dma_start(o["ap"], i["ap"]), 100.0)}, [o], [i], lat=CFG["dma"] + 700, sem=sem, inc=16)
+
     def store(dst, i):
         issue({"y": (lambda: g.sync.dma_start(dst, i["ap"]), 100.0)}, [], [i], lat=CFG["dma"] + 500, sem="out", inc=16)
 
@@ -384,7 +411,6 @@ def rank_program(g, core, T, topo):
     iota(a("JJ"), [[16, 96]])
     iota(a("TF", 0, 128), [[16, 8], [0, 16]])
     iota(a("TF", 128, 144), [[1, 2], [4, 8]])
-    iota(a("TF", 144, 160), [[1, 2], [32, 8]])
     ts(a("PI", 1, 2), a("PI", 0, 1), 15, ALU.bitwise_and)
     ts(a("PI", 2, 3), a("PI", 0, 1), 7, ALU.bitwise_and)
     ts(a("PI", 3, 4), a("PI", 0, 1), 3, ALU.logical_shift_right, 1, ALU.bitwise_and)
@@ -408,10 +434,6 @@ def rank_program(g, core, T, topo):
     ts(cc(15), s8(3), 2.0, ALU.mult, cc(7), ALU.add)
     ts(a("LN", 0, 16), a("TF", 128, 144), cc(15), ALU.add)
     cp2(a("LN", 16, 32), a("JJ", 0, 16))
-    mul2(a("NBO"), a("BO"), -1.0)
-    mul2(a("N16"), a("IB"), -16.0)
-    ts(a("PU"), a("IB"), s8(1), ALU.mult, -1.0, ALU.mult)
-    tt(a("PU"), a("PU"), a("NU"), ALU.subtract)
     cp(a("OZ", 0, 16), a("LN", 0, 16))
     cp2(a("ZT"), ind(a("Z"), a("OZ", 0, 16)))
     for k in range(16):
@@ -422,20 +444,24 @@ def rank_program(g, core, T, topo):
     tt(a("E"), a("DEAD", 0, 96), a("KJ"), ALU.mult)
     mm(a("B7", 0, 96), [(a("BO"), a("SC")), (a("NU"), a("DEAD", 0, 96))])
     mm(a("B7", 96, 98), [(a("BO"), a("SC", 71, 96, 24))])
-    cp(a("R", 0, 768), a("RI", 0, 768))
-    cp(a("R", 768, T0), a("RI", 768, T0))
+    ts(a("RH", 0, 768), a("RI", 0, 768), -2048.0, ALU.add)
+    ts(a("RH", 768, T0), a("RI", 768, T0), -2048.0, ALU.add)
+    cp(a("R", T0 - 128, T0), a("RI", T0 - 128, T0))
     tt(a("E2"), a("E"), a("B7", 0, 96), ALU.subtract)
     cp(a("SM", 0, 2), a("B7", 96, 98))
     ts(a("DST"), a("E2"), cc(4), ALU.add)
-    for c in range(0, 96, 24):
-        cp(ind(a("D", 384, 1920), a("DST", c, c + 24)), a("R" if c >= CFG["rf"] else "RI", 16 * c, 16 * c + 384))
-    for d in range(TAU[0]):
-        asel(a("DGF", 128 * d, 128 * d + 128), [[0, 8], [TAU[0], 16]], ALU.is_ge, -16 * d, 0, a("IB"))
-        asel(a("DGF", 128 * d, 128 * d + 128), [[0, 8], [-TAU[0], 16]], ALU.is_ge, 16 * d + 15, 0)
-    mm(a("B6", 0, 256), [(a("DGF", 128 * d, 128 * d + 128), a("R", d, T0, TAU[0])) for d in range(TAU[0])])
+    for c in range(0, 96, CFG["sn"]):
+        cp(ind(a("D", 384, 1920), a("DST", c, c + CFG["sn"])), a("RI", 16 * c, 16 * (c + CFG["sn"])))
+    for t in range(RO):
+        for d in range(TAU[t]):
+            c = 128 * (DG0[t] + d)
+            asel(a("DG", c, c + 128), [[0, 8], [TAU[t], 16]], ALU.is_ge, -16 * d, 0, a("IB"))
+            asel(a("DG", c, c + 128), [[0, 8], [-TAU[t], 16]], ALU.is_ge, 16 * d + 15, 0)
 
     def places_x(t, c0, c1, nb):
-        cp(a("O%d" % (t % 2), c0, c1), a("B6", 0, c1 - c0))
+        tau = TAU[t]
+        mm(a("B6", 0, c1 - c0), [(a("DG", 128 * (DG0[t] + d), 128 * (DG0[t] + d) + 128), a("RH", c0 * tau + d, c1 * tau, tau)) for d in range(tau)])
+        ts(a("O%d" % (t % 2), c0, c1), a("B6", 0, c1 - c0), 2048.0, ALU.add)
         ops[-1]["early"] = CFG["e0"] if t == 0 else CFG["e1"]
         for c in range(c0, c1, CK):
             e = min(c + CK, c1)
@@ -451,98 +477,91 @@ def rank_program(g, core, T, topo):
     ts(a("SEL"), a("XA"), cc(1), ALU.is_equal, BIG, ALU.mult)
     ts(a("NIB"), a("IB"), -1.0, ALU.mult)
     ts(a("IDX2"), a("XA", 0, 128), 8192.0, ALU.mult)
-    ms(cc(21), 127.75)
+    ms(cc(20), -0.5)
+    ms(cc(21), 128.0)
     ms(cc(22), -128.0)
-    ms(cc(16), float(2 ** 40))
     ts(cc(6), s8(1), 128.0, ALU.mult)
-    ts(cc(12), s8(1), 2.0, ALU.mult)
-    ts(a("OC", 0, 16), a("TF", 144, 160), cc(12), ALU.add)
-    iota(a("C5"), [[0, 16], [1, 16]])
-    act(a("RST"), a("C5"), AF.Relu, bias=cc(16), scale=-float(2 ** 40))
-    cp2(a("ZS"), ind(a("Z"), a("OC", 0, 16)))
-    asel(a("ZS"), [[0, 16], [1, 16]], ALU.is_ge, -PV, 0)
-    ts(a("PAYC"), a("C5"), -8192.0, ALU.mult, 15 * 8192.0, ALU.add)
+    mul2(a("SELH"), a("SEL"), 0.5)
+    mul2(a("SELN"), a("SEL"), -0.5)
+    ms(a("RST"), 0.0)
+    ms(a("RST", 0, 128, 16), float(2 ** 40))
+    ms(a("RS18"), 0.0)
+    ms(a("RS18", 0, 288, 18), float(2 ** 40))
     iota(a("C1"), [[1, 16], [0, 16]])
     iota(a("C3", 0, 128), [[0, 64], [-2, 2]], 1)
     cp(a("S8", 6, 8), a("SI", 0, 2))
     ts(cc(8), s8(6), 2048.0, ALU.is_ge, -4096.0, ALU.mult)
     ts(cc(9), s8(6), cc(8), ALU.add)
     ts(a("SELW"), a("XA"), cc(1), ALU.is_equal, cc(9), ALU.mult)
-    mul2(a("IDX5"), a("C1"), 131072.0)
     ts(a("C4"), a("C1"), s8(1), ALU.is_equal, s8(7), ALU.mult)
     cp2(a("BOF"), a("BO"))
     mm(a("B5", 0, 256), [(a("BOF"), a("C4"))])
     cp2(a("KAP"), a("B5", 0, 256))
-    ts(cc(13), s8(1), 0.0, ALU.is_equal)
     for t in range(RO):
-        iota(a("CN", P * t, P * t + P), [[1, P]], NB + P * t)
-        mul2(a("CN", P * t, P * t + P), a("CN", P * t, P * t + P), cc(13))
+        iota(a("CV", P * t, P * t + P, p=P8), [[2, P]], XW[t])
+        if t:
+            iota(a("X", XW[t - 1] + 1, XW[t], 2), [[0, P]], 0)
+        iota(a("CN", P * t, P * t + P), [[0, P]], 0)
+    shift(a("CN", p=slice(0, 128, 16)), a("CV", p=P8), "cn")
+    iota(a("RHS", 4096, 4352), [[0, P]], 0)
     ts(cc(3), s8(4), -2.0, ALU.mult, 1.0, ALU.add)
-    mul2(a("SGN"), a("C3", 0, 128), cc(3))
-    ts(cc(5), s8(1), 368.0, ALU.add)
-    ts(cc(20), s8(1), 16.0, ALU.mult)
-    ts(a("OC", 16, 32), a("XA", 0, 16), 0.0, ALU.mult, s8(1), ALU.add)
-    ts(a("OC", 32, 48), a("XA", 0, 16), cc(20), ALU.add)
-    ts(a("CI"), a("JJ", 0, 16), 4096.0 + 131072.0, ALU.add)
-    ts(a("LT"), a("XA", 0, 8), -1.0, ALU.mult, 1.0, ALU.add)
+    mul2(a("SGF"), a("C3", 0, 128), cc(3))
+    ts(a("OC"), a("XA", 0, 16), 0.0, ALU.mult, s8(1), ALU.add)
+    cp(a("H3", 0, 16), a("JJ", 0, 16))
+    ms(a("H3", 272, 288), 0)
+    ms(a("H3P", 0, 2), 0.0)
+    ms(a("C4K"), 4096.0)
+    mul2(a("HIB"), a("IB"), 0.5)
+    ts(a("A1", 0, 18), a("JJ", 0, 18), -8.5, ALU.add, 1.0 / 18, ALU.mult)
+    ts(a("SN", 0, 18), a("A1", 0, 18), -287.0, ALU.mult)
+    ts(a("SN", 32, 50), a("JJ", 0, 18), 16.0, ALU.mult)
+    tt(a("SN", 64, 82), a("SN", 0, 18), a("SN", 32, 50), ALU.add)
+    cp(a("OP", 0, 18), a("SN", 64, 82))
+    cp2(a("T3", 0, 128), a("BO"))
+    asel(a("T3", 128, 256), [[-1, 128]], ALU.is_ge, 0, 1, a("BO"))
+    cp2(a("T3", 256, 384), a("IB"))
+    for n in ("FX", "DO", "ZE", "NI"):
+        ms(a(n), 0.0)
+    ts(a("NI", 1, 25), a("JJ", 0, 24), -1.0, ALU.mult, -1.0, ALU.add)
+    ts(a("II", 0, 25), a("NI", 0, 25), -1.0, ALU.mult, -1.0, ALU.add)
+    ts(a("II", 0, 1), a("NI", 0, 1), 0.0, ALU.mult)
     cp(a("C7", 4, 6, p=P8), a("SI", 2, 4, p=P8))
     ts(a("E8F", p=P8), a("TF", 0, 128, p=P8), 15.0, ALU.add, a("CC", 2, 3, p=P8), ALU.is_equal)
     mm(a("B4", 0, 2), [(a("E8F", p=P8), a("C7", 4, 6, p=P8))])
     ts(cc(10), a("B4", 0, 1), BIG, ALU.mult)
     cp(cc(11), a("B4", 1, 2))
-    for c in range(0, 16, 2):
-        sh = a("SH", 128 * c, 128 * c + 256)
-        iota(sh, [[1, 2], [0, 8], [1, 16]], c - 1)
-        ts(sh, sh, 15.0, ALU.min, s8(1), ALU.is_equal)
-        asel(sh, [[0, 2], [-16, 8], [0, 16]], ALU.is_ge, 0, 1)
-        asel(sh, [[0, 2], [16, 8], [0, 16]], ALU.is_ge, 15, -1)
-    cp2(a("SHF"), a("SH", 0, 128))
-    cp2(a("IF"), a("IB"))
-    for t in range(1, RO):
-        for d in range(TAU[t]):
-            c = 128 * (DG0[t] + d)
-            asel(a("DG", c, c + 128), [[0, 8], [TAU[t], 16]], ALU.is_ge, -16 * d, 0, a("IB"))
-            asel(a("DG", c, c + 128), [[0, 8], [-TAU[t], 16]], ALU.is_ge, 16 * d + 15, 0)
-
-    def hilo(c0, c1):
-        cp2(a("RHI", c0, c1), a("R", c0, c1))
-        if CFG["pelo"] == 1 or (CFG["pelo"] == 2 and c0 < T0):
-            mm(a("B6", 0, c1 - c0), [(a("IF"), a("R", c0, c1)), (a("NIB"), a("RHI", c0, c1))])
-            cp2(a("RLO", c0, c1), a("B6", 0, c1 - c0))
-        else:
-            tt(a("RLO", c0, c1), a("R", c0, c1), a("RHI", c0, c1), ALU.subtract)
-
-    for c in range(0, T0, 256):
-        hilo(c, c + 256)
-
-    def places_o(t, c0, c1):
-        tau = TAU[t]
-        terms = []
-        for d in range(tau):
-            for n in ("RHI", "RLO"):
-                terms.append((a("DG", 128 * (DG0[t] + d), 128 * (DG0[t] + d) + 128), a(n, c0 * tau + d, c1 * tau, tau)))
-        mm(a("B6", 0, c1 - c0), terms)
+    iota(a("IDXB"), [[0, 16], [16384, 18]])
+    add2(a("IDXB", 0, 288, 18), a("IDXB", 0, 288, 18), cc(10))
+    ts(a("THL"), a("IDXB", 0, 288, 18), -1.0, ALU.mult, cc(10), ALU.add)
+    ms(a("IDXB", 17, 288, 18), float(2 ** 34))
+    ts(cc(17), cc(14), 2.0, ALU.mult, 15.0, ALU.add)
+    ts(cc(18), cc(14), s8(0), ALU.add)
+    for c in (0, 8, 4, 12):
+        sh = a("SH", 128 * c, 128 * c + 512)
+        iota(sh, [[1, 4], [32, 8], [1, 16]], c - 1)
+        ts(sh, sh, cc(17), ALU.min, cc(18), ALU.is_equal)
+        asel(sh, [[0, 4], [-16, 8], [0, 16]], ALU.is_ge, 0, 1)
 
     def tails(t, ages):
         tau = TAU[t]
         for ag in ages:
             b = "B%d" % (4 + ag % 2)
-            d = ag * tau >> 4
-            mm(a(b, 0, 256), [(a("SH", 128 * ag, 128 * ag + 128), a(n, d, 256 * tau, tau)) for n in ("RHI", "RLO")])
-            cp2(a("RHS", ag, 4096, 16), a(b, 0, 256))
+            for x in (ag, ag + 8):
+                mm(a(b, x // 8, 512, 2), [(a("SH", 128 * x, 128 * x + 128), a("RH", x * tau >> 4, 256 * tau, tau))])
+            ts(a("RHS", ag, 4096, 8), a(b, 0, 512), 2048.0, ALU.add)
 
     old = lambda t: (((T0 + P * (t - 1)) // TAU[t]) // 2) * 2
 
     def s2(t, h, p0, p1, b):
         c0, c1 = 128 * h + 8 * p0, 128 * h + 8 * p1
-        act(a("DX", 16 * c0, 16 * c1), ind(a("X", 0, NB + P * t), a("OT", c0, c1)))
-        mm(a(b, 0, 16 * (c1 - c0)), [(a("IB"), a("ZR", 16 * c0, 16 * c1)), (a("NIB"), a("DX", 16 * c0, 16 * c1))])
-        act(a("M", 16 * c0, 16 * c1), a(b, 0, 16 * (c1 - c0)), AF.Relu)
+        act(a("M", 16 * c0, 16 * c1), ind(a("X", 0, XW[t]), a("OT", c0, c1)))
+        mm(a(b, 0, 16 * (c1 - c0)), [(a("IB"), a("ZR", 16 * c0, 16 * c1)), (a("NIB"), a("M", 16 * c0, 16 * c1))])
+        act(a("DX", 16 * c0, 16 * c1), a(b, 0, 16 * (c1 - c0)), AF.Abs)
 
     def v2(t, h, p0, p1):
         c0, c1 = 128 * h + 8 * p0, 128 * h + 8 * p1
         d, m = a("DX", 16 * c0, 16 * c1), a("M", 16 * c0, 16 * c1)
-        tt(d, ind(a("X", 0, NB + P * t), a("OT", c0, c1)), a("ZR", 16 * c0, 16 * c1), ALU.subtract)
+        tt(d, ind(a("X", 0, XW[t]), a("OT", c0, c1)), a("ZR", 16 * c0, 16 * c1), ALU.subtract)
         ts(m, d, -1.0, ALU.mult, 0.0, ALU.max)
 
     def step2(t, h):
@@ -552,21 +571,17 @@ def rank_program(g, core, T, topo):
         v2(t, h, pm, PV)
         for k, p0 in enumerate(range(sm, 16, 4)):
             s2(t, h, p0, min(p0 + 4, 16), "B%d" % (3 - k % 2))
-        order = list(range(0, pm)) + list(range(PV, sm)) + list(range(pm, PV)) + list(range(sm, 16))
-        mm(a("B%d" % h, 0, 128), [(a("IB"), a("IDX2"))] +
-           [(sel("SEL", p), a("M", 2048 * h + 128 * p, 2048 * h + 128 * p + 128)) for p in order])
+        part = lambda s_, n, p0, p1: [(sel(s_, p), a(n, 2048 * h + 128 * p, 2048 * h + 128 * p + 128)) for p in range(p0, p1)]
+        kb = a("B7" if h else "B1", 0, 128)
+        mm(kb, [(a("IB"), a("IDX2"))] + part("SELN", "M", PV, sm) + part("SEL", "M", 0, pm) + part("SELN", "M", sm, 16) +
+           part("SELH", "DX", PV, sm) + part("SEL", "M", pm, PV) + part("SELH", "DX", sm, 16))
         c = 128 * h
-        scan(a("K0", c, c + 128), a("RST", 0, 128), a("B%d" % h, 0, 128), 0.0, ALU.add, ALU.min)
+        scan(a("K0", c, c + 128), a("RST", 0, 128), kb, 0.0, ALU.add, ALU.min)
         cp(a("A1", 8 * h, 8 * h + 8), a("K0", c + 15, c + 128, 16))
         ts(a("A2", 8 * h, 8 * h + 8), a("A1", 8 * h, 8 * h + 8), 13, ALU.logical_shift_right, 127, ALU.bitwise_and)
         ts(a("AU", 8 * h, 8 * h + 8), a("A2", 8 * h, 8 * h + 8), cc(6), ALU.add)
-        tt(a("TY", c, c + 128), ind(a("DX", 2048 * h, 2048 * h + 2048), a("AU", 8 * h, 8 * h + 8)), a("ZS", c, c + 128), ALU.subtract)
-        dst = a("YS", 128 * t, 128 * t + 128) if h == 0 else a("YE", 256 * t + 128, 256 * t + 256)
-        if CFG["sabs"]:
-            act(dst, a("TY", c, c + 128), AF.Abs)
-        else:
-            ts(a("NY", c, c + 128), a("TY", c, c + 128), -1.0, ALU.mult)
-            tt(dst, a("TY", c, c + 128), a("NY", c, c + 128), ALU.max)
+        dst = a("YS", 128 * t, 128 * t + 128) if h == 0 else a("YL", 1, 256, 2)
+        act(dst, ind(a("DX", 2048 * h, 2048 * h + 2048), a("AU", 8 * h, 8 * h + 8)), AF.Abs)
 
     def move(t):
         to = T.cores[(rank + 1 + t % (N - 1)) % N]
@@ -574,7 +589,7 @@ def rank_program(g, core, T, topo):
         rid, pid, _ = topo.addr(to)
         eng = topo.engines(core, to)[::2]
         mask = sum(1 << e for e in eng)
-        src, dst = a("YS", 128 * t, 128 * t + 128), a("YE", 256 * t, 256 * t + 128)
+        src, dst = a("YS", 128 * t, 128 * t + 128), a("YE", 128 * t, 128 * t + 128)
 
         def send():
             g.remote_dma(dst["ap"], src["ap"], T.sem["arr%d" % t], T.sem["snt%d" % t], pid, rid, mask)
@@ -593,101 +608,117 @@ def rank_program(g, core, T, topo):
         move(t)
         step2(t, 1)
         if t:
-            hilo(Tt - P, Tt)
-            places_o(t, old(t), 256)
-            places_x(t, old(t), 256, NB + P * t)
+            ts(a("RH", Tt - P, Tt), a("R", Tt - P, Tt), -2048.0, ALU.add)
+            places_x(t, old(t), 256, XW[t])
         if not last:
-            places_o(t + 1, 0, old(t + 1))
-            places_x(t + 1, 0, old(t + 1), NB + P * t)
+            places_x(t + 1, 0, old(t + 1), XW[t])
         cp2(a("RR"), ind(dw0, a("GO", 16, 32)))
-        mm(a("B1", 0, 256), [(a("SHF"), a("RR"))])
-        cp2(a("RHS", 4096, 4352), a("B1", 0, 256))
-        tails(t, range(0, 16))
-        ye = 256 * t
-        po = list(range(0, 16, 2)) + list(range(1, 16, 2))
-        mm(a("B7", 0, 16), [(sel("SELW", p), a("YE", ye + (p % 2) * 128 + p // 2, ye + (p % 2) * 128 + 128, 8)) for p in po])
+        shift(a("RHS", 4096, 4352, p=slice(1, 128)), a("RR", p=slice(0, 127)), "nf%d" % t)
+        tails(t, range(0, 8))
+        ye = 128 * t
+        uo = [(sel("SELW", p), a("YL", p, 256, 16)) for p in range(1, 16, 2)]
+        ue = [(sel("SELW", p), a("YE", ye + p // 2, ye + 128, 8)) for p in range(0, 16, 2)]
+        mm(a("B7", 0, 16), uo + ue if CFG["po"] else ue + uo)
         Y = a("YL", 0, 256)
-        cp2(a("YL", 1, 256, 2), a("YE", ye + 128, ye + 256))
         cp2(a("YL", 0, 256, 2), a("YE", ye, ye + 128))
-        for k in range(1, CFG["yr"]):
-            cp2(a("YL", 256 * k, 256 * k + 256), Y)
         cp2(a(XH, 4096, 4352), Y)
         cp(a("UQ", 32, 48), a("B7", 0, 16))
         ts(a("UQ", 0, 16), a("UQ", 32, 48), 4095, ALU.bitwise_and)
         tt(a("UQ", 48, 64), a("UQ", 0, 16), a("UQ", 0, 16), ALU.mult)
-        tt(a("H1"), ind(a("UQ", 0, 16), a("OC", 16, 32)), a("KAP"), ALU.mult)
+        tt(a("H1"), ind(a("UQ", 0, 16), a("OC")), a("KAP"), ALU.mult)
         ts(a("UQ", 16, 32), a("UQ", 48, 64), 5, ALU.logical_shift_right)
-        tt(a("H2"), ind(a("UQ", 16, 32), a("OC", 16, 32)), a("H1"), ALU.add)
-        ts(a("H3"), a("H2"), 4095, ALU.bitwise_and)
-        cp(a("HU"), a("H3"))
-        win = a(XH, 0, 4096)
-
-        def v5(m0, m1):
-            for m in range(m0, m1, CFG["yr"]):
-                e = min(m + CFG["yr"], m1)
-                tt(a("DX5", 256 * m, 256 * e), ind(win, a("HU", 16 * m, 16 * e)), a("YL", 0, 256 * (e - m)), ALU.subtract)
-            ts(a("M5", 256 * m0, 256 * m1), a("DX5", 256 * m0, 256 * m1), 0.0, ALU.min, -2.0, ALU.mult)
-
-        def s5(m0, m1, b):
-            act(a("DX5", 256 * m0, 256 * m1), ind(win, a("HU", 16 * m0, 16 * m1)))
-            for m in range(m0, m1):
-                mm(a(b, 256 * (m - m0), 256 * (m - m0) + 256), [(a("NIB"), Y), (a("IB"), a("DX5", 256 * m, 256 * m + 256))])
-            act(a("M5", 256 * m0, 256 * m1), a(b, 0, 256 * (m1 - m0)), AF.Abs)
-
-        def sc5(m0, m1, both):
-            terms = [(a("IB"), a("IDX5", 16 * m0, 16 * m1))]
-            for n in (("DX5", "M5") if both else ("M5",)):
-                terms += [(sel("SEL", p), a(n, 256 * m0 + p, 256 * m1, 16)) for p in range(16)]
-            mm(a("B0", 16 * m0, 16 * m1), terms)
-
-        vm, sm = (MV + 1) // 2, (MV + 16) // 2
-        v5(0, vm)
-        sl = list(range(MV, 16, 2))
-        for k, m in enumerate(sl):
-            s5(m, min(m + 2, 16), "B%d" % (2 + k % 2))
-        v5(vm, MV)
-        sm = sl[len(sl) // 2]
-        sc5(0, vm, True)
-        sc5(MV, sm, False)
-        sc5(vm, MV, True)
-        sc5(sm, 16, False)
-        tt(a("PAY"), ind(a("H3"), a("OC", 32, 48)), a("PAYC"), ALU.add)
-        cp2(a("K2"), a("B0", 0, 256))
-        cp2(a("K3"), ind(a("K2"), a("OC", 32, 48)))
-        scan(a("B1", 0, 256), a("RST"), a("K3"), 0.0, ALU.add, ALU.min)
-        best = a("B1", 15, 256, 16)
-        fk = a("FK", 16 * t, 16 * t + 16)
-        ts(fk, best, cc(10), ALU.is_lt)
-        mm(a("B7", 0, 16 * t + 16), [(a("SGN"), a("FK", 0, 16 * t + 16))])
-        tt(a("K5"), a("K3"), a("B1", 0, 256), ALU.subtract)
-        ts(a("SM", 16, 32), best, cc(10), ALU.is_ge)
-        sb, b7 = a("SM", 6, 7), a("B7", 0, 16 * t + 16)
-        issue({"v": (lambda sb=sb, b7=b7: g.vector.tensor_reduce(sb["ap"], b7["ap"], AxisListType.X, ALU.add), cost(b7, []))}, [sb], [b7])
-        scan(a("K4"), a("K5"), a("PAY"), 0.0, ALU.min, ALU.max)
+        tt(a("H2"), ind(a("UQ", 16, 32), a("OC")), a("H1"), ALU.add)
+        ts(a("H3", 16, 272), a("H2"), 4095, ALU.bitwise_and)
+        cp(a("HU"), a("H3", 16, 272))
         dc = Tt // 16
-        ts(a("DEAD", dc, dc + 16), fk, sb, ALU.mult, cc(11), ALU.is_gt)
-        tt(a("SM", 32, 48), a("SM", 16, 32), a("CI"), ALU.mult)
-        tt(a("A1", 16, 32), a("K4", 15, 256, 16), a("SM", 32, 48), ALU.max)
-        ts(a("A2", 16, 32), a("A1", 16, 32), 8191, ALU.bitwise_and)
-        cp(a("OF"), a("A2", 16, 32))
-        tt(a("R", Tt, Tt + P), ind(a("RHS"), a("OF")), a("CN", P * t, P * t + P), ALU.max)
-        store(T.yt[:, P * t:P * t + P], a("R", Tt, Tt + P))
-        act(a("XI"), ind(a(XH), a("OF")))
-        mm(a("B1", 0, 256), [(a("IB"), Y), (a("IB"), a("XI"))])
-        act(a("XJ"), a("B1", 0, 256), AF.Identity, bias=cc(21), scale=0.5)
-        act(a("X", NB + P * t, NB + P * t + P), a("XJ"), AF.Identity, bias=cc(22))
-        store(T.yx[:, P * t:P * t + P], a("X", NB + P * t, NB + P * t + P))
-        cp(a("DU", 16 * t, 16 * t + 16), a("DEAD", dc, dc + 16))
-        cp2(a("YA", P * t, P * t + P), ind(a("LT"), a("DU", 16 * t, 16 * t + 16)))
-        store(T.ya[:, P * t:P * t + P], a("YA", P * t, P * t + P, p=slice(0, 128, 16)))
         if not last:
-            dw = a("DEAD", dc - 8, dc + 16)
-            scan(a("SC", 0, 24), dw, a("NEG", 0, 24), 0.0, ALU.add, ALU.add)
-            tt(a("SC", 32, 56), dw, a("XA", 0, 24), ALU.mult)
-            mm(a("B7", 24, 25), [(a("BO"), a("SC", 23, 24))])
-            mm(a("B7", 0, 24), [(a("PU"), dw), (a("NBO"), a("SC", 0, 24)), (a("N16"), a("SC", 32, 56))])
-            ts(a("DST", 0, 24), a("B7", 0, 24), a("B7", 24, 25), ALU.add, cc(5), ALU.add)
-            ts(a("GO"), a("LN"), a("B7", 24, 25), ALU.add, 384.0, ALU.add)
+            if t:
+                act_sum(a("DO", 1, 9), a("LV", 16 * t - 8, 16 * t), AF.Identity, a("FA", 4, 5), 1.0, -1.0)
+            else:
+                act_sum(a("DO", 1, 9), a("DEAD", 88, 96), AF.Identity, a("FA", 4, 5), 0.0, 1.0)
+            scan(a("SUO", 0, 25), a("ZE", 0, 25), a("DO", 0, 25), a("FA", 4, 5), ALU.add, ALU.subtract)
+            tt(a("DI", 0, 25), a("DO", 0, 25), a("NI", 0, 25), ALU.mult)
+            gid[0] += 1
+            gw, bw = gid[0], a("B7", 0, 25)
+            for k, (l, r) in enumerate([(a("IB"), "II"), (a("BO"), "SUO"), (a("T3", 128, 256), "DO"), (a("IB"), "DI")]):
+                mm1(bw, l, a(r, 0, 25), k == 0, False)
+        win = a(XH, 0, 4096)
+        ts(a("H3P", 2, 290), ind(a("H3"), a("OP", 0, 18)), -2048.0, ALU.add)
+        dl = a("B1", 0, 288)
+        gid[0] += 1
+        mm1(dl, a("IB"), a("H3P", 1, 289), True, False)
+        mm1(a("B1", 1, 288, 18), a("IB"), a("C4K"), False, False)
+        mm1(dl, a("NIB"), a("H3P", 2, 290), False, True)
+        sums = []
+        m0, at = 0, 0.0
+        for n in CFG["vc"]:
+            for m in range(m0, m0 + n):
+                tt(a3("DX5", (0, 256), m), ind(win, a("HU", 16 * m, 16 * m + 16)), Y, ALU.subtract)
+            ts(a3("M5", (0, 256), (m0, m0 + n)), a3("DX5", (0, 256), (m0, m0 + n)), 0.0, ALU.min, -2.0, ALU.mult)
+            sums += [(at + 390 * n, "DX5", m0, m0 + n), (at + 500 * n + 200, "M5", m0, m0 + n)]
+            m0, at = m0 + n, at + 500 * n
+        for k, m in enumerate(range(m0, 16, 2)):
+            e, b = min(m + 2, 16), "B%d" % (2 + k % 2)
+            act(a("XS", 256 * m, 256 * e), ind(win, a("HU", 16 * m, 16 * e)))
+            gid[0] += 1
+            for x in range(m, e):
+                mm1(a(b, x - m, 256 * (e - m), e - m), a("NIB"), Y, x == m, False)
+            for x in range(m, e):
+                mm1(a(b, x - m, 256 * (e - m), e - m), a("IB"), a("XS", 256 * x, 256 * x + 256), False, x == e - 1)
+            act(a3("M5", (0, 256), (m, e)), a(b, 0, 256 * (e - m)), AF.Abs)
+        at = 400.0
+        for n in CFG["sc5"]:
+            at += 620 * n
+            sums.append((at, "M5", m0, m0 + n))
+            m0 += n
+        gid[0] += 1
+        keys = a3("B0", (0, 16), (0, 18))
+        mm1(keys, a("IB"), a("IDXB"), True, False)
+        mm1(a3("B0", (0, 16), 0), a("IB"), a("THL"), False, False)
+        for k, (_, n, m0, m1) in enumerate(sorted(sums)):
+            for p in range(16):
+                mm1(a3("B0", (0, 16), (1 + m0, 1 + m1)), sel("SEL", p), a3(n, (p, 256, 16), (m0, m1)), False, k == len(sums) - 1 and p == 15)
+        cp2(a("K3"), keys)
+        scan(a("S1"), a("RS18"), a("K3"), 0.0, ALU.add, ALU.min)
+        tt(a("KP"), keys, a("S1"), ALU.is_gt)
+        scan(a("K4"), dl, a("KP"), 0.0, ALU.add, ALU.mult)
+        cp(a("OF"), a("K4", 17, 288, 18))
+        fk, sb = a("FX", 9, 25), a("B2", 0, 1)
+        act_sum(fk, a("S1", 16, 288, 18), AF.Sign, a("FA", t, t + 1), cc(10), -1.0)
+        mm(sb, [(a("SGF"), a("FA", x, x + 1)) for x in range(t + 1)])
+        if not last:
+            ts(a("MK3"), a("T3"), sb, ALU.mult, cc(11), ALU.is_gt)
+            scan(a("SUF", 0, 25), a("ZE", 0, 25), a("FX", 0, 25), a("FA", t, t + 1), ALU.add, ALU.subtract)
+            tt(a("FI", 0, 25), a("FX", 0, 25), a("NI", 0, 25), ALU.mult)
+            keep_gid, gid[0] = gid[0], gw
+            for k, r in enumerate(("SUF", "FX", "FI")):
+                mm1(bw, a("MK3", 128 * k, 128 * k + 128), a(r, 0, 25), False, k == 2)
+            gid[0] = keep_gid
+        ts(a("LV", 16 * t, 16 * t + 16), fk, sb, ALU.mult, cc(11), ALU.is_le)
+        if t % 2:
+            lv, lt = a("LV", 16 * t - 16, 16 * t + 16), a("LVT", 16 * t - 16, 16 * t + 16)
+            issue({"v": (lambda lv=lv, lt=lt: g.vector.transpose(lt["ap"], lv["ap"]), cost(lt, [lv]))}, [lt], [lv])
+            for x in range(2):
+                store(T.ya[x:8:2, P * t - P:P * t + P], a("LVT", 16 * (t - 1 + x), 16 * (t + x)))
+        tt(a("R", Tt, Tt + P), ind(a("RHS"), a("OF")), a("CN", P * t, P * t + P), ALU.max)
+        ts(a("B6", 0, P), a("R", Tt, Tt + P), 0.5, ALU.mult, 2048.0, ALU.add)
+        tt(a("YT", P * t, P * t + P), a("B6", 0, P), a("R", Tt, Tt + P), ALU.min)
+        store(T.yt[:, P * t:P * t + P], a("YT", P * t, P * t + P))
+        xo = a("XN", P * t, P * t + P)
+        xn = xo if last else a("X", XW[t], XW[t + 1], 2)
+        act(a("XI"), ind(a(XH), a("OF")), AF.Identity, bias=cc(20))
+        mm(a("B3", 0, 256), [(a("HIB"), Y), (a("HIB"), a("XI"))])
+        if t in CFG["xv"]:
+            ts(xn, a("B3", 0, 256), 1.5 * 2 ** 23, ALU.add, 1.5 * 2 ** 23, ALU.subtract)
+        else:
+            act(a("XJ"), a("B3", 0, 256), AF.Identity, bias=cc(21))
+            act(xn, a("XJ"), AF.Identity, bias=cc(22))
+        if not last:
+            cp2(xo, xn)
+        store(T.yx[:, P * t:P * t + P], xo)
+        if not last:
+            cp(a("DST", 0, 24), a("B7", 1, 25))
+            ts(a("GO"), a("LN"), a("B7", 0, 1), ALU.add)
             cp(ind(a("D", 0, 384), a("DST", 0, 24)), a("R", Tt - 128, Tt + P))
 
     if "order" not in PLAN:

@@ -5,30 +5,32 @@ BIG = float(2 ** 21)
 TAU = [(T0 + P * t) // 256 for t in range(RO)]
 DG0 = [sum(TAU[:t]) for t in range(RO + 1)]
 XW = [NB + 2 * P * t for t in range(RO)]
-CFG = dict(pv=8, vc=[4, 4], sc5=[4, 4], po=1, xv=[0, 1, 2, 3], sn=48, gm=300.0, cy=0.83, g=1.56, sc=3.8, pe=0.42, sem=100.0, fix=40.0, dma=2000.0, bw=200.0, rem=2500.0,
-           views=[(1, 0, 1, 0, 200.0, 1, 1), (1.4, 0, 1.7, 0, 180.0, 1.2, 1.3),
-                  (1.25, 0, 1.25, 0, 220.0, 0.8, 0.7), (1.2, 0, 1.2, 0, 160.0, 1.15, 0.9)],
-           starts=24, iters=5, tries=25000, temp=600.0, pelo=1, yr=2, margin=300.0, seed=0, noise=100.0, ck=32, pool=1, sabs=1, rf=0, e0=6000, e1=0)
+CFG = dict(pv=[8, 8], vv=2, ca=0, vc=[4, 4], sc5=[4, 4], sg=[2, 2, 2, 2], sb=["B2", "B3", "B2", "B3"], h4=1, h5=1, es=2, mj=8, xv=[3], jump=0.45, fit=0.3, cut=250, sn=48, gm=300.0, cy=0.83, g=1.56, sc=3.8, pe=0.42, sem=100.0, fix=40.0, dma=2000.0, bw=200.0, rem=2500.0,
+           views=[(1, 0, 1, 0, 200.0, 1, 0.8, 0.7, 0.7), (1.35, 10, 1.7, 0, 170.0, 0.95, 1.2, 0.9, 1.0),
+                  (1.15, 20, 1.3, 0, 150.0, 0.78, 0.7, 1.2, 0.7), (1.15, 0, 1.2, 0, 210.0, 1.2, 1.3, 0.9, 0.9)],
+           starts=30, iters=5, tries=130000, temp=450.0, pelo=1, yr=2, margin=300.0, seed=0, noise=100.0, ck=32, pool=1, sabs=1, rf=0, e0=6000, e1=0)
 PLAN = {}
 
 F32, BF, I32, U16, F16 = "float32", "bfloat16", "int32", "uint16", "float16"
-SCRATCH = {}
+GA = [1]
+RSA, TW = [x for x in GA if x != 1], T0 + 3 * P
+SCRATCH = {"RD": ("dram", [8, 15 + max(GA), TW], F16)}
 for _n, _c, _d in [
-        ("RI", 1536, I32), ("LI", 1536, I32), ("SI", 8, I32), ("LB", 1536, BF), ("X", 5632, BF), ("R", 2560, F32),
+        ("RI", 1536, I32), ("LI", 768, I32), ("SI", 8, I32), ("LB", 768, BF), ("X", 5632, BF), ("R", 2560, F32),
         ("RH", 2304, F16), ("XN", 1024, BF), ("YT", 1024, F32), ("XH0", 4352, BF), ("XH1", 4352, BF), ("RHS", 4352, F32),
         ("D", 1920, F32), ("Z", 256, BF), ("ZR", 4096, BF), ("DX", 4096, BF), ("M", 4096, BF),
         ("XS", 4096, BF), ("YL", 1024, BF), ("SELH", 144, BF), ("SELN", 144, BF), ("T3", 384, BF), ("MK3", 384, BF),
         ("IDXB", 288, BF), ("RS18", 288, F32), ("S1", 288, F32), ("KP", 288, F32), ("H3P", 290, F16),
         ("OP", 32, U16), ("FA", 8, F32), ("FX", 32, BF), ("SUF", 32, BF), ("FI", 32, F16), ("NI", 32, F32), ("II", 32, F16),
         ("DO", 32, BF), ("SUO", 32, BF), ("DI", 32, F16), ("ZE", 32, BF), ("SGF", 128, F32),
-        ("PI", 8, I32), ("CC", 24, F32), ("S8", 8, F32), ("ZT", 256, BF), ("TF", 256, F32),
-        ("XA", 144, F32), ("SEL", 144, BF), ("SELW", 144, F16), ("E8", 144, BF), ("E8F", 128, F32),
-        ("IB", 128, BF), ("NIB", 128, BF), ("BO", 128, BF), ("BOF", 128, F32), ("NU", 128, BF),
-        ("SH", 2048, BF), ("DG", 30 * 128, BF),
+        ("PI", 8, I32), ("CC", 24, F32), ("S8", 8, F32), ("TF", 256, F32),
+        ("XA", 144, F32), ("SEL", 144, BF), ("SELW", 144, F16), ("ONE", 144, BF), ("E80", 144, BF), ("E81", 144, BF), ("E8F", 128, F32),
+        ("NIB", 128, BF), ("BOF", 128, F32), ("NU", 128, BF),
+        ("SH", 2048, BF), ("SV", 512, BF),
         ("JJ", 96, F32), ("KJ", 96, F32), ("LN", 32, F32), ("NEG", 96, BF), ("RST", 128, F32),
-        ("IDX2", 128, BF), ("CN", 1024, F32), ("KAP", 256, F32), ("LT", 8, F32),
+        ("IDX2", 128, BF), ("CN", 256, F32), ("MX", 256, F16), ("NHB", 128, BF), ("RS", TW * max(len(RSA), 1), F16), ("KAP", 256, F32), ("LT", 8, F32),
         ("C1", 256, F32), ("C3", 128, F32), ("C4", 256, F32), ("C7", 32, F32),
-        ("OZ", 16, U16), ("OC", 16, U16), ("DEAD", 160, BF), ("SC", 96, BF), ("E", 96, F32), ("E2", 96, F32),
+        ("OZ", 16, U16), ("OC", 16, U16), ("DEAD", 160, BF), ("SC", 96, BF), ("E", 96, F16),
         ("DST", 96, U16), ("GO", 32, U16), ("OT", 256, U16), ("RR", 256, F32), ("O0", 256, U16), ("O1", 256, U16),
         ("K0", 256, F32), ("K3", 288, F32), ("K4", 288, F32),
         ("A1", 32, I32), ("A2", 32, I32), ("AU", 32, U16),
@@ -41,8 +43,11 @@ for _b in range(8):
 SCRATCH["B0"] = ("psum", [128, 16, 32], F32)
 SCRATCH["DX5"] = ("sbuf", [128, 256, 16], BF)
 SCRATCH["M5"] = ("sbuf", [128, 256, 16], BF)
+SCRATCH["DG"] = ("sbuf", [128, 8 * DG0[RO], 16], BF)
+BANKS = ["B%d" % _b for _b in range(8)]
+ALIAS = {"BO": 0, "IB": 256}
 LOADS = ["ld%d" % i for i in range(10)]
-SEMAPHORES = ["cv", "cs", "ct", "cg", "out", "cn"] + LOADS + ["nf%d" % t for t in range(RO)] + ["arr%d" % t for t in range(RO)] + ["snt%d" % t for t in range(RO)]
+SEMAPHORES = ["cv", "cs", "ct", "cg", "out", "cn", "sz", "xf", "zf1", "zf2"] + LOADS + ["cn%d" % t for t in range(RO)] + ["nf%d" % t for t in range(RO)] + ["wr%d" % t for t in range(RO)] + ["sh%d" % j for j in range(len(RSA))] + ["arr%d" % t for t in range(RO)] + ["snt%d" % t for t in range(RO)]
 WIDE = {F32: 4, BF: 2, I32: 4, U16: 2, F16: 2}
 
 
@@ -62,7 +67,7 @@ def lay_out(ops):
     for i in range(n - 1, -1, -1):
         o = ops[i]
         prio[i] = min(o["cost"].values()) + o["lat"] + max([prio[j] + (0 if ops[j]["deps"][i] == "o" else sem) for j in succ[i]] or [0])
-    cur = [None, 0.0, 0.0, 0.0]
+    cur = [None, 0.0, 0.0, 0.0, None]
     fwd = [o["deps"] for o in ops]
     bwd = [{j: ops[j]["deps"][i] for j in succ[i]} for i in range(n)]
 
@@ -74,11 +79,11 @@ def lay_out(ops):
             for q, c in cur[0][i].items():
                 r = 0.0
                 for d, k in deps[i].items():
-                    x = fin[d] - (0 if back else ops[d]["lat"]) if (k == "o" or (k == "rr" and eng[d] == q)) else fin[d] + cur[1]
+                    x = fin[d] - (0 if back else cur[4][d]) if (k == "o" or (k == "rr" and eng[d] == q)) else fin[d] + cur[1]
                     if x > r:
                         r = x
                 if back:
-                    r += o["lat"]
+                    r += cur[4][i]
                 b = busy[q]
                 lo, hi = 0, len(b)
                 while lo < hi:
@@ -96,7 +101,7 @@ def lay_out(ops):
             _, q, r, c, lo = best
             busy[q].insert(lo, (r, r + c))
             eng[i], start[i] = q, r
-            fin[i] = r + c + (0 if back else o["lat"])
+            fin[i] = r + c + (0 if back else cur[4][i])
         return start, fin, eng
 
     def topo_order(deps, nxt, key):
@@ -120,42 +125,40 @@ def lay_out(ops):
         f = {"v": (h[0], h[1]), "s": (h[0], h[1]), "g": (h[0], 0), "t": (h[2], h[3])}
         return [{q: c * f.get(q, (1, 0))[0] * (1, h[5], h[6])[o["ix"]] + f.get(q, (1, 0))[1] for q, c in o["cost"].items()} for o in ops]
 
-    hard = [[d for d, k in f.items() if k == "w"] for f in fwd]
-    soft = [[(d, k) for d, k in f.items() if k != "w"] for f in fwd]
-    lats = [o["lat"] for o in ops]
+    below, hard, soft = [0] * n, [], []
+    for i, f in enumerate(fwd):
+        w = [d for d, k in f.items() if k == "w"]
+        far = 0
+        for d in f:
+            far |= below[d]
+        hard.append(tuple(d for d in w if not far >> d & 1))
+        soft.append(tuple((d, k == "o") for d, k in f.items() if k != "w"))
+        below[i] = far | sum(1 << d for d in w)
 
-    def replay(order, cs, wake, pairs=None):
-        fin, end, eng, free = [0.0] * n, [0.0] * n, [None] * n, {q: 0.0 for q in "vstgyr"}
-        why, prev = [None] * n, {}
-        for i, q in order:
-            r, y = free[q], None
+    def replay(order, cs, wake, k0=0, fin=None, end=None, eng=None, free=None):
+        fin, end, eng = fin or [0.0] * n, end or [0.0] * n, eng or [None] * n
+        free = free or {q: 0.0 for q in "vstgyr"}
+        for i, q in order[k0:]:
+            r = free[q]
             for d in hard[i]:
                 if fin[d] > r:
-                    r, y = fin[d], d
-            for d, k in soft[i]:
-                x = end[d] if (k == "o" or eng[d] == q) else fin[d]
-                if x > r:
-                    r, y = x, d
+                    r = fin[d]
+            if soft[i]:
+                for d, k in soft[i]:
+                    x = end[d] if k or eng[d] == q else fin[d]
+                    if x > r:
+                        r = x
             eng[i] = q
-            free[q] = end[i] = r + cs[i][q]
-            fin[i] = end[i] + lats[i] + wake
-            if pairs is not None:
-                why[i] = (y, False) if y is not None else (prev.get(q), True)
-                prev[q] = i
-        if pairs is not None:
-            i = fin.index(max(fin))
-            while why[i][0] is not None:
-                if why[i][1]:
-                    pairs.append((why[i][0], i))
-                i = why[i][0]
+            free[q] = end[i] = r = r + cs[i][q]
+            fin[i] = r + wake[i]
         return max(fin)
 
-    views = [(priced(h), h[4]) for h in CFG["views"]]
+    views = [(priced(h), [o["lat"] * h[8 if "r" in o["cost"] else 7] + h[4] for o in ops]) for h in CFG["views"]]
     best = None
     for rs in range(CFG["starts"]):
         h = CFG["views"][rs % len(views)]
         cur[0], cur[1], cur[2] = views[rs % len(views)][0], h[4], CFG["margin"] * 2 * draw()
-        cur[3] = CFG["gm"] * 2 * draw()
+        cur[3], cur[4] = CFG["gm"] * 2 * draw(), [x - h[4] for x in views[rs % len(views)][1]]
         key, nz = [-x for x in prio], CFG["noise"] * 2 * draw()
         for it in range(CFG["iters"]):
             for i in range(n - 1, -1, -1):
@@ -170,46 +173,102 @@ def lay_out(ops):
                     best = (order, tm)
             _, fin, _ = place(bwd, topo_order(bwd, fwd, [-x + nz * draw() for x in fin]), True)
             key = [-x + nz * draw() for x in fin]
-    now = None
+
+    def settle(order, st, eng):
+        cs, end = views[0][0], st[0][1]
+        order = [x for _, _, x in sorted((end[x[0]] - cs[x[0]][x[1]], k, x) for k, x in enumerate(order))]
+        gaps, prev, last, pos = [], [None] * n, {}, [0] * n
+        for k, (i, q) in enumerate(order):
+            pos[i], prev[i] = k, last.get(q)
+            idle = end[i] - cs[i][q] - (end[last[q]] if q in last else 0.0)
+            if idle > 60:
+                gaps.append((k, q, idle))
+            last[q] = i
+        pairs = []
+        for (cs, w), (fin, end) in zip(views, st):
+            j = fin.index(max(fin))
+            while j is not None:
+                r, i = end[j] - cs[j][eng[j]] - 0.01, prev[j]
+                if i is not None and end[i] >= r:
+                    pairs.append((i, j))
+                else:
+                    i = next((d for d in fwd[j] if fin[d] >= r), None)
+                j = i
+        return order, st, eng, pairs, pos, gaps
+
+    wt = [best[1][0] / x for x in best[1]]
+    score = lambda tm: sum(x * w for x, w in zip(tm, wt))
+    st, eng = [([0.0] * n, [0.0] * n) for _ in views], [None] * n
+    for (cs, w), (fin, end) in zip(views, st):
+        replay(best[0], cs, w, 0, fin, end, eng)
+    now, tm0 = settle(best[0], st, eng), best[1]
     for rs in range(CFG["tries"]):
-        if now is None or rs % 8 == 0:
-            now = now or best
-            pairs = []
-            replay(now[0], *views[int(len(views) * draw())], pairs)
-            pos = {i: k for k, (i, q) in enumerate(now[0])}
-        order = list(now[0])
+        base, st, eng0, pairs, pos, gaps = now
         i, j = pairs[int(len(pairs) * draw())]
-        k, q, u = pos[i], order[pos[i]][1], draw()
-        if u < 0.3 and len(ops[i]["cost"]) > 1:
+        k, q, u, to, hops = pos[i], base[pos[i]][1], draw(), pos[j], int(5 * draw() * draw())
+        if u < CFG["jump"]:
+            lo, hi, c = max([pos[d] for d in fwd[i]] or [-1]), min([pos[d] for d in bwd[i]] or [n]), ops[i]["cost"]
+            fit = [(m, x) for m, x, idle in gaps if lo < m <= hi and x in c and idle > c[x] * CFG["fit"] and not 0 <= m - k <= 1]
+            if not fit:
+                continue
+            m, x = fit[int(len(fit) * draw())]
+            order = list(base)
+            order.insert(m, (i, x))
+            order.pop(k + (m <= k))
+            k, to = min(k, m), max(k, m)
+        elif u < CFG["jump"] + 0.15:
+            i = i if draw() < 0.6 else j
             qs = [x for x in sorted(ops[i]["cost"]) if x != q]
+            if not qs:
+                continue
+            k, order = pos[i], list(base)
             order[k] = (i, qs[int(len(qs) * draw())])
         else:
-            hops, m, to = 1 + int(4 * draw() * draw()), k + 1, None
-            while m < n and hops and order[m][0] not in bwd[i]:
-                if order[m][1] == q:
-                    hops, to = hops - 1, m
-                m += 1
-            if to is None:
-                m = pos[j] - 1
-                while m >= k and order[m][0] not in fwd[j]:
-                    m -= 1
-                if m >= k:
-                    continue
-                order.insert(k, order.pop(pos[j]))
+            late = draw() < 0.5
+            if late:
+                m, moved, other = to, {i}, j
+                while m < n - 1 and hops:
+                    m += 1
+                    if base[m][1] == q:
+                        hops, to = hops - 1, m
+                for m in range(k + 1, to + 1):
+                    if not moved.isdisjoint(fwd[base[m][0]]):
+                        moved.add(base[m][0])
             else:
-                order.insert(to, order.pop(k))
-        tm = []
-        for cs, w in views:
-            tm.append(replay(order, cs, w))
-            if tm[-1] > now[1][len(tm) - 1] + 600:
+                moved, other = {j}, i
+                while k > 0 and hops:
+                    k -= 1
+                    hops -= base[k][1] == q
+                for m in range(to - 1, k - 1, -1):
+                    if not moved.isdisjoint(bwd[base[m][0]]):
+                        moved.add(base[m][0])
+            if other in moved or len(moved) > 8:
+                continue
+            stay, go = [x for x in base[k:to + 1] if x[0] not in moved], [x for x in base[k:to + 1] if x[0] in moved]
+            order = base[:k] + (stay + go if late else go + stay) + base[to + 1:]
+        last, m = {}, k - 1
+        while m >= 0 and len(last) < 6:
+            last.setdefault(base[m][1], base[m][0])
+            m -= 1
+        tm, new, eng, room = [], [], list(eng0), CFG["temp"] * draw() * (1 - rs / CFG["tries"])
+        for v, (cs, w) in enumerate(views):
+            fin, end = list(st[v][0]), list(st[v][1])
+            free = {x: end[last[x]] if x in last else 0.0 for x in "vstgyr"}
+            if v == 0 and to + 120 < n:
+                replay(order[:to + 120], cs, w, k, fin, end, eng, free)
+                a, b = (next(x for x, y in order[to + 119::-1] if y == z) for z in "vs")
+                if min(end[a] - st[0][1][a], end[b] - st[0][1][b]) > CFG["cut"]:
+                    break
+                tm.append(replay(order, cs, w, to + 120, fin, end, eng, free))
+            else:
+                tm.append(replay(order, cs, w, k, fin, end, eng, free))
+            new.append((fin, end))
+            if tm[-1] > tm0[v] + 500:
                 break
-        if len(tm) == len(views) and sum(tm) <= sum(now[1]) + CFG["temp"] * draw() * (1 - rs / CFG["tries"]):
-            now = (order, tm)
-            pairs = []
-            replay(order, *views[int(len(views) * draw())], pairs)
-            pos = {i: k for k, (i, q) in enumerate(order)}
-            if sum(tm) < sum(best[1]):
-                best = now
+        if len(tm) == len(views) and score(tm) <= score(tm0) + room:
+            now, tm0 = settle(order, new, eng), tm
+            if score(tm) < score(best[1]):
+                best = (now[0], tm)
     return best
 
 
@@ -218,11 +277,13 @@ def rank_program(g, core, T, topo):
     if rank is None:
         return
     N = len(T.cores)
-    PV, CK, CY = CFG["pv"], CFG["ck"], CFG["cy"]
+    CK, CY = CFG["ck"], CFG["cy"]
     Q = {"v": g.vector, "s": g.scalar, "t": g.tensor, "g": g, "y": g.sync}
     ops, hist = [], {}
 
     def a(n, c0=0, c1=None, st=1, p=None):
+        if n in ALIAS:
+            n, c0, c1 = "T3", ALIAS[n], ALIAS[n] + 128
         where, shape, dty = SCRATCH[n]
         c1 = shape[1] if c1 is None else c1
         m = 0
@@ -245,22 +306,23 @@ def rank_program(g, core, T, topo):
         return {"ap": ap, "acc": [(n, m)], "n": len(rs) * len(cs), "w": WIDE[dty], "ps": where == "psum", "fl": True}
 
     def ind(win, off):
-        return {"ap": win["ap"].indirect(off["ap"]), "acc": win["acc"], "off": off["acc"], "n": 16 * off["n"], "w": win["w"], "ps": False}
+        return {"ap": win["ap"].indirect(off["ap"]), "acc": win["acc"], "off": off["acc"], "n": 16 * off["n"], "w": win["w"], "ps": False, "fl": win["fl"]}
 
-    def issue(fns, outs, ins, lat=0.0, sem=None, inc=1, grp=None, after=None):
+    def issue(fns, outs, ins, lat=0.0, sem=None, inc=1, grp=None, after=None, join=False):
         acc = []
         for o in outs:
             acc += [(n, m, True) for n, m in o["acc"]] + [(n, m, False) for n, m in o.get("off", [])]
         for i in ins:
             if isinstance(i, dict):
                 acc += [(n, m, False) for n, m in i["acc"] + i.get("off", [])]
-        deps, me = {}, len(ops)
+        deps, me = (ops[-1]["deps"], len(ops) - 1) if join else ({}, len(ops))
         if after is not None:
             deps[after] = "o"
         for n, m, w in acc:
             h = hist.setdefault(n, [])
-            if SCRATCH[n][0] == "psum":
-                for (m2, w2, d) in h:
+            if n in BANKS:
+                same = grp is not None and h and ops[h[0][2]]["grp"] == grp
+                for (m2, w2, d) in h[:1] if same else h:
                     if d != me:
                         k = "o" if grp is not None and ops[d]["grp"] is not None else ("w" if w or w2 else "rr")
                         deps[d] = "w" if deps.get(d) == "w" else k
@@ -270,13 +332,18 @@ def rank_program(g, core, T, topo):
                     deps[d] = "w"
         for n, m, w in acc:
             h = hist[n]
-            if SCRATCH[n][0] == "psum":
-                h[:] = [(m, w, me)]
+            if n in BANKS:
+                same = grp is not None and h and h[0][2] < len(ops) and ops[h[0][2]]["grp"] == grp
+                h[:] = (h if same else []) + [(m, w, me)]
             else:
                 if w:
                     h[:] = [e for e in h if e[0] & ~m]
                 h.append((m, w, me))
-        ops.append({"nm": outs[0]["acc"][0][0] if outs else "-", "fn": {q: f for q, (f, c) in fns.items()}, "cost": {q: c for q, (f, c) in fns.items()}, "deps": deps,
+        if join:
+            ops[me]["fn"]["t"].append(fns["t"][0])
+            ops[me]["cost"]["t"] += fns["t"][1]
+            return me
+        ops.append({"nm": outs[0]["acc"][0][0] if outs else "-", "fn": {q: [f] for q, (f, c) in fns.items()}, "cost": {q: c for q, (f, c) in fns.items()}, "deps": deps,
                     "lat": lat, "sem": sem, "inc": inc, "grp": grp,
                     "ix": 2 if any("off" in o for o in outs) else int(any(isinstance(i, dict) and "off" in i for i in ins))})
         return me
@@ -313,8 +380,8 @@ def rank_program(g, core, T, topo):
     def cp(o, i):
         issue({"v": f_cp(o, i)}, [o], [i])
 
-    def cp2(o, i):
-        fns = {"v": f_cp(o, i), "s": f_act(o, i)}
+    def cp2(o, i, pool=False):
+        fns = {} if pool else {"v": f_cp(o, i), "s": f_act(o, i)}
         if CFG["pool"] and "off" not in i and not i["ps"]:
             fns["g"] = (lambda: g.affine_select(o["ap"], i["ap"], [[0, o["n"]]], ALU.is_ge, 0.0, 0, 0), 170 + 2 * o["n"] * CY)
         issue(fns, [o], [i])
@@ -331,7 +398,7 @@ def rank_program(g, core, T, topo):
 
     def ts(o, i, s1, op0, s2=None, op1=None):
         fns = {"v": f_ts(o, i, s1, op0, s2, op1)}
-        if o["fl"] and i["fl"] and not any(isinstance(x, dict) and x["ps"] for x in (s1, s2)):
+        if o["fl"] and i["fl"] and "off" not in o and not any(isinstance(x, dict) and x["ps"] for x in (s1, s2)):
             if op0 == ALU.mult and op1 is None:
                 fns["s"] = f_act(o, i, AF.Copy, scale=s1)
             elif op0 == ALU.add and op1 is None:
@@ -358,14 +425,24 @@ def rank_program(g, core, T, topo):
 
     gid = [0]
 
-    def mm1(o, l, r, first, last):
-        c = max(64, r["n"]) * CFG["pe"] * (4 if l["w"] == 4 else 1)
-        issue({"t": (lambda: g.tensor.matmul(o["ap"], l["ap"], r["ap"], first, last), c)}, [o], [l, r], grp=gid[0])
+    left = {}
 
-    def mm(o, terms):
+    def mm1(o, l, r, first, join=False, grp=None):
+        grp = grp or gid[0]
+        left[grp] = left.get(grp, 0) + 1
+        c = max(64, r["n"]) * CFG["pe"] * (4 if l["w"] == 4 else 1)
+
+        def fn():
+            left[grp] -= 1
+            return g.tensor.matmul(o["ap"], l["ap"], r["ap"], first, left[grp] == 0)
+
+        issue({"t": (fn, c)}, [o], [l, r], grp=grp, join=join)
+
+    def mm(o, *steps):
         gid[0] += 1
-        for k, (l, r) in enumerate(terms):
-            mm1(o, l, r, k == 0, k == len(terms) - 1)
+        for k, terms in enumerate([x for x in steps if x]):
+            for j, (l, r) in enumerate(terms):
+                mm1(o, l, r, k + j == 0, j > 0)
 
     def iota(o, pat, base=0, cm=0):
         if SCRATCH[o["acc"][0][0]][2] == I32:
@@ -374,9 +451,9 @@ def rank_program(g, core, T, topo):
             f = lambda: g.iota(o["ap"], pat, base, cm, allow_small_or_imprecise_dtypes=True)
         issue({"g": (f, 130 + 2 * o["n"] * CY)}, [o], [])
 
-    def asel(o, pat, op, base, cm, i=None):
+    def asel(o, pat, op, base, cm, i=None, fill=0.0):
         i = i or o
-        issue({"g": (lambda: g.affine_select(o["ap"], i["ap"], pat, op, 0.0, base, cm), 170 + 2 * o["n"] * CY)}, [o], [i])
+        issue({"g": (lambda: g.affine_select(o["ap"], i["ap"], pat, op, fill, base, cm), 170 + 2 * o["n"] * CY)}, [o], [i])
 
     nld = [0, None]
 
@@ -385,22 +462,23 @@ def rank_program(g, core, T, topo):
         nld[0] += 1
         nld[1] = issue({q: (lambda: Q[q].dma_start(o["ap"], src), 100.0)}, [o], [], lat=CFG["dma"] + nbytes / CFG["bw"], sem=s, inc=16, after=nld[1])
 
-    def shift(o, i, sem):
-        issue({"y": (lambda: g.sync.dma_start(o["ap"], i["ap"]), 100.0)}, [o], [i], lat=CFG["dma"] + 700, sem=sem, inc=16)
+    def shift(o, i, sem, more=700):
+        issue({"y": (lambda: g.sync.dma_start(o["ap"], i["ap"]), 100.0)}, [o], [i], lat=CFG["dma"] + more, sem=sem, inc=16)
 
-    def store(dst, i):
-        issue({"y": (lambda: g.sync.dma_start(dst, i["ap"]), 100.0)}, [], [i], lat=CFG["dma"] + 500, sem="out", inc=16)
+    def store(dst, i, q="y"):
+        issue({q: (lambda: Q[q].dma_start(dst, i["ap"]), 100.0)}, [], [i], lat=CFG["dma"] + 500, sem="out", inc=16)
 
     cc = lambda k: a("CC", k, k + 1)
     s8 = lambda k: a("S8", k, k + 1)
     P8 = slice(0, 8)
     sel = lambda n, p, pp=None: a(n, 15 - p, 143 - p, p=pp)
 
-    load("y", a("LI", p=P8), T.live[:], 49152)
+    load("y", a("LI", p=P8), T.live[:, 0:768], 24576)
+    load("s", dict(a("LI", p=slice(8, 16)), acc=[("LI", 1 << 768)]), T.live[:, 768:T0], 49152)
     load("y", a("RI", 0, 768), T.rings[:, 0:768], 440000)
-    load("y", a("RI", 768, T0), T.rings[:, 768:T0], 830000)
+    load("s", a("RI", 768, T0), T.rings[:, 768:T0], 830000)
     load("y", a("Z"), T.z[:], 900000)
-    load("y", a("X", 0, NB), T.x0[:], 1950000)
+    load("s", a("X", 0, NB), T.x0[:], 1950000)
     load("y", a("SI", 0, 1), T.w[:], 0)
     load("y", a("SI", 1, 2), T.kap[:], 0)
     load("y", a("SI", 2, 3, p=P8), T.th[:], 0)
@@ -422,45 +500,52 @@ def rank_program(g, core, T, topo):
     ts(cc(2), s8(0), 16.0, ALU.mult, 15.0, ALU.add)
     ts(cc(14), s8(0), s8(1), ALU.subtract)
     ts(cc(4), s8(1), -16.0, ALU.add)
-    ts(a("E8", p=P8), a("XA", p=P8), a("CC", 2, 3, p=P8), ALU.is_equal)
-    cp(a("LB", p=P8), a("LI", p=P8))
-    mm(a("B7", 0, 96), [(sel("E8", p, P8), a("LB", p, T0, 16, p=P8)) for p in range(16)])
+    P16 = slice(0, 16)
+    cp(a("LB", p=P16), dict(a("LI", p=P16), acc=[("LI", (1 << 769) - 1)]))
+    ms(a("ONE"), 1.0)
+    for x in range(2):
+        asel(a("E8%d" % x, p=P16), [[1, 144]], ALU.is_equal, 128 * x - 15, -16, a("ONE", p=P16))
+        mm(a("B7", 48 * x, 48 * x + 48), [(sel("E8%d" % x, p, P16), a("LB", p, 768, 16, p=P16)) for p in range(16)])
     ts(a("BO"), a("TF", 0, 128), cc(14), ALU.is_equal)
     ts(a("JJ"), a("JJ"), s8(1), ALU.add)
     ts(a("NU"), a("BO"), -1.0, ALU.mult)
     asel(a("NU"), [[-1, 128]], ALU.is_gt, 0, 1)
     asel(a("IB"), [[-1, 128]], ALU.is_equal, 0, 1)
     ts(cc(7), s8(2), 32.0, ALU.mult)
-    ts(cc(15), s8(3), 2.0, ALU.mult, cc(7), ALU.add)
-    ts(a("LN", 0, 16), a("TF", 128, 144), cc(15), ALU.add)
+    ts(cc(19), s8(3), 2.0, ALU.mult, cc(7), ALU.add)
+    ts(a("LN", 0, 16), a("TF", 128, 144), cc(19), ALU.add)
     cp2(a("LN", 16, 32), a("JJ", 0, 16))
     cp(a("OZ", 0, 16), a("LN", 0, 16))
-    cp2(a("ZT"), ind(a("Z"), a("OZ", 0, 16)))
-    for k in range(16):
-        cp2(a("ZR", k, 4096, 16), a("ZT"))
+    cp2(a("ZR", 0, 4096, 16), ind(a("Z"), a("OZ", 0, 16)))
+    for k in range(1, 16):
+        cp2(a("ZR", k, 4096, 16), a("ZR", 0, 4096, 16))
     ts(a("KJ"), a("JJ"), -1.0, ALU.mult, float(T0), ALU.add)
     ts(a("DEAD", 0, 96), a("B7", 0, 96), -1.0, ALU.mult, 1.0, ALU.add)
     scan(a("SC"), a("DEAD", 0, 96), a("NEG"), 0.0, ALU.add, ALU.add)
     tt(a("E"), a("DEAD", 0, 96), a("KJ"), ALU.mult)
-    mm(a("B7", 0, 96), [(a("BO"), a("SC")), (a("NU"), a("DEAD", 0, 96))])
+    ts(a("NIB"), a("IB"), -1.0, ALU.mult)
+    mm(a("B7", 0, 96), [(a("NU"), a("DEAD", 0, 96))], [(a("BO"), a("SC"))], [(a("NIB"), a("E"))])
     mm(a("B7", 96, 98), [(a("BO"), a("SC", 71, 96, 24))])
     ts(a("RH", 0, 768), a("RI", 0, 768), -2048.0, ALU.add)
     ts(a("RH", 768, T0), a("RI", 768, T0), -2048.0, ALU.add)
-    cp(a("R", T0 - 128, T0), a("RI", T0 - 128, T0))
-    tt(a("E2"), a("E"), a("B7", 0, 96), ALU.subtract)
+    cp2(a("R", T0 - 128, T0), a("RH", T0 - 128, T0), True)
+    ts(a("DST"), a("B7", 0, 96), -1.0, ALU.mult, cc(4), ALU.add)
     cp(a("SM", 0, 2), a("B7", 96, 98))
-    ts(a("DST"), a("E2"), cc(4), ALU.add)
     for c in range(0, 96, CFG["sn"]):
         cp(ind(a("D", 384, 1920), a("DST", c, c + CFG["sn"])), a("RI", 16 * c, 16 * (c + CFG["sn"])))
+    dg = lambda t, d0, d1, ks=(0, 16): a3("DG", (8 * (DG0[t] + d0), 8 * (DG0[t] + d1)), ks)
+    for t in (0, RO - 1):
+        iota(dg(t, 0, TAU[t]), [[0, 128 * TAU[t]]])
+    for t in range(1, RO - 1):
+        shift(dg(t, 0, TAU[t]), dg(RO - 1, 0, TAU[t]), "zf%d" % t)
     for t in range(RO):
         for d in range(TAU[t]):
-            c = 128 * (DG0[t] + d)
-            asel(a("DG", c, c + 128), [[0, 8], [TAU[t], 16]], ALU.is_ge, -16 * d, 0, a("IB"))
-            asel(a("DG", c, c + 128), [[0, 8], [-TAU[t], 16]], ALU.is_ge, 16 * d + 15, 0)
+            ks = [k for k in range(16) if k * TAU[t] >> 4 == d]
+            asel(dg(t, d, d + 1, (ks[0], ks[-1] + 1)), [[-16, 8], [-1, len(ks)]], ALU.is_equal, -ks[0], 1, a("ONE", 0, 8 * len(ks)))
 
     def places_x(t, c0, c1, nb):
         tau = TAU[t]
-        mm(a("B6", 0, c1 - c0), [(a("DG", 128 * (DG0[t] + d), 128 * (DG0[t] + d) + 128), a("RH", c0 * tau + d, c1 * tau, tau)) for d in range(tau)])
+        mm(a("B6", 0, c1 - c0), [(dg(t, d, d + 1), a("RH", c0 * tau + d, c1 * tau, tau)) for d in range(tau)])
         ts(a("O%d" % (t % 2), c0, c1), a("B6", 0, c1 - c0), 2048.0, ALU.add)
         ops[-1]["early"] = CFG["e0"] if t == 0 else CFG["e1"]
         for c in range(c0, c1, CK):
@@ -475,7 +560,6 @@ def rank_program(g, core, T, topo):
     tt(a("SN", 64, 96), a("SN", 0, 32), a("SN", 32, 64), ALU.add)
     cp(a("GO"), a("SN", 64, 96))
     ts(a("SEL"), a("XA"), cc(1), ALU.is_equal, BIG, ALU.mult)
-    ts(a("NIB"), a("IB"), -1.0, ALU.mult)
     ts(a("IDX2"), a("XA", 0, 128), 8192.0, ALU.mult)
     ms(cc(20), -0.5)
     ms(cc(21), 128.0)
@@ -494,16 +578,15 @@ def rank_program(g, core, T, topo):
     ts(cc(9), s8(6), cc(8), ALU.add)
     ts(a("SELW"), a("XA"), cc(1), ALU.is_equal, cc(9), ALU.mult)
     ts(a("C4"), a("C1"), s8(1), ALU.is_equal, s8(7), ALU.mult)
-    cp2(a("BOF"), a("BO"))
+    cp2(a("BOF"), a("BO"), True)
     mm(a("B5", 0, 256), [(a("BOF"), a("C4"))])
     cp2(a("KAP"), a("B5", 0, 256))
-    for t in range(RO):
-        iota(a("CV", P * t, P * t + P, p=P8), [[2, P]], XW[t])
-        if t:
-            iota(a("X", XW[t - 1] + 1, XW[t], 2), [[0, P]], 0)
-        iota(a("CN", P * t, P * t + P), [[0, P]], 0)
-    shift(a("CN", p=slice(0, 128, 16)), a("CV", p=P8), "cn")
-    iota(a("RHS", 4096, 4352), [[0, P]], 0)
+    for t in range(0, RO, 2):
+        iota(a("CV", P * t, P * t + 2 * P, p=P8), [[2, 2 * P]], XW[t] - 2048)
+    iota(a("CN"), [[0, P]], -4096)
+    shift(a("X", NB, XW[RO - 1]), a("X", 0, XW[RO - 1] - NB), "xf")
+    shift(a("RHS", 4096, 4352, p=slice(0, 1)), a("CV", 0, P, p=slice(0, 1)), "cn", 0)
+    mul2(a("NHB"), a("IB"), -0.5)
     ts(cc(3), s8(4), -2.0, ALU.mult, 1.0, ALU.add)
     mul2(a("SGF"), a("C3", 0, 128), cc(3))
     ts(a("OC"), a("XA", 0, 16), 0.0, ALU.mult, s8(1), ALU.add)
@@ -511,15 +594,14 @@ def rank_program(g, core, T, topo):
     ms(a("H3", 272, 288), 0)
     ms(a("H3P", 0, 2), 0.0)
     ms(a("C4K"), 4096.0)
-    mul2(a("HIB"), a("IB"), 0.5)
+    iota(a("HIB"), [[0, 128]])
+    asel(a("HIB"), [[-1, 128]], ALU.not_equal, 0, 1, fill=0.5)
     ts(a("A1", 0, 18), a("JJ", 0, 18), -8.5, ALU.add, 1.0 / 18, ALU.mult)
     ts(a("SN", 0, 18), a("A1", 0, 18), -287.0, ALU.mult)
     ts(a("SN", 32, 50), a("JJ", 0, 18), 16.0, ALU.mult)
     tt(a("SN", 64, 82), a("SN", 0, 18), a("SN", 32, 50), ALU.add)
     cp(a("OP", 0, 18), a("SN", 64, 82))
-    cp2(a("T3", 0, 128), a("BO"))
     asel(a("T3", 128, 256), [[-1, 128]], ALU.is_ge, 0, 1, a("BO"))
-    cp2(a("T3", 256, 384), a("IB"))
     for n in ("FX", "DO", "ZE", "NI"):
         ms(a(n), 0.0)
     ts(a("NI", 1, 25), a("JJ", 0, 24), -1.0, ALU.mult, -1.0, ALU.add)
@@ -536,35 +618,74 @@ def rank_program(g, core, T, topo):
     ms(a("IDXB", 17, 288, 18), float(2 ** 34))
     ts(cc(17), cc(14), 2.0, ALU.mult, 15.0, ALU.add)
     ts(cc(18), cc(14), s8(0), ALU.add)
+    for x in range(2):
+        ts(a("C7", 8 + 4 * x, 12 + 4 * x), a("XA", 0, 16, 4), -1.0, ALU.mult, cc(17 + x), ALU.add)
+    iota(a("SV"), [[1, 4], [32, 8], [1, 16]], -1)
     for c in (0, 8, 4, 12):
         sh = a("SH", 128 * c, 128 * c + 512)
-        iota(sh, [[1, 4], [32, 8], [1, 16]], c - 1)
-        ts(sh, sh, cc(17), ALU.min, cc(18), ALU.is_equal)
+        ts(sh, a("SV"), a("C7", 8 + c // 4, 9 + c // 4), ALU.min, a("C7", 12 + c // 4, 13 + c // 4), ALU.is_equal)
         asel(sh, [[0, 4], [-16, 8], [0, 16]], ALU.is_ge, 0, 1)
 
     def tails(t, ages):
         tau = TAU[t]
         for ag in ages:
             b = "B%d" % (4 + ag % 2)
+            if ag == 1 and (t == 0 or 9 not in GA):
+                cp2(a("RHS", 1, 4096, 16), a("RH", tau >> 4, 256 * tau, tau), True)
+                mm(a(b, 0, 256), [(a("SH", 128 * 9, 128 * 10), a("RH", 9 * tau >> 4, 256 * tau, tau))])
+                cp2(a("RHS", 9, 4096, 16), a(b, 0, 256))
+                continue
             for x in (ag, ag + 8):
-                mm(a(b, x // 8, 512, 2), [(a("SH", 128 * x, 128 * x + 128), a("RH", x * tau >> 4, 256 * tau, tau))])
-            ts(a("RHS", ag, 4096, 8), a(b, 0, 512), 2048.0, ALU.add)
+                if t and x in GA:
+                    c = 0 if x == 1 else TW * RSA.index(x)
+                    i = a("RH" if x == 1 else "RS", c + (x * tau >> 4), c + 256 * tau, tau)
+                    if x == 0:
+                        i["acc"] = i["acc"] + [("RS", i["acc"][0][1] << TW * len(RSA))]
+                    cp2(a("RHS", x, 4096, 16), i, True)
+                else:
+                    mm(a(b, x // 8, 512, 2), [(a("SH", 128 * x, 128 * x + 128), a("RH", x * tau >> 4, 256 * tau, tau))])
+            if not (t and ag in GA):
+                cp2(a("RHS", ag, 4096, 8), a(b, 0, 512))
+
+    def shifted(k, c0, c1, gate=()):
+        each = 128 * (c1 - c0) * 2 / CFG["bw"]
+        rd = lambda ap, bit: {"ap": ap, "acc": [("RD", bit << 16 * k)]}
+        if not gate:
+            shift(rd(T["RD"][:, 0:16, c0:c1], 1), a("RH", c0, c1), "wr%d" % k, each)
+            for j in range(max(RSA) - 1):
+                shift(rd(T["RD"][:, 16 + j, c0:c1], 2 << j), a("RH", c0, c1, p=slice(15, 128, 16)), "wr%d" % k, each)
+            return
+        for j, x in enumerate(RSA):
+            c = TW * j
+            if x:
+                i = rd(T["RD"][:, x - 1:x + 15, c0:c1], 0xFFFF)
+                shift(a("RS", c + c0, c + c1), dict(i, acc=i["acc"] + list(gate)), "sh%d" % j, 300 + each * j)
+            else:
+                o = a("RS", c + c0, c + c1, p=slice(1, 128))
+                i = a("RH", c0, c1, p=slice(0, 127))
+                shift(o, dict(i, acc=i["acc"] + list(gate)), "sh%d" % j, 300 + each)
+                o = a("RS", c + c0, c + c1, p=slice(0, 1))
+                shift(dict(o, acc=[("RS", o["acc"][0][1] << TW * len(RSA))]), a("RH", c0, c1, p=slice(0, 1)), "sz", 0)
 
     old = lambda t: (((T0 + P * (t - 1)) // TAU[t]) // 2) * 2
 
     def s2(t, h, p0, p1, b):
         c0, c1 = 128 * h + 8 * p0, 128 * h + 8 * p1
         act(a("M", 16 * c0, 16 * c1), ind(a("X", 0, XW[t]), a("OT", c0, c1)))
-        mm(a(b, 0, 16 * (c1 - c0)), [(a("IB"), a("ZR", 16 * c0, 16 * c1)), (a("NIB"), a("M", 16 * c0, 16 * c1))])
+        mm(a(b, 0, 16 * (c1 - c0)), [(a("IB"), a("ZR", 16 * c0, 16 * c1))], [(a("NIB"), a("M", 16 * c0, 16 * c1))])
         act(a("DX", 16 * c0, 16 * c1), a(b, 0, 16 * (c1 - c0)), AF.Abs)
 
     def v2(t, h, p0, p1):
         c0, c1 = 128 * h + 8 * p0, 128 * h + 8 * p1
         d, m = a("DX", 16 * c0, 16 * c1), a("M", 16 * c0, 16 * c1)
         tt(d, ind(a("X", 0, XW[t]), a("OT", c0, c1)), a("ZR", 16 * c0, 16 * c1), ALU.subtract)
-        ts(m, d, -1.0, ALU.mult, 0.0, ALU.max)
+        fns = {"v": f_ts(m, d, -1.0, ALU.mult, 0.0, ALU.max)}
+        if CFG["ca"]:
+            fns["s"] = f_act(m, d, AF.Relu, scale=-1.0)
+        issue(fns, [m], [d])
 
     def step2(t, h):
+        PV = CFG["pv"][h]
         pm, sm = (PV + 1) // 2, min(PV + 4, 16)
         v2(t, h, 0, pm)
         s2(t, h, PV, sm, "B2")
@@ -573,8 +694,8 @@ def rank_program(g, core, T, topo):
             s2(t, h, p0, min(p0 + 4, 16), "B%d" % (3 - k % 2))
         part = lambda s_, n, p0, p1: [(sel(s_, p), a(n, 2048 * h + 128 * p, 2048 * h + 128 * p + 128)) for p in range(p0, p1)]
         kb = a("B7" if h else "B1", 0, 128)
-        mm(kb, [(a("IB"), a("IDX2"))] + part("SELN", "M", PV, sm) + part("SEL", "M", 0, pm) + part("SELN", "M", sm, 16) +
-           part("SELH", "DX", PV, sm) + part("SEL", "M", pm, PV) + part("SELH", "DX", sm, 16))
+        mm(kb, [(a("IB"), a("IDX2"))], part("SELN", "M", PV, sm), part("SEL", "M", 0, pm), part("SELN", "M", sm, 16),
+           part("SELH", "DX", PV, sm), part("SEL", "M", pm, PV), part("SELH", "DX", sm, 16))
         c = 128 * h
         scan(a("K0", c, c + 128), a("RST", 0, 128), kb, 0.0, ALU.add, ALU.min)
         cp(a("A1", 8 * h, 8 * h + 8), a("K0", c + 15, c + 128, 16))
@@ -587,15 +708,15 @@ def rank_program(g, core, T, topo):
         to = T.cores[(rank + 1 + t % (N - 1)) % N]
         fr = T.cores[(rank - 1 - t % (N - 1)) % N]
         rid, pid, _ = topo.addr(to)
-        eng = topo.engines(core, to)[::2]
+        eng = topo.engines(core, to)[::CFG["es"]]
         mask = sum(1 << e for e in eng)
         src, dst = a("YS", 128 * t, 128 * t + 128), a("YE", 128 * t, 128 * t + 128)
 
         def send():
             g.remote_dma(dst["ap"], src["ap"], T.sem["arr%d" % t], T.sem["snt%d" % t], pid, rid, mask)
 
-        me = issue({"g": (send, 300.0)}, [], [src], sem="snt%d" % t, inc=len(eng))
-        issue({"r": (lambda: None, 0.0)}, [dst], [], lat=CFG["rem"] + 300, sem="arr%d" % t, inc=len(topo.engines(fr, core)[::2]), after=me)
+        me = issue({"g": (send, 300.0)}, [{"acc": [("GATE", 1 << t)]}], [src], sem="snt%d" % t, inc=len(eng))
+        issue({"r": (lambda: None, 0.0)}, [dst], [], lat=CFG["rem"] + 300, sem="arr%d" % t, inc=len(topo.engines(fr, core)[::CFG["es"]]), after=me)
 
     for t in range(RO):
         Tt = T0 + P * t
@@ -608,28 +729,33 @@ def rank_program(g, core, T, topo):
         move(t)
         step2(t, 1)
         if t:
-            ts(a("RH", Tt - P, Tt), a("R", Tt - P, Tt), -2048.0, ALU.add)
             places_x(t, old(t), 256, XW[t])
+        elif RSA:
+            shifted(0, 0, T0)
+        if RSA:
+            shifted(t, Tt - P if t else 0, Tt, [("GATE", 1 << t)])
         if not last:
             places_x(t + 1, 0, old(t + 1), XW[t])
-        cp2(a("RR"), ind(dw0, a("GO", 16, 32)))
+        ts(a("RR"), ind(dw0, a("GO", 16, 32)), -2048.0, ALU.add)
         shift(a("RHS", 4096, 4352, p=slice(1, 128)), a("RR", p=slice(0, 127)), "nf%d" % t)
         tails(t, range(0, 8))
         ye = 128 * t
         uo = [(sel("SELW", p), a("YL", p, 256, 16)) for p in range(1, 16, 2)]
         ue = [(sel("SELW", p), a("YE", ye + p // 2, ye + 128, 8)) for p in range(0, 16, 2)]
-        mm(a("B7", 0, 16), uo + ue if CFG["po"] else ue + uo)
+        mm(a("B7", 0, 16), [(a("IB"), a("ZE", 0, 16))], uo, ue)
         Y = a("YL", 0, 256)
         cp2(a("YL", 0, 256, 2), a("YE", ye, ye + 128))
-        cp2(a(XH, 4096, 4352), Y)
+        cp2(a(XH, 4096, 4352), Y, True)
         cp(a("UQ", 32, 48), a("B7", 0, 16))
         ts(a("UQ", 0, 16), a("UQ", 32, 48), 4095, ALU.bitwise_and)
         tt(a("UQ", 48, 64), a("UQ", 0, 16), a("UQ", 0, 16), ALU.mult)
         tt(a("H1"), ind(a("UQ", 0, 16), a("OC")), a("KAP"), ALU.mult)
         ts(a("UQ", 16, 32), a("UQ", 48, 64), 5, ALU.logical_shift_right)
-        tt(a("H2"), ind(a("UQ", 16, 32), a("OC")), a("H1"), ALU.add)
-        ts(a("H3", 16, 272), a("H2"), 4095, ALU.bitwise_and)
-        cp(a("HU"), a("H3", 16, 272))
+        mv = 16 - sum(CFG["sg"])
+        for m0, m1 in ((mv, 16), (0, mv)) if CFG["h4"] else ((0, 16),):
+            tt(a("H2", 16 * m0, 16 * m1), ind(a("UQ", 16, 32), a("OC", 0, m1 - m0)), a("H1", 16 * m0, 16 * m1), ALU.add)
+            ts(a("H3", 16 + 16 * m0, 16 + 16 * m1), a("H2", 16 * m0, 16 * m1), 4095, ALU.bitwise_and)
+            cp(a("HU", 16 * m0, 16 * m1), a("H3", 16 + 16 * m0, 16 + 16 * m1))
         dc = Tt // 16
         if not last:
             if t:
@@ -641,85 +767,96 @@ def rank_program(g, core, T, topo):
             gid[0] += 1
             gw, bw = gid[0], a("B7", 0, 25)
             for k, (l, r) in enumerate([(a("IB"), "II"), (a("BO"), "SUO"), (a("T3", 128, 256), "DO"), (a("IB"), "DI")]):
-                mm1(bw, l, a(r, 0, 25), k == 0, False)
+                mm1(bw, l, a(r, 0, 25), k == 0, k > 0)
         win = a(XH, 0, 4096)
         ts(a("H3P", 2, 290), ind(a("H3"), a("OP", 0, 18)), -2048.0, ALU.add)
         dl = a("B1", 0, 288)
         gid[0] += 1
-        mm1(dl, a("IB"), a("H3P", 1, 289), True, False)
-        mm1(a("B1", 1, 288, 18), a("IB"), a("C4K"), False, False)
+        mm1(dl, a("IB"), a("H3P", 1, 289), True)
+        mm1(a("B1", 1, 288, 18), a("IB"), a("C4K"), False, True)
         mm1(dl, a("NIB"), a("H3P", 2, 290), False, True)
-        sums = []
-        m0, at = 0, 0.0
+        sums, m0 = [], 0
         for n in CFG["vc"]:
             for m in range(m0, m0 + n):
                 tt(a3("DX5", (0, 256), m), ind(win, a("HU", 16 * m, 16 * m + 16)), Y, ALU.subtract)
-            ts(a3("M5", (0, 256), (m0, m0 + n)), a3("DX5", (0, 256), (m0, m0 + n)), 0.0, ALU.min, -2.0, ALU.mult)
-            sums += [(at + 390 * n, "DX5", m0, m0 + n), (at + 500 * n + 200, "M5", m0, m0 + n)]
-            m0, at = m0 + n, at + 500 * n
-        for k, m in enumerate(range(m0, 16, 2)):
-            e, b = min(m + 2, 16), "B%d" % (2 + k % 2)
+            ts(a3("M5", (0, 256), (m0, m0 + n)), a3("DX5", (0, 256), (m0, m0 + n)), -2.0, ALU.mult, 0.0, ALU.max)
+            sums += [("DX5", m0, m0 + n), ("M5", m0, m0 + n)]
+            m0 += n
+        for m in range(m0, mv):
+            tt(a3("DX5", (0, 256), m), ind(win, a("HU", 16 * m, 16 * m + 16)), Y, ALU.subtract)
+            act(a3("M5", (0, 256), m), a3("DX5", (0, 256), m), AF.Abs)
+        for k, n in enumerate(CFG["sg"]):
+            m = mv + sum(CFG["sg"][:k])
+            e, b = m + n, CFG["sb"][k]
             act(a("XS", 256 * m, 256 * e), ind(win, a("HU", 16 * m, 16 * e)))
             gid[0] += 1
             for x in range(m, e):
-                mm1(a(b, x - m, 256 * (e - m), e - m), a("NIB"), Y, x == m, False)
+                mm1(a(b, x - m, 256 * (e - m), e - m), a("NIB"), Y, x == m, x > m)
             for x in range(m, e):
-                mm1(a(b, x - m, 256 * (e - m), e - m), a("IB"), a("XS", 256 * x, 256 * x + 256), False, x == e - 1)
+                mm1(a(b, x - m, 256 * (e - m), e - m), a("IB"), a("XS", 256 * x, 256 * x + 256), False, x > m)
             act(a3("M5", (0, 256), (m, e)), a(b, 0, 256 * (e - m)), AF.Abs)
-        at = 400.0
         for n in CFG["sc5"]:
-            at += 620 * n
-            sums.append((at, "M5", m0, m0 + n))
+            sums.append(("M5", m0, m0 + n))
             m0 += n
         gid[0] += 1
-        keys = a3("B0", (0, 16), (0, 18))
-        mm1(keys, a("IB"), a("IDXB"), True, False)
-        mm1(a3("B0", (0, 16), 0), a("IB"), a("THL"), False, False)
-        for k, (_, n, m0, m1) in enumerate(sorted(sums)):
+        mm1(a3("B0", (0, 16), (0, 18)), a("IB"), a("IDXB"), True)
+        mm1(a3("B0", (0, 16), 0), a("IB"), a("THL"), False, True)
+        for n, m0, m1 in sums:
             for p in range(16):
-                mm1(a3("B0", (0, 16), (1 + m0, 1 + m1)), sel("SEL", p), a3(n, (p, 256, 16), (m0, m1)), False, k == len(sums) - 1 and p == 15)
-        cp2(a("K3"), keys)
-        scan(a("S1"), a("RS18"), a("K3"), 0.0, ALU.add, ALU.min)
-        tt(a("KP"), keys, a("S1"), ALU.is_gt)
-        scan(a("K4"), dl, a("KP"), 0.0, ALU.add, ALU.mult)
+                mm1(a3("B0", (0, 16), (1 + m0, 1 + m1)), sel("SEL", p), a3(n, (p, 256, 16), (m0, m1)), False, p % CFG["mj"] > 0)
+        parts = [(0, 8), (8, 16)] if CFG["h5"] else [(0, 16)]
+        for c0, c1 in parts:
+            cp2(a("K3", 18 * c0, 18 * c1), a3("B0", (c0, c1), (0, 18)))
+            scan(a("S1", 18 * c0, 18 * c1), a("RS18", 18 * c0, 18 * c1), a("K3", 18 * c0, 18 * c1), 0.0, ALU.add, ALU.min)
+        for c0, c1 in parts:
+            tt(a("KP", 18 * c0, 18 * c1), a3("B0", (c0, c1), (0, 18)), a("S1", 18 * c0, 18 * c1), ALU.is_gt)
+            scan(a("K4", 18 * c0, 18 * c1), a("B1", 18 * c0, 18 * c1), a("KP", 18 * c0, 18 * c1), 0.0, ALU.add, ALU.mult)
         cp(a("OF"), a("K4", 17, 288, 18))
         fk, sb = a("FX", 9, 25), a("B2", 0, 1)
         act_sum(fk, a("S1", 16, 288, 18), AF.Sign, a("FA", t, t + 1), cc(10), -1.0)
-        mm(sb, [(a("SGF"), a("FA", x, x + 1)) for x in range(t + 1)])
+        mm(sb, [(a("SGF"), a("FA", x, x + 1)) for x in range(t)], [(a("SGF"), a("FA", t, t + 1))])
         if not last:
             ts(a("MK3"), a("T3"), sb, ALU.mult, cc(11), ALU.is_gt)
             scan(a("SUF", 0, 25), a("ZE", 0, 25), a("FX", 0, 25), a("FA", t, t + 1), ALU.add, ALU.subtract)
             tt(a("FI", 0, 25), a("FX", 0, 25), a("NI", 0, 25), ALU.mult)
-            keep_gid, gid[0] = gid[0], gw
             for k, r in enumerate(("SUF", "FX", "FI")):
-                mm1(bw, a("MK3", 128 * k, 128 * k + 128), a(r, 0, 25), False, k == 2)
-            gid[0] = keep_gid
+                mm1(bw, a("MK3", 128 * k, 128 * k + 128), a(r, 0, 25), False, k > 0, gw)
         ts(a("LV", 16 * t, 16 * t + 16), fk, sb, ALU.mult, cc(11), ALU.is_le)
         if t % 2:
             lv, lt = a("LV", 16 * t - 16, 16 * t + 16), a("LVT", 16 * t - 16, 16 * t + 16)
             issue({"v": (lambda lv=lv, lt=lt: g.vector.transpose(lt["ap"], lv["ap"]), cost(lt, [lv]))}, [lt], [lv])
             for x in range(2):
                 store(T.ya[x:8:2, P * t - P:P * t + P], a("LVT", 16 * (t - 1 + x), 16 * (t + x)))
-        tt(a("R", Tt, Tt + P), ind(a("RHS"), a("OF")), a("CN", P * t, P * t + P), ALU.max)
-        ts(a("B6", 0, P), a("R", Tt, Tt + P), 0.5, ALU.mult, 2048.0, ALU.add)
-        tt(a("YT", P * t, P * t + P), a("B6", 0, P), a("R", Tt, Tt + P), ALU.min)
-        store(T.yt[:, P * t:P * t + P], a("YT", P * t, P * t + P))
+        rn, yt = a("R", Tt, Tt + P), a("YT", P * t, P * t + P)
+        shift(a("CN", p=slice(0, 128, 16)), a("CV", P * t, P * t + P, p=P8), "cn%d" % t, 0)
+        tt(rn, ind(a("RHS"), a("OF")), a("CN"), ALU.max)
+        if not last:
+            cp(a("DST", 0, 24), a("B7", 1, 25))
+            ts(a("GO"), a("LN"), a("B7", 0, 1), ALU.add)
+            ts(ind(a("D", 0, 384), a("DST", 0, 24)), a("R", Tt - 128, Tt + P), 1.0, ALU.mult, 2048.0, ALU.add)
+            cp2(a("RH", Tt, Tt + P), rn, True)
+            if RSA:
+                shifted(t + 1, Tt, Tt + P)
+            ts(a("MX"), a("RH", Tt, Tt + P), 2048.0, ALU.max)
+            mm(a("B6", 0, P), [(a("IB"), a("RH", Tt, Tt + P)), (a("NHB"), a("MX"))])
+            ts(yt, a("B6", 0, P), 3072.0, ALU.add)
+        else:
+            ts(a("B6", 0, P), rn, 0.5, ALU.mult, 3072.0, ALU.add)
+            ts(a("RR"), rn, 2048.0, ALU.add)
+            tt(yt, a("B6", 0, P), a("RR"), ALU.min)
+        store(T.yt[:, P * t:P * t + P], yt, "s" if last else "y")
         xo = a("XN", P * t, P * t + P)
         xn = xo if last else a("X", XW[t], XW[t + 1], 2)
         act(a("XI"), ind(a(XH), a("OF")), AF.Identity, bias=cc(20))
-        mm(a("B3", 0, 256), [(a("HIB"), Y), (a("HIB"), a("XI"))])
+        mm(a("B3", 0, 256), [(a("HIB"), Y)], [(a("HIB"), a("XI"))])
         if t in CFG["xv"]:
             ts(xn, a("B3", 0, 256), 1.5 * 2 ** 23, ALU.add, 1.5 * 2 ** 23, ALU.subtract)
         else:
             act(a("XJ"), a("B3", 0, 256), AF.Identity, bias=cc(21))
             act(xn, a("XJ"), AF.Identity, bias=cc(22))
         if not last:
-            cp2(xo, xn)
+            cp2(xo, xn, True)
         store(T.yx[:, P * t:P * t + P], xo)
-        if not last:
-            cp(a("DST", 0, 24), a("B7", 1, 25))
-            ts(a("GO"), a("LN"), a("B7", 0, 1), ALU.add)
-            cp(ind(a("D", 0, 384), a("DST", 0, 24)), a("R", Tt - 128, Tt + P))
 
     if "order" not in PLAN:
         PLAN["order"], PLAN["time"] = lay_out(ops)
@@ -736,7 +873,7 @@ def rank_program(g, core, T, topo):
         o = ops[i]
         eng[i] = q
         sem = o["sem"] or "c" + q
-        cnt[sem] = cnt.get(sem, 0) + o["inc"]
+        cnt[sem] = cnt.get(sem, 0) + o["inc"] * len(o["fn"][q])
         mark[i] = (sem, cnt[sem])
         if q == "r":
             continue
@@ -746,9 +883,10 @@ def rank_program(g, core, T, topo):
                 need[mark[d][0]] = max(need.get(mark[d][0], 0), mark[d][1])
         for s_ in sorted(need, key=lambda s_: s_ == "c" + q):
             wait(q, s_, need[s_])
-        call = o["fn"][q]()
-        if call is not None:
-            call.then_inc(T.sem[sem], o["inc"])
+        for fn in o["fn"][q]:
+            call = fn()
+            if call is not None:
+                call.then_inc(T.sem[sem], o["inc"])
         snap[mark[i]] = dict(clock[q])
     for s_ in sorted(cnt):
         if s_ != "out" and not any(clock[q].get(s_, 0) >= cnt[s_] for q in "vstg"):

from concourse.mybir import AluOpType as ALU, AxisListType, ActivationFunctionType as AF

NB, T0, P, RO = 4096, 1536, 256, 4
BIG = float(2 ** 21)
TAU = [(T0 + P * t) // 256 for t in range(RO)]
DG0 = [sum(TAU[:t]) for t in range(RO + 1)]
XW = [NB + 2 * P * t for t in range(RO)]
CFG = dict(pv=[8, 8], vv=2, ca=0, vc=[4, 4], sc5=[4, 4], sg=[2, 2, 2, 2], sb=["B2", "B3", "B2", "B3"], h4=1, h5=1, es=2, mj=8, xv=[3], jump=0.45, fit=0.3, cut=250, sn=48, gm=300.0, cy=0.83, g=1.56, sc=3.8, pe=0.42, sem=100.0, fix=40.0, dma=2000.0, bw=200.0, rem=2500.0,
           views=[(1, 0, 1, 0, 200.0, 1, 0.8, 0.7, 0.7), (1.35, 10, 1.7, 0, 170.0, 0.95, 1.2, 0.9, 1.0),
                  (1.15, 20, 1.3, 0, 150.0, 0.78, 0.7, 1.2, 0.7), (1.15, 0, 1.2, 0, 210.0, 1.2, 1.3, 0.9, 0.9)],
           starts=30, iters=5, tries=130000, temp=450.0, pelo=1, yr=2, margin=300.0, seed=0, noise=100.0, ck=32, pool=1, sabs=1, rf=0, e0=6000, e1=0)
PLAN = {}

F32, BF, I32, U16, F16 = "float32", "bfloat16", "int32", "uint16", "float16"
GA = [1]
RSA, TW = [x for x in GA if x != 1], T0 + 3 * P
SCRATCH = {"RD": ("dram", [8, 15 + max(GA), TW], F16)}
for _n, _c, _d in [
        ("RI", 1536, I32), ("LI", 768, I32), ("SI", 8, I32), ("LB", 768, BF), ("X", 5632, BF), ("R", 2560, F32),
        ("RH", 2304, F16), ("XN", 1024, BF), ("YT", 1024, F32), ("XH0", 4352, BF), ("XH1", 4352, BF), ("RHS", 4352, F32),
        ("D", 1920, F32), ("Z", 256, BF), ("ZR", 4096, BF), ("DX", 4096, BF), ("M", 4096, BF),
        ("XS", 4096, BF), ("YL", 1024, BF), ("SELH", 144, BF), ("SELN", 144, BF), ("T3", 384, BF), ("MK3", 384, BF),
        ("IDXB", 288, BF), ("RS18", 288, F32), ("S1", 288, F32), ("KP", 288, F32), ("H3P", 290, F16),
        ("OP", 32, U16), ("FA", 8, F32), ("FX", 32, BF), ("SUF", 32, BF), ("FI", 32, F16), ("NI", 32, F32), ("II", 32, F16),
        ("DO", 32, BF), ("SUO", 32, BF), ("DI", 32, F16), ("ZE", 32, BF), ("SGF", 128, F32),
        ("PI", 8, I32), ("CC", 24, F32), ("S8", 8, F32), ("TF", 256, F32),
        ("XA", 144, F32), ("SEL", 144, BF), ("SELW", 144, F16), ("ONE", 144, BF), ("E80", 144, BF), ("E81", 144, BF), ("E8F", 128, F32),
        ("NIB", 128, BF), ("BOF", 128, F32), ("NU", 128, BF),
        ("SH", 2048, BF), ("SV", 512, BF),
        ("JJ", 96, F32), ("KJ", 96, F32), ("LN", 32, F32), ("NEG", 96, BF), ("RST", 128, F32),
        ("IDX2", 128, BF), ("CN", 256, F32), ("MX", 256, F16), ("NHB", 128, BF), ("RS", TW * max(len(RSA), 1), F16), ("KAP", 256, F32), ("LT", 8, F32),
        ("C1", 256, F32), ("C3", 128, F32), ("C4", 256, F32), ("C7", 32, F32),
        ("OZ", 16, U16), ("OC", 16, U16), ("DEAD", 160, BF), ("SC", 96, BF), ("E", 96, F16),
        ("DST", 96, U16), ("GO", 32, U16), ("OT", 256, U16), ("RR", 256, F32), ("O0", 256, U16), ("O1", 256, U16),
        ("K0", 256, F32), ("K3", 288, F32), ("K4", 288, F32),
        ("A1", 32, I32), ("A2", 32, I32), ("AU", 32, U16),
        ("YS", 512, BF), ("YE", 1024, BF), ("UQ", 64, I32), ("H1", 256, F32), ("H2", 256, I32), ("H3", 288, I32),
        ("HU", 256, U16), ("SM", 64, F32), ("SN", 96, F32), ("OF", 16, U16), ("XI", 256, BF), ("XJ", 256, BF),
        ("CV", 1024, F32), ("LV", 64, F32), ("LVT", 64, F32), ("C4K", 16, BF), ("HIB", 128, BF), ("THL", 16, BF)]:
    SCRATCH[_n] = ("sbuf", [128, _c], _d)
for _b in range(8):
    SCRATCH["B%d" % _b] = ("psum", [128, 512], F32)
SCRATCH["B0"] = ("psum", [128, 16, 32], F32)
SCRATCH["DX5"] = ("sbuf", [128, 256, 16], BF)
SCRATCH["M5"] = ("sbuf", [128, 256, 16], BF)
SCRATCH["DG"] = ("sbuf", [128, 8 * DG0[RO], 16], BF)
BANKS = ["B%d" % _b for _b in range(8)]
ALIAS = {"BO": 0, "IB": 256}
LOADS = ["ld%d" % i for i in range(10)]
SEMAPHORES = ["cv", "cs", "ct", "cg", "out", "cn", "sz", "xf", "zf1", "zf2"] + LOADS + ["cn%d" % t for t in range(RO)] + ["nf%d" % t for t in range(RO)] + ["wr%d" % t for t in range(RO)] + ["sh%d" % j for j in range(len(RSA))] + ["arr%d" % t for t in range(RO)] + ["snt%d" % t for t in range(RO)]
WIDE = {F32: 4, BF: 2, I32: 4, U16: 2, F16: 2}


def lay_out(ops):
    n, sem = len(ops), CFG["sem"]
    succ = [[] for _ in ops]
    for i, o in enumerate(ops):
        for d in o["deps"]:
            succ[d].append(i)
    rnd = [CFG["seed"] * 7919 + 1]

    def draw():
        rnd[0] = (rnd[0] * 1103515245 + 12345) % 2 ** 31
        return rnd[0] / 2 ** 31

    prio = [0.0] * n
    for i in range(n - 1, -1, -1):
        o = ops[i]
        prio[i] = min(o["cost"].values()) + o["lat"] + max([prio[j] + (0 if ops[j]["deps"][i] == "o" else sem) for j in succ[i]] or [0])
    cur = [None, 0.0, 0.0, 0.0, None]
    fwd = [o["deps"] for o in ops]
    bwd = [{j: ops[j]["deps"][i] for j in succ[i]} for i in range(n)]

    def place(deps, seq, back):
        fin, eng, start = [0.0] * n, [None] * n, [0.0] * n
        busy = {q: [] for q in "vstgyr"}
        for i in seq:
            o, best = ops[i], None
            for q, c in cur[0][i].items():
                r = 0.0
                for d, k in deps[i].items():
                    x = fin[d] - (0 if back else cur[4][d]) if (k == "o" or (k == "rr" and eng[d] == q)) else fin[d] + cur[1]
                    if x > r:
                        r = x
                if back:
                    r += cur[4][i]
                b = busy[q]
                lo, hi = 0, len(b)
                while lo < hi:
                    mid = (lo + hi) // 2
                    if b[mid][1] <= r:
                        lo = mid + 1
                    else:
                        hi = mid
                while lo < len(b) and b[lo][0] < r + c:
                    r = max(r, b[lo][1])
                    lo += 1
                key = r + c + (cur[2] if q == "v" else -cur[3] if q == "g" else 0)
                if best is None or key < best[0]:
                    best = (key, q, r, c, lo)
            _, q, r, c, lo = best
            busy[q].insert(lo, (r, r + c))
            eng[i], start[i] = q, r
            fin[i] = r + c + (0 if back else cur[4][i])
        return start, fin, eng

    def topo_order(deps, nxt, key):
        left = [len(d) for d in deps]
        cand = sorted(((key[i], i) for i in range(n) if left[i] == 0), reverse=True)
        seq = []
        while cand:
            _, i = cand.pop()
            seq.append(i)
            new = False
            for j in nxt[i]:
                left[j] -= 1
                if left[j] == 0:
                    cand.append((key[j], j))
                    new = True
            if new:
                cand.sort(reverse=True)
        return seq

    def priced(h):
        f = {"v": (h[0], h[1]), "s": (h[0], h[1]), "g": (h[0], 0), "t": (h[2], h[3])}
        return [{q: c * f.get(q, (1, 0))[0] * (1, h[5], h[6])[o["ix"]] + f.get(q, (1, 0))[1] for q, c in o["cost"].items()} for o in ops]

    below, hard, soft = [0] * n, [], []
    for i, f in enumerate(fwd):
        w = [d for d, k in f.items() if k == "w"]
        far = 0
        for d in f:
            far |= below[d]
        hard.append(tuple(d for d in w if not far >> d & 1))
        soft.append(tuple((d, k == "o") for d, k in f.items() if k != "w"))
        below[i] = far | sum(1 << d for d in w)

    def replay(order, cs, wake, k0=0, fin=None, end=None, eng=None, free=None):
        fin, end, eng = fin or [0.0] * n, end or [0.0] * n, eng or [None] * n
        free = free or {q: 0.0 for q in "vstgyr"}
        for i, q in order[k0:]:
            r = free[q]
            for d in hard[i]:
                if fin[d] > r:
                    r = fin[d]
            if soft[i]:
                for d, k in soft[i]:
                    x = end[d] if k or eng[d] == q else fin[d]
                    if x > r:
                        r = x
            eng[i] = q
            free[q] = end[i] = r = r + cs[i][q]
            fin[i] = r + wake[i]
        return max(fin)

    views = [(priced(h), [o["lat"] * h[8 if "r" in o["cost"] else 7] + h[4] for o in ops]) for h in CFG["views"]]
    best = None
    for rs in range(CFG["starts"]):
        h = CFG["views"][rs % len(views)]
        cur[0], cur[1], cur[2] = views[rs % len(views)][0], h[4], CFG["margin"] * 2 * draw()
        cur[3], cur[4] = CFG["gm"] * 2 * draw(), [x - h[4] for x in views[rs % len(views)][1]]
        key, nz = [-x for x in prio], CFG["noise"] * 2 * draw()
        for it in range(CFG["iters"]):
            for i in range(n - 1, -1, -1):
                key[i] = min([key[i] - ops[i].get("early", 0)] + [key[j] - 1 for j in succ[i]])
            seq = topo_order(fwd, bwd, key)
            start, fin, eng = place(fwd, seq, False)
            if it:
                pos = {i: k for k, i in enumerate(seq)}
                order = [(i, eng[i]) for i in sorted(range(n), key=lambda i: (start[i], pos[i]))]
                tm = [replay(order, cs, w) for cs, w in views]
                if best is None or sum(tm) < sum(best[1]):
                    best = (order, tm)
            _, fin, _ = place(bwd, topo_order(bwd, fwd, [-x + nz * draw() for x in fin]), True)
            key = [-x + nz * draw() for x in fin]

    def settle(order, st, eng):
        cs, end = views[0][0], st[0][1]
        order = [x for _, _, x in sorted((end[x[0]] - cs[x[0]][x[1]], k, x) for k, x in enumerate(order))]
        gaps, prev, last, pos = [], [None] * n, {}, [0] * n
        for k, (i, q) in enumerate(order):
            pos[i], prev[i] = k, last.get(q)
            idle = end[i] - cs[i][q] - (end[last[q]] if q in last else 0.0)
            if idle > 60:
                gaps.append((k, q, idle))
            last[q] = i
        pairs = []
        for (cs, w), (fin, end) in zip(views, st):
            j = fin.index(max(fin))
            while j is not None:
                r, i = end[j] - cs[j][eng[j]] - 0.01, prev[j]
                if i is not None and end[i] >= r:
                    pairs.append((i, j))
                else:
                    i = next((d for d in fwd[j] if fin[d] >= r), None)
                j = i
        return order, st, eng, pairs, pos, gaps

    wt = [best[1][0] / x for x in best[1]]
    score = lambda tm: sum(x * w for x, w in zip(tm, wt))
    st, eng = [([0.0] * n, [0.0] * n) for _ in views], [None] * n
    for (cs, w), (fin, end) in zip(views, st):
        replay(best[0], cs, w, 0, fin, end, eng)
    now, tm0 = settle(best[0], st, eng), best[1]
    for rs in range(CFG["tries"]):
        base, st, eng0, pairs, pos, gaps = now
        i, j = pairs[int(len(pairs) * draw())]
        k, q, u, to, hops = pos[i], base[pos[i]][1], draw(), pos[j], int(5 * draw() * draw())
        if u < CFG["jump"]:
            lo, hi, c = max([pos[d] for d in fwd[i]] or [-1]), min([pos[d] for d in bwd[i]] or [n]), ops[i]["cost"]
            fit = [(m, x) for m, x, idle in gaps if lo < m <= hi and x in c and idle > c[x] * CFG["fit"] and not 0 <= m - k <= 1]
            if not fit:
                continue
            m, x = fit[int(len(fit) * draw())]
            order = list(base)
            order.insert(m, (i, x))
            order.pop(k + (m <= k))
            k, to = min(k, m), max(k, m)
        elif u < CFG["jump"] + 0.15:
            i = i if draw() < 0.6 else j
            qs = [x for x in sorted(ops[i]["cost"]) if x != q]
            if not qs:
                continue
            k, order = pos[i], list(base)
            order[k] = (i, qs[int(len(qs) * draw())])
        else:
            late = draw() < 0.5
            if late:
                m, moved, other = to, {i}, j
                while m < n - 1 and hops:
                    m += 1
                    if base[m][1] == q:
                        hops, to = hops - 1, m
                for m in range(k + 1, to + 1):
                    if not moved.isdisjoint(fwd[base[m][0]]):
                        moved.add(base[m][0])
            else:
                moved, other = {j}, i
                while k > 0 and hops:
                    k -= 1
                    hops -= base[k][1] == q
                for m in range(to - 1, k - 1, -1):
                    if not moved.isdisjoint(bwd[base[m][0]]):
                        moved.add(base[m][0])
            if other in moved or len(moved) > 8:
                continue
            stay, go = [x for x in base[k:to + 1] if x[0] not in moved], [x for x in base[k:to + 1] if x[0] in moved]
            order = base[:k] + (stay + go if late else go + stay) + base[to + 1:]
        last, m = {}, k - 1
        while m >= 0 and len(last) < 6:
            last.setdefault(base[m][1], base[m][0])
            m -= 1
        tm, new, eng, room = [], [], list(eng0), CFG["temp"] * draw() * (1 - rs / CFG["tries"])
        for v, (cs, w) in enumerate(views):
            fin, end = list(st[v][0]), list(st[v][1])
            free = {x: end[last[x]] if x in last else 0.0 for x in "vstgyr"}
            if v == 0 and to + 120 < n:
                replay(order[:to + 120], cs, w, k, fin, end, eng, free)
                a, b = (next(x for x, y in order[to + 119::-1] if y == z) for z in "vs")
                if min(end[a] - st[0][1][a], end[b] - st[0][1][b]) > CFG["cut"]:
                    break
                tm.append(replay(order, cs, w, to + 120, fin, end, eng, free))
            else:
                tm.append(replay(order, cs, w, k, fin, end, eng, free))
            new.append((fin, end))
            if tm[-1] > tm0[v] + 500:
                break
        if len(tm) == len(views) and score(tm) <= score(tm0) + room:
            now, tm0 = settle(order, new, eng), tm
            if score(tm) < score(best[1]):
                best = (now[0], tm)
    return best


def rank_program(g, core, T, topo):
    rank = T.rank_of(core)
    if rank is None:
        return
    N = len(T.cores)
    CK, CY = CFG["ck"], CFG["cy"]
    Q = {"v": g.vector, "s": g.scalar, "t": g.tensor, "g": g, "y": g.sync}
    ops, hist = [], {}

    def a(n, c0=0, c1=None, st=1, p=None):
        if n in ALIAS:
            n, c0, c1 = "T3", ALIAS[n], ALIAS[n] + 128
        where, shape, dty = SCRATCH[n]
        c1 = shape[1] if c1 is None else c1
        m = 0
        if st == 1:
            m = ((1 << (c1 - c0)) - 1) << c0
        else:
            for c in range(c0, c1, st):
                m |= 1 << c
        ps = slice(None) if p is None else p
        ap = T[n][ps, c0:c1] if st == 1 else T[n][ps, c0:c1:st]
        return {"ap": ap, "acc": [(n, m)], "n": len(range(c0, c1, st)), "w": WIDE[dty], "ps": where == "psum", "fl": dty in (F32, BF)}

    def a3(n, r, c):
        where, shape, dty = SCRATCH[n]
        rs = range(*r)
        cs = range(*c) if isinstance(c, tuple) else [c]
        row = sum(1 << x for x in cs)
        m = sum(row << (shape[2] * x) for x in rs)
        ap = T[n][:, slice(*r), slice(*c) if isinstance(c, tuple) else c]
        return {"ap": ap, "acc": [(n, m)], "n": len(rs) * len(cs), "w": WIDE[dty], "ps": where == "psum", "fl": True}

    def ind(win, off):
        return {"ap": win["ap"].indirect(off["ap"]), "acc": win["acc"], "off": off["acc"], "n": 16 * off["n"], "w": win["w"], "ps": False, "fl": win["fl"]}

    def issue(fns, outs, ins, lat=0.0, sem=None, inc=1, grp=None, after=None, join=False):
        acc = []
        for o in outs:
            acc += [(n, m, True) for n, m in o["acc"]] + [(n, m, False) for n, m in o.get("off", [])]
        for i in ins:
            if isinstance(i, dict):
                acc += [(n, m, False) for n, m in i["acc"] + i.get("off", [])]
        deps, me = (ops[-1]["deps"], len(ops) - 1) if join else ({}, len(ops))
        if after is not None:
            deps[after] = "o"
        for n, m, w in acc:
            h = hist.setdefault(n, [])
            if n in BANKS:
                same = grp is not None and h and ops[h[0][2]]["grp"] == grp
                for (m2, w2, d) in h[:1] if same else h:
                    if d != me:
                        k = "o" if grp is not None and ops[d]["grp"] is not None else ("w" if w or w2 else "rr")
                        deps[d] = "w" if deps.get(d) == "w" else k
                continue
            for (m2, w2, d) in h:
                if m & m2 and (w or w2) and d != me:
                    deps[d] = "w"
        for n, m, w in acc:
            h = hist[n]
            if n in BANKS:
                same = grp is not None and h and h[0][2] < len(ops) and ops[h[0][2]]["grp"] == grp
                h[:] = (h if same else []) + [(m, w, me)]
            else:
                if w:
                    h[:] = [e for e in h if e[0] & ~m]
                h.append((m, w, me))
        if join:
            ops[me]["fn"]["t"].append(fns["t"][0])
            ops[me]["cost"]["t"] += fns["t"][1]
            return me
        ops.append({"nm": outs[0]["acc"][0][0] if outs else "-", "fn": {q: [f] for q, (f, c) in fns.items()}, "cost": {q: c for q, (f, c) in fns.items()}, "deps": deps,
                    "lat": lat, "sem": sem, "inc": inc, "grp": grp,
                    "ix": 2 if any("off" in o for o in outs) else int(any(isinstance(i, dict) and "off" in i for i in ins))})
        return me

    def sv(x):
        return x["ap"] if isinstance(x, dict) else x

    def cost(o, ins, per=None):
        if "off" in o:
            return 50 + o["n"] * CFG["sc"] * CY
        if any("off" in i for i in ins):
            return 55 + o["n"] * CFG["g"] * CY
        if per is None:
            per = 0.5 if all(x["w"] == 2 for x in [o] + ins) else 1
        return CFG["fix"] + max(64, per * o["n"]) * CY

    def f_cp(o, i):
        return lambda: g.vector.tensor_copy(o["ap"], i["ap"]), cost(o, [i])

    def f_ts(o, i, s1, op0, s2=None, op1=None):
        if op1 is None:
            return lambda: g.vector.tensor_scalar(o["ap"], i["ap"], sv(s1), None, op0), cost(o, [i])
        return lambda: g.vector.tensor_scalar(o["ap"], i["ap"], sv(s1), sv(s2), op0, op1), cost(o, [i])

    def f_act(o, i, f=AF.Copy, bias=None, scale=None):
        if bias is not None and scale is not None:
            return lambda: g.scalar.activation(o["ap"], i["ap"], f, bias=sv(bias), scale=sv(scale)), cost(o, [i], 1)
        if bias is not None:
            return lambda: g.scalar.activation(o["ap"], i["ap"], f, bias=sv(bias)), cost(o, [i], 1)
        if scale is not None:
            return lambda: g.scalar.activation(o["ap"], i["ap"], f, scale=sv(scale)), cost(o, [i], 1)
        return lambda: g.scalar.activation(o["ap"], i["ap"], f), cost(o, [i], 1)

    def cp(o, i):
        issue({"v": f_cp(o, i)}, [o], [i])

    def cp2(o, i, pool=False):
        fns = {} if pool else {"v": f_cp(o, i), "s": f_act(o, i)}
        if CFG["pool"] and "off" not in i and not i["ps"]:
            fns["g"] = (lambda: g.affine_select(o["ap"], i["ap"], [[0, o["n"]]], ALU.is_ge, 0.0, 0, 0), 170 + 2 * o["n"] * CY)
        issue(fns, [o], [i])

    def add2(o, i, col):
        issue({"v": f_ts(o, i, col, ALU.add), "s": f_act(o, i, AF.Identity, bias=col)}, [o], [i, col])

    def mul2(o, i, col):
        issue({"v": f_ts(o, i, col, ALU.mult), "s": f_act(o, i, AF.Copy, scale=col)}, [o], [i, col])

    def tt(o, i, j, op):
        per = 1 if i["ps"] or j["ps"] or o["w"] + i["w"] + j["w"] == 6 else 2
        issue({"v": (lambda: g.vector.tensor_tensor(o["ap"], i["ap"], j["ap"], op), cost(o, [i, j], per))}, [o], [i, j])

    def ts(o, i, s1, op0, s2=None, op1=None):
        fns = {"v": f_ts(o, i, s1, op0, s2, op1)}
        if o["fl"] and i["fl"] and "off" not in o and not any(isinstance(x, dict) and x["ps"] for x in (s1, s2)):
            if op0 == ALU.mult and op1 is None:
                fns["s"] = f_act(o, i, AF.Copy, scale=s1)
            elif op0 == ALU.add and op1 is None:
                fns["s"] = f_act(o, i, AF.Identity, bias=s1)
            elif op0 == ALU.mult and op1 == ALU.add:
                fns["s"] = f_act(o, i, AF.Identity, bias=s2, scale=s1)
        issue(fns, [o], [i, s1, s2])

    def scan(o, d0, d1, init, op0, op1):
        issue({"v": (lambda: g.vector.tensor_tensor_scan(o["ap"], d0["ap"], d1["ap"], sv(init), op0, op1), cost(o, [d0, d1]))}, [o], [d0, d1, init])

    def ms(o, c):
        fns = {"v": (lambda: g.vector.memset(o["ap"], c), cost(o, []))}
        if o["fl"] and c == int(c) and abs(c) < 256:
            fns["g"] = (lambda: g.iota(o["ap"], [[0, o["n"]]], int(c), 0, allow_small_or_imprecise_dtypes=True), 130 + 2 * o["n"] * CY)
        issue(fns, [o], [])

    def act(o, i, f=AF.Copy, bias=None, scale=None):
        issue({"s": f_act(o, i, f, bias, scale)}, [o], [i, bias, scale])

    def act_sum(o, i, f, col, bias, scale):
        fn = lambda: g.scalar.activation(o["ap"], i["ap"], f, bias=sv(bias), scale=sv(scale), accum_out=col["ap"])
        issue({"s": (fn, cost(o, [i], 1) + 20)}, [o, col], [i, bias, scale])

    gid = [0]

    left = {}

    def mm1(o, l, r, first, join=False, grp=None):
        grp = grp or gid[0]
        left[grp] = left.get(grp, 0) + 1
        c = max(64, r["n"]) * CFG["pe"] * (4 if l["w"] == 4 else 1)

        def fn():
            left[grp] -= 1
            return g.tensor.matmul(o["ap"], l["ap"], r["ap"], first, left[grp] == 0)

        issue({"t": (fn, c)}, [o], [l, r], grp=grp, join=join)

    def mm(o, *steps):
        gid[0] += 1
        for k, terms in enumerate([x for x in steps if x]):
            for j, (l, r) in enumerate(terms):
                mm1(o, l, r, k + j == 0, j > 0)

    def iota(o, pat, base=0, cm=0):
        if SCRATCH[o["acc"][0][0]][2] == I32:
            f = lambda: g.iota(o["ap"], pat, base, cm)
        else:
            f = lambda: g.iota(o["ap"], pat, base, cm, allow_small_or_imprecise_dtypes=True)
        issue({"g": (f, 130 + 2 * o["n"] * CY)}, [o], [])

    def asel(o, pat, op, base, cm, i=None, fill=0.0):
        i = i or o
        issue({"g": (lambda: g.affine_select(o["ap"], i["ap"], pat, op, fill, base, cm), 170 + 2 * o["n"] * CY)}, [o], [i])

    nld = [0, None]

    def load(q, o, src, nbytes):
        s = LOADS[nld[0]]
        nld[0] += 1
        nld[1] = issue({q: (lambda: Q[q].dma_start(o["ap"], src), 100.0)}, [o], [], lat=CFG["dma"] + nbytes / CFG["bw"], sem=s, inc=16, after=nld[1])

    def shift(o, i, sem, more=700):
        issue({"y": (lambda: g.sync.dma_start(o["ap"], i["ap"]), 100.0)}, [o], [i], lat=CFG["dma"] + more, sem=sem, inc=16)

    def store(dst, i, q="y"):
        issue({q: (lambda: Q[q].dma_start(dst, i["ap"]), 100.0)}, [], [i], lat=CFG["dma"] + 500, sem="out", inc=16)

    cc = lambda k: a("CC", k, k + 1)
    s8 = lambda k: a("S8", k, k + 1)
    P8 = slice(0, 8)
    sel = lambda n, p, pp=None: a(n, 15 - p, 143 - p, p=pp)

    load("y", a("LI", p=P8), T.live[:, 0:768], 24576)
    load("s", dict(a("LI", p=slice(8, 16)), acc=[("LI", 1 << 768)]), T.live[:, 768:T0], 49152)
    load("y", a("RI", 0, 768), T.rings[:, 0:768], 440000)
    load("s", a("RI", 768, T0), T.rings[:, 768:T0], 830000)
    load("y", a("Z"), T.z[:], 900000)
    load("s", a("X", 0, NB), T.x0[:], 1950000)
    load("y", a("SI", 0, 1), T.w[:], 0)
    load("y", a("SI", 1, 2), T.kap[:], 0)
    load("y", a("SI", 2, 3, p=P8), T.th[:], 0)
    load("y", a("SI", 3, 4, p=P8), T.cap[:], 0)

    iota(a("PI", 0, 1), [[0, 1]], 0, 1)
    iota(a("XA"), [[1, 144]])
    iota(a("JJ"), [[16, 96]])
    iota(a("TF", 0, 128), [[16, 8], [0, 16]])
    iota(a("TF", 128, 144), [[1, 2], [4, 8]])
    ts(a("PI", 1, 2), a("PI", 0, 1), 15, ALU.bitwise_and)
    ts(a("PI", 2, 3), a("PI", 0, 1), 7, ALU.bitwise_and)
    ts(a("PI", 3, 4), a("PI", 0, 1), 3, ALU.logical_shift_right, 1, ALU.bitwise_and)
    ts(a("PI", 4, 5), a("PI", 0, 1), 1, ALU.bitwise_and)
    ms(a("NEG"), -1.0)
    ms(a("IB"), 1.0)
    cp(a("S8", 0, 5), a("PI", 0, 5))
    ts(cc(1), s8(0), s8(1), ALU.subtract, 15.0, ALU.add)
    ts(cc(2), s8(0), 16.0, ALU.mult, 15.0, ALU.add)
    ts(cc(14), s8(0), s8(1), ALU.subtract)
    ts(cc(4), s8(1), -16.0, ALU.add)
    P16 = slice(0, 16)
    cp(a("LB", p=P16), dict(a("LI", p=P16), acc=[("LI", (1 << 769) - 1)]))
    ms(a("ONE"), 1.0)
    for x in range(2):
        asel(a("E8%d" % x, p=P16), [[1, 144]], ALU.is_equal, 128 * x - 15, -16, a("ONE", p=P16))
        mm(a("B7", 48 * x, 48 * x + 48), [(sel("E8%d" % x, p, P16), a("LB", p, 768, 16, p=P16)) for p in range(16)])
    ts(a("BO"), a("TF", 0, 128), cc(14), ALU.is_equal)
    ts(a("JJ"), a("JJ"), s8(1), ALU.add)
    ts(a("NU"), a("BO"), -1.0, ALU.mult)
    asel(a("NU"), [[-1, 128]], ALU.is_gt, 0, 1)
    asel(a("IB"), [[-1, 128]], ALU.is_equal, 0, 1)
    ts(cc(7), s8(2), 32.0, ALU.mult)
    ts(cc(19), s8(3), 2.0, ALU.mult, cc(7), ALU.add)
    ts(a("LN", 0, 16), a("TF", 128, 144), cc(19), ALU.add)
    cp2(a("LN", 16, 32), a("JJ", 0, 16))
    cp(a("OZ", 0, 16), a("LN", 0, 16))
    cp2(a("ZR", 0, 4096, 16), ind(a("Z"), a("OZ", 0, 16)))
    for k in range(1, 16):
        cp2(a("ZR", k, 4096, 16), a("ZR", 0, 4096, 16))
    ts(a("KJ"), a("JJ"), -1.0, ALU.mult, float(T0), ALU.add)
    ts(a("DEAD", 0, 96), a("B7", 0, 96), -1.0, ALU.mult, 1.0, ALU.add)
    scan(a("SC"), a("DEAD", 0, 96), a("NEG"), 0.0, ALU.add, ALU.add)
    tt(a("E"), a("DEAD", 0, 96), a("KJ"), ALU.mult)
    ts(a("NIB"), a("IB"), -1.0, ALU.mult)
    mm(a("B7", 0, 96), [(a("NU"), a("DEAD", 0, 96))], [(a("BO"), a("SC"))], [(a("NIB"), a("E"))])
    mm(a("B7", 96, 98), [(a("BO"), a("SC", 71, 96, 24))])
    ts(a("RH", 0, 768), a("RI", 0, 768), -2048.0, ALU.add)
    ts(a("RH", 768, T0), a("RI", 768, T0), -2048.0, ALU.add)
    cp2(a("R", T0 - 128, T0), a("RH", T0 - 128, T0), True)
    ts(a("DST"), a("B7", 0, 96), -1.0, ALU.mult, cc(4), ALU.add)
    cp(a("SM", 0, 2), a("B7", 96, 98))
    for c in range(0, 96, CFG["sn"]):
        cp(ind(a("D", 384, 1920), a("DST", c, c + CFG["sn"])), a("RI", 16 * c, 16 * (c + CFG["sn"])))
    dg = lambda t, d0, d1, ks=(0, 16): a3("DG", (8 * (DG0[t] + d0), 8 * (DG0[t] + d1)), ks)
    for t in (0, RO - 1):
        iota(dg(t, 0, TAU[t]), [[0, 128 * TAU[t]]])
    for t in range(1, RO - 1):
        shift(dg(t, 0, TAU[t]), dg(RO - 1, 0, TAU[t]), "zf%d" % t)
    for t in range(RO):
        for d in range(TAU[t]):
            ks = [k for k in range(16) if k * TAU[t] >> 4 == d]
            asel(dg(t, d, d + 1, (ks[0], ks[-1] + 1)), [[-16, 8], [-1, len(ks)]], ALU.is_equal, -ks[0], 1, a("ONE", 0, 8 * len(ks)))

    def places_x(t, c0, c1, nb):
        tau = TAU[t]
        mm(a("B6", 0, c1 - c0), [(dg(t, d, d + 1), a("RH", c0 * tau + d, c1 * tau, tau)) for d in range(tau)])
        ts(a("O%d" % (t % 2), c0, c1), a("B6", 0, c1 - c0), 2048.0, ALU.add)
        ops[-1]["early"] = CFG["e0"] if t == 0 else CFG["e1"]
        for c in range(c0, c1, CK):
            e = min(c + CK, c1)
            cp2(a("XH%d" % (t % 2), 16 * c, 16 * e), ind(a("X", 0, nb), a("O%d" % (t % 2), c, e)))

    places_x(0, 0, 256, NB)
    ts(a("SM", 2, 3), a("SM", 1, 2), a("SM", 0, 1), ALU.subtract)
    ts(a("SM", 3, 4), a("SM", 1, 2), -1.0, ALU.mult)
    ts(a("SN", 0, 32), a("LN"), a("SM", 2, 3), ALU.add)
    ts(a("SN", 32, 64), a("SN", 0, 32), 0.0, ALU.is_lt, a("SM", 3, 4), ALU.mult)
    tt(a("SN", 64, 96), a("SN", 0, 32), a("SN", 32, 64), ALU.add)
    cp(a("GO"), a("SN", 64, 96))
    ts(a("SEL"), a("XA"), cc(1), ALU.is_equal, BIG, ALU.mult)
    ts(a("IDX2"), a("XA", 0, 128), 8192.0, ALU.mult)
    ms(cc(20), -0.5)
    ms(cc(21), 128.0)
    ms(cc(22), -128.0)
    ts(cc(6), s8(1), 128.0, ALU.mult)
    mul2(a("SELH"), a("SEL"), 0.5)
    mul2(a("SELN"), a("SEL"), -0.5)
    ms(a("RST"), 0.0)
    ms(a("RST", 0, 128, 16), float(2 ** 40))
    ms(a("RS18"), 0.0)
    ms(a("RS18", 0, 288, 18), float(2 ** 40))
    iota(a("C1"), [[1, 16], [0, 16]])
    iota(a("C3", 0, 128), [[0, 64], [-2, 2]], 1)
    cp(a("S8", 6, 8), a("SI", 0, 2))
    ts(cc(8), s8(6), 2048.0, ALU.is_ge, -4096.0, ALU.mult)
    ts(cc(9), s8(6), cc(8), ALU.add)
    ts(a("SELW"), a("XA"), cc(1), ALU.is_equal, cc(9), ALU.mult)
    ts(a("C4"), a("C1"), s8(1), ALU.is_equal, s8(7), ALU.mult)
    cp2(a("BOF"), a("BO"), True)
    mm(a("B5", 0, 256), [(a("BOF"), a("C4"))])
    cp2(a("KAP"), a("B5", 0, 256))
    for t in range(0, RO, 2):
        iota(a("CV", P * t, P * t + 2 * P, p=P8), [[2, 2 * P]], XW[t] - 2048)
    iota(a("CN"), [[0, P]], -4096)
    shift(a("X", NB, XW[RO - 1]), a("X", 0, XW[RO - 1] - NB), "xf")
    shift(a("RHS", 4096, 4352, p=slice(0, 1)), a("CV", 0, P, p=slice(0, 1)), "cn", 0)
    mul2(a("NHB"), a("IB"), -0.5)
    ts(cc(3), s8(4), -2.0, ALU.mult, 1.0, ALU.add)
    mul2(a("SGF"), a("C3", 0, 128), cc(3))
    ts(a("OC"), a("XA", 0, 16), 0.0, ALU.mult, s8(1), ALU.add)
    cp(a("H3", 0, 16), a("JJ", 0, 16))
    ms(a("H3", 272, 288), 0)
    ms(a("H3P", 0, 2), 0.0)
    ms(a("C4K"), 4096.0)
    iota(a("HIB"), [[0, 128]])
    asel(a("HIB"), [[-1, 128]], ALU.not_equal, 0, 1, fill=0.5)
    ts(a("A1", 0, 18), a("JJ", 0, 18), -8.5, ALU.add, 1.0 / 18, ALU.mult)
    ts(a("SN", 0, 18), a("A1", 0, 18), -287.0, ALU.mult)
    ts(a("SN", 32, 50), a("JJ", 0, 18), 16.0, ALU.mult)
    tt(a("SN", 64, 82), a("SN", 0, 18), a("SN", 32, 50), ALU.add)
    cp(a("OP", 0, 18), a("SN", 64, 82))
    asel(a("T3", 128, 256), [[-1, 128]], ALU.is_ge, 0, 1, a("BO"))
    for n in ("FX", "DO", "ZE", "NI"):
        ms(a(n), 0.0)
    ts(a("NI", 1, 25), a("JJ", 0, 24), -1.0, ALU.mult, -1.0, ALU.add)
    ts(a("II", 0, 25), a("NI", 0, 25), -1.0, ALU.mult, -1.0, ALU.add)
    ts(a("II", 0, 1), a("NI", 0, 1), 0.0, ALU.mult)
    cp(a("C7", 4, 6, p=P8), a("SI", 2, 4, p=P8))
    ts(a("E8F", p=P8), a("TF", 0, 128, p=P8), 15.0, ALU.add, a("CC", 2, 3, p=P8), ALU.is_equal)
    mm(a("B4", 0, 2), [(a("E8F", p=P8), a("C7", 4, 6, p=P8))])
    ts(cc(10), a("B4", 0, 1), BIG, ALU.mult)
    cp(cc(11), a("B4", 1, 2))
    iota(a("IDXB"), [[0, 16], [16384, 18]])
    add2(a("IDXB", 0, 288, 18), a("IDXB", 0, 288, 18), cc(10))
    ts(a("THL"), a("IDXB", 0, 288, 18), -1.0, ALU.mult, cc(10), ALU.add)
    ms(a("IDXB", 17, 288, 18), float(2 ** 34))
    ts(cc(17), cc(14), 2.0, ALU.mult, 15.0, ALU.add)
    ts(cc(18), cc(14), s8(0), ALU.add)
    for x in range(2):
        ts(a("C7", 8 + 4 * x, 12 + 4 * x), a("XA", 0, 16, 4), -1.0, ALU.mult, cc(17 + x), ALU.add)
    iota(a("SV"), [[1, 4], [32, 8], [1, 16]], -1)
    for c in (0, 8, 4, 12):
        sh = a("SH", 128 * c, 128 * c + 512)
        ts(sh, a("SV"), a("C7", 8 + c // 4, 9 + c // 4), ALU.min, a("C7", 12 + c // 4, 13 + c // 4), ALU.is_equal)
        asel(sh, [[0, 4], [-16, 8], [0, 16]], ALU.is_ge, 0, 1)

    def tails(t, ages):
        tau = TAU[t]
        for ag in ages:
            b = "B%d" % (4 + ag % 2)
            if ag == 1 and (t == 0 or 9 not in GA):
                cp2(a("RHS", 1, 4096, 16), a("RH", tau >> 4, 256 * tau, tau), True)
                mm(a(b, 0, 256), [(a("SH", 128 * 9, 128 * 10), a("RH", 9 * tau >> 4, 256 * tau, tau))])
                cp2(a("RHS", 9, 4096, 16), a(b, 0, 256))
                continue
            for x in (ag, ag + 8):
                if t and x in GA:
                    c = 0 if x == 1 else TW * RSA.index(x)
                    i = a("RH" if x == 1 else "RS", c + (x * tau >> 4), c + 256 * tau, tau)
                    if x == 0:
                        i["acc"] = i["acc"] + [("RS", i["acc"][0][1] << TW * len(RSA))]
                    cp2(a("RHS", x, 4096, 16), i, True)
                else:
                    mm(a(b, x // 8, 512, 2), [(a("SH", 128 * x, 128 * x + 128), a("RH", x * tau >> 4, 256 * tau, tau))])
            if not (t and ag in GA):
                cp2(a("RHS", ag, 4096, 8), a(b, 0, 512))

    def shifted(k, c0, c1, gate=()):
        each = 128 * (c1 - c0) * 2 / CFG["bw"]
        rd = lambda ap, bit: {"ap": ap, "acc": [("RD", bit << 16 * k)]}
        if not gate:
            shift(rd(T["RD"][:, 0:16, c0:c1], 1), a("RH", c0, c1), "wr%d" % k, each)
            for j in range(max(RSA) - 1):
                shift(rd(T["RD"][:, 16 + j, c0:c1], 2 << j), a("RH", c0, c1, p=slice(15, 128, 16)), "wr%d" % k, each)
            return
        for j, x in enumerate(RSA):
            c = TW * j
            if x:
                i = rd(T["RD"][:, x - 1:x + 15, c0:c1], 0xFFFF)
                shift(a("RS", c + c0, c + c1), dict(i, acc=i["acc"] + list(gate)), "sh%d" % j, 300 + each * j)
            else:
                o = a("RS", c + c0, c + c1, p=slice(1, 128))
                i = a("RH", c0, c1, p=slice(0, 127))
                shift(o, dict(i, acc=i["acc"] + list(gate)), "sh%d" % j, 300 + each)
                o = a("RS", c + c0, c + c1, p=slice(0, 1))
                shift(dict(o, acc=[("RS", o["acc"][0][1] << TW * len(RSA))]), a("RH", c0, c1, p=slice(0, 1)), "sz", 0)

    old = lambda t: (((T0 + P * (t - 1)) // TAU[t]) // 2) * 2

    def s2(t, h, p0, p1, b):
        c0, c1 = 128 * h + 8 * p0, 128 * h + 8 * p1
        act(a("M", 16 * c0, 16 * c1), ind(a("X", 0, XW[t]), a("OT", c0, c1)))
        mm(a(b, 0, 16 * (c1 - c0)), [(a("IB"), a("ZR", 16 * c0, 16 * c1))], [(a("NIB"), a("M", 16 * c0, 16 * c1))])
        act(a("DX", 16 * c0, 16 * c1), a(b, 0, 16 * (c1 - c0)), AF.Abs)

    def v2(t, h, p0, p1):
        c0, c1 = 128 * h + 8 * p0, 128 * h + 8 * p1
        d, m = a("DX", 16 * c0, 16 * c1), a("M", 16 * c0, 16 * c1)
        tt(d, ind(a("X", 0, XW[t]), a("OT", c0, c1)), a("ZR", 16 * c0, 16 * c1), ALU.subtract)
        fns = {"v": f_ts(m, d, -1.0, ALU.mult, 0.0, ALU.max)}
        if CFG["ca"]:
            fns["s"] = f_act(m, d, AF.Relu, scale=-1.0)
        issue(fns, [m], [d])

    def step2(t, h):
        PV = CFG["pv"][h]
        pm, sm = (PV + 1) // 2, min(PV + 4, 16)
        v2(t, h, 0, pm)
        s2(t, h, PV, sm, "B2")
        v2(t, h, pm, PV)
        for k, p0 in enumerate(range(sm, 16, 4)):
            s2(t, h, p0, min(p0 + 4, 16), "B%d" % (3 - k % 2))
        part = lambda s_, n, p0, p1: [(sel(s_, p), a(n, 2048 * h + 128 * p, 2048 * h + 128 * p + 128)) for p in range(p0, p1)]
        kb = a("B7" if h else "B1", 0, 128)
        mm(kb, [(a("IB"), a("IDX2"))], part("SELN", "M", PV, sm), part("SEL", "M", 0, pm), part("SELN", "M", sm, 16),
           part("SELH", "DX", PV, sm), part("SEL", "M", pm, PV), part("SELH", "DX", sm, 16))
        c = 128 * h
        scan(a("K0", c, c + 128), a("RST", 0, 128), kb, 0.0, ALU.add, ALU.min)
        cp(a("A1", 8 * h, 8 * h + 8), a("K0", c + 15, c + 128, 16))
        ts(a("A2", 8 * h, 8 * h + 8), a("A1", 8 * h, 8 * h + 8), 13, ALU.logical_shift_right, 127, ALU.bitwise_and)
        ts(a("AU", 8 * h, 8 * h + 8), a("A2", 8 * h, 8 * h + 8), cc(6), ALU.add)
        dst = a("YS", 128 * t, 128 * t + 128) if h == 0 else a("YL", 1, 256, 2)
        act(dst, ind(a("DX", 2048 * h, 2048 * h + 2048), a("AU", 8 * h, 8 * h + 8)), AF.Abs)

    def move(t):
        to = T.cores[(rank + 1 + t % (N - 1)) % N]
        fr = T.cores[(rank - 1 - t % (N - 1)) % N]
        rid, pid, _ = topo.addr(to)
        eng = topo.engines(core, to)[::CFG["es"]]
        mask = sum(1 << e for e in eng)
        src, dst = a("YS", 128 * t, 128 * t + 128), a("YE", 128 * t, 128 * t + 128)

        def send():
            g.remote_dma(dst["ap"], src["ap"], T.sem["arr%d" % t], T.sem["snt%d" % t], pid, rid, mask)

        me = issue({"g": (send, 300.0)}, [{"acc": [("GATE", 1 << t)]}], [src], sem="snt%d" % t, inc=len(eng))
        issue({"r": (lambda: None, 0.0)}, [dst], [], lat=CFG["rem"] + 300, sem="arr%d" % t, inc=len(topo.engines(fr, core)[::CFG["es"]]), after=me)

    for t in range(RO):
        Tt = T0 + P * t
        XH = "XH%d" % (t % 2)
        last = t == RO - 1
        dw0 = a("D", 384, 1920) if t == 0 else a("D", 0, 640)
        cp(a("OT", 0, 128), ind(dw0, a("GO", 0, 8)))
        cp(a("OT", 128, 256), ind(dw0, a("GO", 8, 16)))
        step2(t, 0)
        move(t)
        step2(t, 1)
        if t:
            places_x(t, old(t), 256, XW[t])
        elif RSA:
            shifted(0, 0, T0)
        if RSA:
            shifted(t, Tt - P if t else 0, Tt, [("GATE", 1 << t)])
        if not last:
            places_x(t + 1, 0, old(t + 1), XW[t])
        ts(a("RR"), ind(dw0, a("GO", 16, 32)), -2048.0, ALU.add)
        shift(a("RHS", 4096, 4352, p=slice(1, 128)), a("RR", p=slice(0, 127)), "nf%d" % t)
        tails(t, range(0, 8))
        ye = 128 * t
        uo = [(sel("SELW", p), a("YL", p, 256, 16)) for p in range(1, 16, 2)]
        ue = [(sel("SELW", p), a("YE", ye + p // 2, ye + 128, 8)) for p in range(0, 16, 2)]
        mm(a("B7", 0, 16), [(a("IB"), a("ZE", 0, 16))], uo, ue)
        Y = a("YL", 0, 256)
        cp2(a("YL", 0, 256, 2), a("YE", ye, ye + 128))
        cp2(a(XH, 4096, 4352), Y, True)
        cp(a("UQ", 32, 48), a("B7", 0, 16))
        ts(a("UQ", 0, 16), a("UQ", 32, 48), 4095, ALU.bitwise_and)
        tt(a("UQ", 48, 64), a("UQ", 0, 16), a("UQ", 0, 16), ALU.mult)
        tt(a("H1"), ind(a("UQ", 0, 16), a("OC")), a("KAP"), ALU.mult)
        ts(a("UQ", 16, 32), a("UQ", 48, 64), 5, ALU.logical_shift_right)
        mv = 16 - sum(CFG["sg"])
        for m0, m1 in ((mv, 16), (0, mv)) if CFG["h4"] else ((0, 16),):
            tt(a("H2", 16 * m0, 16 * m1), ind(a("UQ", 16, 32), a("OC", 0, m1 - m0)), a("H1", 16 * m0, 16 * m1), ALU.add)
            ts(a("H3", 16 + 16 * m0, 16 + 16 * m1), a("H2", 16 * m0, 16 * m1), 4095, ALU.bitwise_and)
            cp(a("HU", 16 * m0, 16 * m1), a("H3", 16 + 16 * m0, 16 + 16 * m1))
        dc = Tt // 16
        if not last:
            if t:
                act_sum(a("DO", 1, 9), a("LV", 16 * t - 8, 16 * t), AF.Identity, a("FA", 4, 5), 1.0, -1.0)
            else:
                act_sum(a("DO", 1, 9), a("DEAD", 88, 96), AF.Identity, a("FA", 4, 5), 0.0, 1.0)
            scan(a("SUO", 0, 25), a("ZE", 0, 25), a("DO", 0, 25), a("FA", 4, 5), ALU.add, ALU.subtract)
            tt(a("DI", 0, 25), a("DO", 0, 25), a("NI", 0, 25), ALU.mult)
            gid[0] += 1
            gw, bw = gid[0], a("B7", 0, 25)
            for k, (l, r) in enumerate([(a("IB"), "II"), (a("BO"), "SUO"), (a("T3", 128, 256), "DO"), (a("IB"), "DI")]):
                mm1(bw, l, a(r, 0, 25), k == 0, k > 0)
        win = a(XH, 0, 4096)
        ts(a("H3P", 2, 290), ind(a("H3"), a("OP", 0, 18)), -2048.0, ALU.add)
        dl = a("B1", 0, 288)
        gid[0] += 1
        mm1(dl, a("IB"), a("H3P", 1, 289), True)
        mm1(a("B1", 1, 288, 18), a("IB"), a("C4K"), False, True)
        mm1(dl, a("NIB"), a("H3P", 2, 290), False, True)
        sums, m0 = [], 0
        for n in CFG["vc"]:
            for m in range(m0, m0 + n):
                tt(a3("DX5", (0, 256), m), ind(win, a("HU", 16 * m, 16 * m + 16)), Y, ALU.subtract)
            ts(a3("M5", (0, 256), (m0, m0 + n)), a3("DX5", (0, 256), (m0, m0 + n)), -2.0, ALU.mult, 0.0, ALU.max)
            sums += [("DX5", m0, m0 + n), ("M5", m0, m0 + n)]
            m0 += n
        for m in range(m0, mv):
            tt(a3("DX5", (0, 256), m), ind(win, a("HU", 16 * m, 16 * m + 16)), Y, ALU.subtract)
            act(a3("M5", (0, 256), m), a3("DX5", (0, 256), m), AF.Abs)
        for k, n in enumerate(CFG["sg"]):
            m = mv + sum(CFG["sg"][:k])
            e, b = m + n, CFG["sb"][k]
            act(a("XS", 256 * m, 256 * e), ind(win, a("HU", 16 * m, 16 * e)))
            gid[0] += 1
            for x in range(m, e):
                mm1(a(b, x - m, 256 * (e - m), e - m), a("NIB"), Y, x == m, x > m)
            for x in range(m, e):
                mm1(a(b, x - m, 256 * (e - m), e - m), a("IB"), a("XS", 256 * x, 256 * x + 256), False, x > m)
            act(a3("M5", (0, 256), (m, e)), a(b, 0, 256 * (e - m)), AF.Abs)
        for n in CFG["sc5"]:
            sums.append(("M5", m0, m0 + n))
            m0 += n
        gid[0] += 1
        mm1(a3("B0", (0, 16), (0, 18)), a("IB"), a("IDXB"), True)
        mm1(a3("B0", (0, 16), 0), a("IB"), a("THL"), False, True)
        for n, m0, m1 in sums:
            for p in range(16):
                mm1(a3("B0", (0, 16), (1 + m0, 1 + m1)), sel("SEL", p), a3(n, (p, 256, 16), (m0, m1)), False, p % CFG["mj"] > 0)
        parts = [(0, 8), (8, 16)] if CFG["h5"] else [(0, 16)]
        for c0, c1 in parts:
            cp2(a("K3", 18 * c0, 18 * c1), a3("B0", (c0, c1), (0, 18)))
            scan(a("S1", 18 * c0, 18 * c1), a("RS18", 18 * c0, 18 * c1), a("K3", 18 * c0, 18 * c1), 0.0, ALU.add, ALU.min)
        for c0, c1 in parts:
            tt(a("KP", 18 * c0, 18 * c1), a3("B0", (c0, c1), (0, 18)), a("S1", 18 * c0, 18 * c1), ALU.is_gt)
            scan(a("K4", 18 * c0, 18 * c1), a("B1", 18 * c0, 18 * c1), a("KP", 18 * c0, 18 * c1), 0.0, ALU.add, ALU.mult)
        cp(a("OF"), a("K4", 17, 288, 18))
        fk, sb = a("FX", 9, 25), a("B2", 0, 1)
        act_sum(fk, a("S1", 16, 288, 18), AF.Sign, a("FA", t, t + 1), cc(10), -1.0)
        mm(sb, [(a("SGF"), a("FA", x, x + 1)) for x in range(t)], [(a("SGF"), a("FA", t, t + 1))])
        if not last:
            ts(a("MK3"), a("T3"), sb, ALU.mult, cc(11), ALU.is_gt)
            scan(a("SUF", 0, 25), a("ZE", 0, 25), a("FX", 0, 25), a("FA", t, t + 1), ALU.add, ALU.subtract)
            tt(a("FI", 0, 25), a("FX", 0, 25), a("NI", 0, 25), ALU.mult)
            for k, r in enumerate(("SUF", "FX", "FI")):
                mm1(bw, a("MK3", 128 * k, 128 * k + 128), a(r, 0, 25), False, k > 0, gw)
        ts(a("LV", 16 * t, 16 * t + 16), fk, sb, ALU.mult, cc(11), ALU.is_le)
        if t % 2:
            lv, lt = a("LV", 16 * t - 16, 16 * t + 16), a("LVT", 16 * t - 16, 16 * t + 16)
            issue({"v": (lambda lv=lv, lt=lt: g.vector.transpose(lt["ap"], lv["ap"]), cost(lt, [lv]))}, [lt], [lv])
            for x in range(2):
                store(T.ya[x:8:2, P * t - P:P * t + P], a("LVT", 16 * (t - 1 + x), 16 * (t + x)))
        rn, yt = a("R", Tt, Tt + P), a("YT", P * t, P * t + P)
        shift(a("CN", p=slice(0, 128, 16)), a("CV", P * t, P * t + P, p=P8), "cn%d" % t, 0)
        tt(rn, ind(a("RHS"), a("OF")), a("CN"), ALU.max)
        if not last:
            cp(a("DST", 0, 24), a("B7", 1, 25))
            ts(a("GO"), a("LN"), a("B7", 0, 1), ALU.add)
            ts(ind(a("D", 0, 384), a("DST", 0, 24)), a("R", Tt - 128, Tt + P), 1.0, ALU.mult, 2048.0, ALU.add)
            cp2(a("RH", Tt, Tt + P), rn, True)
            if RSA:
                shifted(t + 1, Tt, Tt + P)
            ts(a("MX"), a("RH", Tt, Tt + P), 2048.0, ALU.max)
            mm(a("B6", 0, P), [(a("IB"), a("RH", Tt, Tt + P)), (a("NHB"), a("MX"))])
            ts(yt, a("B6", 0, P), 3072.0, ALU.add)
        else:
            ts(a("B6", 0, P), rn, 0.5, ALU.mult, 3072.0, ALU.add)
            ts(a("RR"), rn, 2048.0, ALU.add)
            tt(yt, a("B6", 0, P), a("RR"), ALU.min)
        store(T.yt[:, P * t:P * t + P], yt, "s" if last else "y")
        xo = a("XN", P * t, P * t + P)
        xn = xo if last else a("X", XW[t], XW[t + 1], 2)
        act(a("XI"), ind(a(XH), a("OF")), AF.Identity, bias=cc(20))
        mm(a("B3", 0, 256), [(a("HIB"), Y)], [(a("HIB"), a("XI"))])
        if t in CFG["xv"]:
            ts(xn, a("B3", 0, 256), 1.5 * 2 ** 23, ALU.add, 1.5 * 2 ** 23, ALU.subtract)
        else:
            act(a("XJ"), a("B3", 0, 256), AF.Identity, bias=cc(21))
            act(xn, a("XJ"), AF.Identity, bias=cc(22))
        if not last:
            cp2(xo, xn, True)
        store(T.yx[:, P * t:P * t + P], xo)

    if "order" not in PLAN:
        PLAN["order"], PLAN["time"] = lay_out(ops)
    cnt, clock, mark, snap, eng = {}, {q: {} for q in Q}, {}, {}, {}

    def wait(q, sem, val):
        if clock[q].get(sem, 0) < val:
            Q[q].wait_ge(T.sem[sem], val)
            clock[q][sem] = val
            for s2_, v2_ in snap.get((sem, val), {}).items():
                clock[q][s2_] = max(clock[q].get(s2_, 0), v2_)

    for i, q in PLAN["order"]:
        o = ops[i]
        eng[i] = q
        sem = o["sem"] or "c" + q
        cnt[sem] = cnt.get(sem, 0) + o["inc"] * len(o["fn"][q])
        mark[i] = (sem, cnt[sem])
        if q == "r":
            continue
        need = {}
        for d, k in o["deps"].items():
            if k == "w" or (k == "rr" and eng[d] != q):
                need[mark[d][0]] = max(need.get(mark[d][0], 0), mark[d][1])
        for s_ in sorted(need, key=lambda s_: s_ == "c" + q):
            wait(q, s_, need[s_])
        for fn in o["fn"][q]:
            call = fn()
            if call is not None:
                call.then_inc(T.sem[sem], o["inc"])
        snap[mark[i]] = dict(clock[q])
    for s_ in sorted(cnt):
        if s_ != "out" and not any(clock[q].get(s_, 0) >= cnt[s_] for q in "vstg"):
            wait("g", s_, cnt[s_])
    g.sync.wait_ge(T.sem["out"], cnt["out"])
